import numpy as np
import ml_dtypes


def mxq(x, axis, fmt="e4m3"):
    dtype, down = {"e4m3": (ml_dtypes.float8_e4m3fn, 7), "e5m2": (ml_dtypes.float8_e5m2, 14)}[fmt]
    v = np.moveaxis(np.asarray(x, np.float32).astype(ml_dtypes.bfloat16).astype(np.float64), axis, -1)
    blocks = v.reshape(v.shape[:-1] + (-1, 32))
    amax = np.abs(blocks).max(-1, keepdims=True)
    byte = np.maximum(np.where(amax > 0, np.frexp(amax)[1] - 1 + 127, 0) - down, 1)
    scale = np.exp2(byte - 127.0)
    codes = (blocks / scale).astype(np.float32).astype(dtype).astype(np.float64)
    return np.moveaxis((codes * scale).reshape(v.shape), -1, axis)


WIDE = False


def mx_kscale(k):
    if not WIDE:
        return np.ones(k)
    levels = np.array([10, -10, 5, -5, 0])
    if k % 512:
        return np.exp2(np.random.permutation(np.resize(levels, k // 32))).repeat(32)
    a = np.empty((k // 512, 16))
    for p in range(k // 512):
        a[p, :8] = np.random.permutation(np.resize(levels, 8))
        for g in range(8):
            far = levels[np.abs(levels - a[p, g]) >= 10]
            a[p, g + 8] = far[np.random.randint(len(far))]
    return np.exp2(a.ravel()).repeat(32)


def f64(x):
    return np.asarray(x).astype(np.float64)


def striped(idx):
    return np.tile(idx.reshape(-1, 16).T, (8, 1)).astype(np.uint16)


def unstriped(offs):
    return offs[:16].T.reshape(-1).astype(np.int64)


def pack_weight(w):
    k, n = w.shape
    w = f64(np.asarray(w, np.float32).astype(ml_dtypes.bfloat16)).reshape(k // 32, 32, n)
    amax = np.abs(w).max(1)
    byte = np.clip(np.where(amax > 0, np.frexp(amax)[1] - 1 + 127 - 7, 1), 1, 254)
    scaled = (w * np.exp2(127.0 - byte)[:, None, :]).reshape(k, n).astype(np.float32)
    words = np.ascontiguousarray(scaled.reshape(k // 512, 128, 4, n).transpose(0, 1, 3, 2)).astype(ml_dtypes.float8_e4m3fn).view(np.uint8)
    return words, np.ascontiguousarray(byte.astype(np.uint8).reshape(k // 512, 16, n))


def unpack_weight(words, scales):
    g, p, n, _ = words.shape
    vals = np.ascontiguousarray(words).view(ml_dtypes.float8_e4m3fn).astype(np.float64) * np.repeat(np.exp2(scales.astype(np.float64) - 127.0), 8, axis=1)[..., None]
    return vals.transpose(0, 1, 3, 2).reshape(g * 512, n)


E2M1 = np.array([0.0, 0.5, 1.0, 1.5, 2.0, 3.0, 4.0, 6.0, -0.0, -0.5, -1.0, -1.5, -2.0, -3.0, -4.0, -6.0])


def pack_fp4(w):
    k, n = w.shape
    w = f64(np.asarray(w, np.float32).astype(ml_dtypes.bfloat16)).reshape(k // 32, 32, n)
    amax = np.abs(w).max(1)
    mant, ex = np.frexp(amax / 6.0)
    byte = np.clip(np.where(amax > 0, np.where(mant > 0.5, ex, ex - 1) + 127, 1), 1, 254)
    scaled = (w * np.exp2(127.0 - byte)[:, None, :]).reshape(k, n).astype(np.float32)
    c = np.ascontiguousarray(scaled.reshape(k // 512, 128, 4, n).transpose(0, 1, 3, 2)).astype(ml_dtypes.float4_e2m1fn).view(np.uint8) & 0xF
    words = (c[..., 0::2] | (c[..., 1::2] << 4)).reshape(k // 512, 128, 2 * n)
    return np.ascontiguousarray(words), np.ascontiguousarray(byte.astype(np.uint8).reshape(k // 512, 16, n))


def unpack_fp4(words, scales):
    g, _, n = scales.shape
    words = np.ascontiguousarray(words).reshape(g, 128, n, 2)
    nib = np.empty((g, 128, n, 4), np.uint8)
    nib[..., 0::2] = words & 0xF
    nib[..., 1::2] = words >> 4
    vals = E2M1[nib] * np.repeat(np.exp2(scales.astype(np.float64) - 127.0), 8, axis=1)[..., None]
    return vals.transpose(0, 1, 3, 2).reshape(g * 512, n)


def relu(v):
    return np.maximum(v, 0.0)

def planes(y):
    n, m = y.shape
    v = y.astype(np.float32).astype(ml_dtypes.bfloat16).astype(np.float64).reshape(n // 32, 32, m)
    top = np.abs(v).max(1)
    byte = np.clip(np.where(top > 0, np.frexp(top)[1] - 1 + 127 - 7, 1), 1, 254)
    codes = (v * np.exp2(127.0 - byte)[:, None, :]).reshape(n, m).astype(np.float32).astype(ml_dtypes.float8_e4m3fn).view(np.uint8)
    words = codes.reshape(n // 512, 128, 4, m).transpose(0, 1, 3, 2)
    return np.ascontiguousarray(words), np.ascontiguousarray(byte.astype(np.uint8).reshape(n // 512, 16, m))


K, T, S, D, V, H, U = 512, 2048, 1024, 3, 512, 512, 256
P = 2 ** 7


def setup_inputs():
    n = np.random.standard_normal
    s = mx_kscale(K)[:, None]
    u = mx_kscale(H)
    packed_xT = pack_weight(n((K, T)) * s)
    packed_w2 = pack_fp4(n((H, H)) / np.sqrt(H) / u[:, None])
    return {
        "x_words": packed_xT[0],
        "x_scales": packed_xT[1],
        "w1": (n((K, H)) / np.sqrt(K) / s * u).astype(np.float32),
        "w2_words": packed_w2[0],
        "w2_scales": packed_w2[1],
        "gate": (np.tile(np.random.uniform(0.2, 1.0, (D, 1, V)) / np.sqrt(D), (1, P, 1))).astype(np.float32),
        "gate2": (np.tile(np.random.uniform(0.2, 1.0, (D, 1, U)) / np.sqrt(D), (1, P, 1))).astype(np.float32),
        "offs": striped(np.random.permutation(T)[:S]),
        "pos1": striped(np.random.permutation(S)[:V]),
        "pos2": striped(np.random.permutation(S)[:V]),
        "pos3": striped(np.random.permutation(S)[:V]),
        "nxt1": striped(np.random.permutation(V)[:U]),
        "nxt2": striped(np.random.permutation(V)[:U]),
        "nxt3": striped(np.random.permutation(V)[:U]),
    }


def reference(x_words, x_scales, w1, w2_words, w2_scales, gate, gate2, offs, pos1, pos2, pos3, nxt1, nxt2, nxt3):
    xq = unpack_weight(x_words, x_scales)[:, unstriped(offs)]
    h = relu(mxq(f64(w1), 0, "e4m3").T @ xq)
    z = h[:, unstriped(pos1)] * f64(gate)[0, :1] + h[:, unstriped(pos2)] * f64(gate)[1, :1] + h[:, unstriped(pos3)] * f64(gate)[2, :1]
    g = relu(unpack_fp4(w2_words, w2_scales).T @ mxq(z, 0, "e4m3"))
    out_0 = g[:, unstriped(nxt1)] * f64(gate2)[0, :1] + g[:, unstriped(nxt2)] * f64(gate2)[1, :1] + g[:, unstriped(nxt3)] * f64(gate2)[2, :1]
    return (out_0,) + planes(out_0)

@@ -1,0 +1,257 @@
+from contextlib import ExitStack
+
+import concourse.mybir as mybir
+from concourse.masks import make_identity
+
+K, T, S, D, V, H, U = 512, 2048, 1024, 3, 512, 512, 256
+FLOPS = 2 * K * H * S + 2 * H * H * V
+
+F32 = mybir.dt.float32
+BF16 = mybir.dt.bfloat16
+I32 = mybir.dt.int32
+U32 = mybir.dt.uint32
+U16 = mybir.dt.uint16
+U8 = mybir.dt.uint8
+FP8X4 = mybir.dt.float8_e4m3fn_x4
+FP4X4 = mybir.dt.float4_e2m1fn_x4
+RELU = mybir.ActivationFunctionType.Relu
+MULT = mybir.AluOpType.mult
+MAX = mybir.AluOpType.max
+
+P = 128
+PACK = 4
+BLOCKS = H // P
+X_PIECES = ((0, 512), (512, 768), (768, 1024))
+V_CHUNKS = ((0, 256), (256, 384), (384, 512))
+R_CHUNKS = ((0, 128), (128, 256))
+
+
+def tile_picked_hop2_relu_po_kernel(
+    tc, x_words, x_scales, w1, w2_words, w2_scales, gate, gate2,
+    offs, pos1, pos2, pos3, nxt1, nxt2, nxt3, out_0, out_1, out_2,
+):
+    nc = tc.nc
+    with ExitStack() as ctx:
+        keep = ctx.enter_context(tc.tile_pool(name="keep", bufs=1))
+        psum = ctx.enter_context(tc.psum_pool(name="psum", bufs=1))
+
+        def sb(name, shape, dtype):
+            return keep.tile(shape, dtype, name=name, align_bytes=64)
+
+        def bank(tag, bufs):
+            return psum.tile([P, 512], F32, name=tag, tag=tag, bufs=bufs)
+
+        def load_list(name, src):
+            lst = keep.tile(list(src.shape), U16, name=name)
+            nc.sync.dma_start(lst[:], src)
+            return lst
+
+        def load_scale_rows(plane, rows):
+            for q in range(4):
+                nc.sync.dma_start(plane[32 * q : 32 * q + 4, :].bitcast(I32), rows[4 * q : 4 * q + 4, :].bitcast(I32))
+
+        xs = sb("xs", [P, T], U8)
+        nc.gpsimd.memset(xs[:].bitcast(I32), 0)
+        w2s = sb("w2s", [P, H], U8)
+        nc.vector.memset(w2s[:].bitcast(I32), 0)
+        ident = sb("ident", [P, P], F32)
+        make_identity(nc, ident[:])
+        warm = sb("warm", [P, 1], F32)
+        nc.scalar.activation(warm[:], ident[:, 0:1], RELU)
+
+        w1_rows = w1.rearrange("(p j) c -> p j c", j=PACK)
+
+        def load_w1(a, queue):
+            raw = keep.tile([P, PACK, P], F32, name="w1_raw", tag="w1_raw", bufs=2, align_bytes=64)
+            queue.dma_start(raw[:], w1_rows[:, :, a * P : (a + 1) * P])
+            return raw
+
+        offs_t = load_list("offs_t", offs)
+        w1_raw = [load_w1(0, nc.sync)]
+        load_scale_rows(xs, x_scales[0])
+        xw = sb("xw", [P, T], U32)
+        nc.sync.dma_start(xw[:].bitcast(I32), x_words[0].rearrange("p n t -> p (n t)").bitcast(I32))
+        w1_raw.append(load_w1(1, nc.sync))
+        pos_t = [load_list("pos%d_t" % d, src) for d, src in enumerate((pos1, pos2, pos3))]
+        gate_rows = gate.rearrange("d p v -> p d v")
+        gate_t = []
+        for c, (v0, v1) in enumerate(V_CHUNKS):
+            gate_t.append(sb("gate_%d" % c, [P, D, v1 - v0], F32))
+        nc.sync.dma_start(gate_t[0][:], gate_rows[:, :, V_CHUNKS[0][0] : V_CHUNKS[0][1]])
+        for c in range(1, len(V_CHUNKS)):
+            nc.sync.dma_start(gate_t[c][:], gate_rows[:, :, V_CHUNKS[c][0] : V_CHUNKS[c][1]])
+        w2w = sb("w2w", [P, 2 * H], U8)
+        nc.sync.dma_start(w2w[:].bitcast(I32), w2_words[0].bitcast(I32))
+        load_scale_rows(w2s, w2_scales[0])
+        nxt_t = [load_list("nxt%d_t" % d, src) for d, src in enumerate((nxt1, nxt2, nxt3))]
+        gate2_t = sb("gate2_t", [P, D, U], F32)
+        nc.sync.dma_start(gate2_t[:], gate2.rearrange("d p r -> p d r"))
+
+        xq = sb("xq", [P, S], U32)
+        xqs = sb("xqs", [P, S], U8)
+        w1_bf = [sb("w1_bf%d" % a, [P, P, PACK], BF16) for a in range(BLOCKS)]
+        w1q = [sb("w1q%d" % a, [P, P], U32) for a in range(BLOCKS)]
+        w1s = [sb("w1s%d" % a, [P, P], U8) for a in range(BLOCKS)]
+        h = [sb("h%d" % a, [P, S], F32) for a in range(BLOCKS)]
+        g = [sb("g%d" % a, [P, V], F32) for a in range(BLOCKS)]
+
+        def round_w1(a):
+            nc.scalar.copy(w1_bf[a][:], w1_raw[a][:].rearrange("p j c -> p c j"))
+            if a + 2 < BLOCKS:
+                w1_raw.append(load_w1(a + 2, nc.scalar))
+
+        def quantise_w1(a):
+            nc.vector.quantize_mx(w1q[a][:].bitcast(FP8X4), w1s[a][:], w1_bf[a][:].rearrange("p c j -> p (c j)"))
+
+        def gather_words(j0, j1):
+            nc.vector.tensor_copy(xq[:, j0:j1], xw[:].indirect(offs_t[:, j0 // 16 : j1 // 16]))
+
+        def first_product(a, j0, j1):
+            acc = bank("product", 3)
+            nc.tensor.matmul_mx(
+                acc[:, 0 : j1 - j0], lhsT=w1q[a][:].bitcast(FP8X4), lhsT_scale=w1s[a][:],
+                rhs=xq[:, j0:j1].bitcast(FP8X4), rhs_scale=xqs[:, j0:j1], start=True, stop=True,
+            )
+            nc.scalar.activation(h[a][:, j0:j1], acc[:, 0 : j1 - j0], RELU)
+
+        nc.vector.tensor_copy(xqs[:], xs[:].indirect(offs_t[:]))
+        round_w1(0)
+        gather_words(*X_PIECES[0])
+        quantise_w1(0)
+        first_product(0, *X_PIECES[0])
+        round_w1(1)
+        for piece in X_PIECES[1:]:
+            gather_words(*piece)
+            first_product(0, *piece)
+        quantise_w1(1)
+
+        def weighted_sums(name, a, window, lists, weights, w0, c0, c1, sums):
+            for d in range(D):
+                term = keep.tile([P, c1 - c0], F32, name="term", tag="term", bufs=6, align_bytes=64)
+                nc.vector.tensor_tensor(
+                    term[:], window[:].indirect(lists[d][:, c0 // 16 : c1 // 16]), weights[:, d, w0 : w0 + c1 - c0], MULT
+                )
+                for s, dst in enumerate(sums):
+                    nc.tensor.matmul(
+                        dst, lhsT=term[:, s * P : (s + 1) * P], rhs=ident[:],
+                        start=(d == 0), stop=(d == D - 1), is_transpose=True,
+                    )
+
+        def hop1_chunk(c, between):
+            v0, v1 = V_CHUNKS[c]
+            last = c == len(V_CHUNKS) - 1
+            n_sub = (v1 - v0) // P
+            banks = [bank("sums", 3) for s in range(n_sub)]
+            zt = [sb("zt_%d_%d" % (c, s), [P, 2, P, 2], BF16) for s in range(n_sub)]
+            for a in range(BLOCKS):
+                if last and a == BLOCKS - 1:
+                    nc.scalar.copy(zt[0][:, :, 0:96, :], banks[0][:, 0:384].rearrange("v (p u e) -> v u p e", u=2, e=2))
+                    banks = [bank("sums", 3)]
+                weighted_sums("term1_%d" % c, a, h[a], pos_t, gate_t[c], 0, v0, v1, [b[:, a * P : (a + 1) * P] for b in banks])
+                between(a)
+            if last:
+                nc.vector.tensor_copy(zt[0][:, :, 96:128, :], banks[0][:, 384:512].rearrange("v (p u e) -> v u p e", u=2, e=2))
+            else:
+                for s in range(n_sub):
+                    nc.scalar.copy(zt[s][:], banks[s][:].rearrange("v (p u e) -> v u p e", u=2, e=2))
+            zb = sb("zb_%d" % c, [P, v1 - v0, PACK], BF16)
+            for s in range(n_sub):
+                back = bank("back", 2)
+                words = zt[s][:].rearrange("v u p e -> v (u p e)").bitcast(F32)
+                for u in range(2):
+                    nc.tensor.transpose(back[:, u * P : (u + 1) * P], words[:, u * P : (u + 1) * P], ident[:])
+                dst = zb[:, s * P : (s + 1) * P, :].rearrange("p v t -> p (v t)").bitcast(F32).rearrange("p (v u) -> p v u", u=2)
+                src = back[:, 0 : 2 * P].rearrange("p (u v) -> p v u", u=2)
+                if last:
+                    nc.vector.tensor_copy(dst, src)
+                else:
+                    nc.scalar.copy(dst, src)
+            return zb
+
+        def second_product(c, zb):
+            v0, v1 = V_CHUNKS[c]
+            last = c == len(V_CHUNKS) - 1
+            zq = sb("zq_%d" % c, [P, v1 - v0], U32)
+            zs = sb("zs_%d" % c, [P, v1 - v0], U8)
+            nc.vector.quantize_mx(zq[:].bitcast(FP8X4), zs[:], zb[:].rearrange("p v t -> p (v t)"))
+            for a in range(BLOCKS):
+                acc = bank("product", 3)
+                nc.tensor.matmul_mx(
+                    acc[:, 0 : v1 - v0], lhsT=w2w[:, 2 * P * a : 2 * P * (a + 1)].bitcast(FP4X4),
+                    lhsT_scale=w2s[:, P * a : P * (a + 1)],
+                    rhs=zq[:].bitcast(FP8X4), rhs_scale=zs[:], start=True, stop=True,
+                )
+                if last and a == 0:
+                    nc.vector.tensor_scalar(g[a][:, v0:v1], acc[:, 0 : v1 - v0], 0.0, None, MAX)
+                else:
+                    nc.scalar.activation(g[a][:, v0:v1], acc[:, 0 : v1 - v0], RELU)
+
+        def next_h(a):
+            if a + 2 < BLOCKS:
+                round_w1(a + 2)
+                quantise_w1(a + 2)
+            if a + 2 < BLOCKS:
+                for j0 in (0, 512):
+                    first_product(a + 2, j0, j0 + 512)
+
+        for j0 in (0, 512):
+            first_product(1, j0, j0 + 512)
+        zb_prev = hop1_chunk(0, next_h)
+        for c in range(1, len(V_CHUNKS)):
+            zb_prev = hop1_chunk(c, lambda a, c=c, zb=zb_prev: second_product(c - 1, zb) if a == 1 else None)
+        second_product(len(V_CHUNKS) - 1, zb_prev)
+
+        codes = sb("codes", [P, U], U32)
+        scales = sb("scales", [P, U], U8)
+        out_rows = out_0.rearrange("(p t) r -> p t r", t=PACK)
+        code_rows = out_1[0].rearrange("p r t -> p (r t)").bitcast(I32)
+
+        def hop2_chunk(c, between):
+            r0, r1 = R_CHUNKS[c]
+            last = c == len(R_CHUNKS) - 1
+            sums = bank("sums", 3)
+            ot = sb("ot_%d" % c, [P, PACK, P], F32)
+            for a in range(BLOCKS):
+                if last and a == BLOCKS - 1:
+                    nc.scalar.copy(ot[:, :, 0:96], sums[:, 0:384].rearrange("r (p t) -> r t p", t=PACK))
+                    sums = bank("sums", 3)
+                weighted_sums("term2_%d" % c, a, g[a], nxt_t, gate2_t, r0, r0, r1, [sums[:, a * P : (a + 1) * P]])
+                between(a)
+            if last:
+                nc.vector.tensor_copy(ot[:, :, 96:128], sums[:, 384:512].rearrange("r (p t) -> r t p", t=PACK))
+            else:
+                nc.scalar.copy(ot[:], sums[:].rearrange("r (p t) -> r t p", t=PACK))
+            y = sb("y_%d" % c, [P, PACK, P], F32)
+            yb = sb("yb_%d" % c, [P, P, PACK], BF16)
+            if last:
+                for half in range(2):
+                    back = bank("back", 2)
+                    for t in range(2):
+                        nc.tensor.transpose(back[:, t * P : (t + 1) * P], ot[:, 2 * half + t, :], ident[:])
+                    dst = y[:, 2 * half : 2 * half + 2, :].rearrange("p t r -> p (t r)")
+                    if half == 0:
+                        nc.scalar.copy(dst, back[:, 0 : 2 * P])
+                    else:
+                        nc.vector.tensor_copy(dst, back[:, 0 : 2 * P])
+                nc.sync.dma_start(out_rows[:, :, r0:r1], y[:])
+                nc.vector.tensor_copy(yb[:], y[:].rearrange("p t r -> p r t"))
+            else:
+                back = bank("back", 2)
+                for t in range(PACK):
+                    nc.tensor.transpose(back[:, t * P : (t + 1) * P], ot[:, t, :], ident[:])
+                nc.scalar.copy(y[:].rearrange("p t r -> p (t r)"), back[:])
+                nc.sync.dma_start(out_rows[:, :, r0:r1], y[:])
+                nc.scalar.copy(yb[:], y[:].rearrange("p t r -> p r t"))
+            return yb
+
+        def planes(c, yb):
+            r0, r1 = R_CHUNKS[c]
+            nc.vector.quantize_mx(codes[:, r0:r1].bitcast(FP8X4), scales[:, r0:r1], yb[:].rearrange("p r t -> p (r t)"))
+            nc.sync.dma_start(code_rows[:, r0:r1], codes[:, r0:r1].bitcast(I32))
+
+        yb_prev = hop2_chunk(0, lambda a: None)
+        yb_last = hop2_chunk(1, lambda a: planes(0, yb_prev) if a == 2 else None)
+        planes(1, yb_last)
+        for q in range(4):
+            queue = nc.scalar if q % 2 else nc.sync
+            queue.dma_start(out_2[0, 4 * q : 4 * q + 4, :].bitcast(I32), scales[32 * q : 32 * q + 4, :].bitcast(I32))

@@ -1,7 +1,6 @@
 from contextlib import ExitStack
 
 import concourse.mybir as mybir
-from concourse.masks import make_identity
 
 K, T, S, D, V, H, U = 512, 2048, 1024, 3, 512, 512, 256
 FLOPS = 2 * K * H * S + 2 * H * H * V
@@ -14,16 +13,19 @@ U16 = mybir.dt.uint16
 U8 = mybir.dt.uint8
 FP8X4 = mybir.dt.float8_e4m3fn_x4
 FP4X4 = mybir.dt.float4_e2m1fn_x4
+ABS = mybir.ActivationFunctionType.Abs
 RELU = mybir.ActivationFunctionType.Relu
 MULT = mybir.AluOpType.mult
-MAX = mybir.AluOpType.max
 
 P = 128
 PACK = 4
 BLOCKS = H // P
+QUARTER = P // BLOCKS
+BANK = 512
 X_PIECES = ((0, 512), (512, 768), (768, 1024))
-V_CHUNKS = ((0, 256), (256, 384), (384, 512))
-R_CHUNKS = ((0, 128), (128, 256))
+V_PIECES = ((0, 256), (256, 384), (384, 512))
+R_PIECES = ((0, 128), (128, 256))
+TERM_TILES = 6
 
 
 def tile_picked_hop2_relu_po_kernel(
@@ -39,12 +41,17 @@ def tile_picked_hop2_relu_po_kernel(
             return keep.tile(shape, dtype, name=name, align_bytes=64)
 
         def bank(tag, bufs):
-            return psum.tile([P, 512], F32, name=tag, tag=tag, bufs=bufs)
+            return psum.tile([P, BANK], F32, name=tag, tag=tag, bufs=bufs)
 
         def load_list(name, src):
             lst = keep.tile(list(src.shape), U16, name=name)
             nc.sync.dma_start(lst[:], src)
             return lst
+
+        def load(name, src):
+            dst = sb(name, list(src.shape), F32)
+            nc.sync.dma_start(dst[:], src)
+            return dst
 
         def load_scale_rows(plane, rows):
             for q in range(4):
@@ -55,37 +62,33 @@ def tile_picked_hop2_relu_po_kernel(
         w2s = sb("w2s", [P, H], U8)
         nc.vector.memset(w2s[:].bitcast(I32), 0)
         ident = sb("ident", [P, P], F32)
-        make_identity(nc, ident[:])
-        warm = sb("warm", [P, 1], F32)
-        nc.scalar.activation(warm[:], ident[:, 0:1], RELU)
+        row_less_column = sb("row_less_column", [P, P], F32)
+        nc.gpsimd.iota(row_less_column[:], [[-1, P]], base=0, channel_multiplier=1, allow_small_or_imprecise_dtypes=True)
+        distance = sb("distance", [P, P], F32)
+        nc.scalar.activation(distance[:], row_less_column[:], ABS)
+        nc.scalar.activation(ident[:], distance[:], RELU, bias=1.0, scale=-1.0)
 
         w1_rows = w1.rearrange("(p j) c -> p j c", j=PACK)
-
-        def load_w1(a, queue):
-            raw = keep.tile([P, PACK, P], F32, name="w1_raw", tag="w1_raw", bufs=2, align_bytes=64)
-            queue.dma_start(raw[:], w1_rows[:, :, a * P : (a + 1) * P])
-            return raw
-
         offs_t = load_list("offs_t", offs)
-        w1_raw = [load_w1(0, nc.sync)]
+        pos_t = [load_list("pos1_t", pos1)]
         load_scale_rows(xs, x_scales[0])
+        w1_b0 = load("w1_b0", w1_rows[:, :, 0:P])
         xw = sb("xw", [P, T], U32)
         nc.sync.dma_start(xw[:].bitcast(I32), x_words[0].rearrange("p n t -> p (n t)").bitcast(I32))
-        w1_raw.append(load_w1(1, nc.sync))
-        pos_t = [load_list("pos%d_t" % d, src) for d, src in enumerate((pos1, pos2, pos3))]
-        gate_rows = gate.rearrange("d p v -> p d v")
-        gate_t = []
-        for c, (v0, v1) in enumerate(V_CHUNKS):
-            gate_t.append(sb("gate_%d" % c, [P, D, v1 - v0], F32))
-        nc.sync.dma_start(gate_t[0][:], gate_rows[:, :, V_CHUNKS[0][0] : V_CHUNKS[0][1]])
-        for c in range(1, len(V_CHUNKS)):
-            nc.sync.dma_start(gate_t[c][:], gate_rows[:, :, V_CHUNKS[c][0] : V_CHUNKS[c][1]])
+        gate_t = [load("gate_0", gate[0])]
+        w1_b1 = load("w1_b1", w1_rows[:, :, P : 2 * P])
+        pos_t.append(load_list("pos2_t", pos2))
+        pos_t.append(load_list("pos3_t", pos3))
+        gate_t.append(load("gate_1", gate[1]))
+        w1_b23 = load("w1_b23", w1_rows[:, :, 2 * P : H])
+        gate_t.append(load("gate_2", gate[2]))
         w2w = sb("w2w", [P, 2 * H], U8)
         nc.sync.dma_start(w2w[:].bitcast(I32), w2_words[0].bitcast(I32))
         load_scale_rows(w2s, w2_scales[0])
         nxt_t = [load_list("nxt%d_t" % d, src) for d, src in enumerate((nxt1, nxt2, nxt3))]
-        gate2_t = sb("gate2_t", [P, D, U], F32)
-        nc.sync.dma_start(gate2_t[:], gate2.rearrange("d p r -> p d r"))
+        gate2_all = load("gate2_all", gate2.rearrange("d p r -> p d r"))
+        gate2_t = [gate2_all[:, d, :] for d in range(D)]
+        w1_raw = [w1_b0[:], w1_b1[:], w1_b23[:, :, 0:P], w1_b23[:, :, P : 2 * P]]
 
         xq = sb("xq", [P, S], U32)
         xqs = sb("xqs", [P, S], U8)
@@ -95,163 +98,119 @@ def tile_picked_hop2_relu_po_kernel(
         h = [sb("h%d" % a, [P, S], F32) for a in range(BLOCKS)]
         g = [sb("g%d" % a, [P, V], F32) for a in range(BLOCKS)]
 
-        def round_w1(a):
-            nc.scalar.copy(w1_bf[a][:], w1_raw[a][:].rearrange("p j c -> p c j"))
-            if a + 2 < BLOCKS:
-                w1_raw.append(load_w1(a + 2, nc.scalar))
-
-        def quantise_w1(a):
+        def quantise_w1(a, copy):
+            copy(w1_bf[a][:], w1_raw[a].rearrange("p j c -> p c j"))
             nc.vector.quantize_mx(w1q[a][:].bitcast(FP8X4), w1s[a][:], w1_bf[a][:].rearrange("p c j -> p (c j)"))
 
-        def gather_words(j0, j1):
-            nc.vector.tensor_copy(xq[:, j0:j1], xw[:].indirect(offs_t[:, j0 // 16 : j1 // 16]))
-
-        def first_product(a, j0, j1):
+        def product(dst, lhsT, lhsT_scale, rhs, rhs_scale, c0, c1):
             acc = bank("product", 3)
             nc.tensor.matmul_mx(
-                acc[:, 0 : j1 - j0], lhsT=w1q[a][:].bitcast(FP8X4), lhsT_scale=w1s[a][:],
-                rhs=xq[:, j0:j1].bitcast(FP8X4), rhs_scale=xqs[:, j0:j1], start=True, stop=True,
+                acc[:, 0 : c1 - c0], lhsT=lhsT, lhsT_scale=lhsT_scale,
+                rhs=rhs[:, c0:c1].bitcast(FP8X4), rhs_scale=rhs_scale[:, c0:c1], start=True, stop=True,
             )
-            nc.scalar.activation(h[a][:, j0:j1], acc[:, 0 : j1 - j0], RELU)
+            nc.scalar.activation(dst[:, c0:c1], acc[:, 0 : c1 - c0], RELU)
+
+        def first_product(a, j0, j1):
+            product(h[a], w1q[a][:].bitcast(FP8X4), w1s[a][:], xq, xqs, j0, j1)
+
+        def first_product_block(a, copy):
+            quantise_w1(a, copy)
+            for j0 in range(0, S, BANK):
+                first_product(a, j0, j0 + BANK)
 
         nc.vector.tensor_copy(xqs[:], xs[:].indirect(offs_t[:]))
-        round_w1(0)
-        gather_words(*X_PIECES[0])
-        quantise_w1(0)
-        first_product(0, *X_PIECES[0])
-        round_w1(1)
-        for piece in X_PIECES[1:]:
-            gather_words(*piece)
-            first_product(0, *piece)
-        quantise_w1(1)
+        quantise_w1(0, nc.scalar.copy)
+        for j0, j1 in X_PIECES:
+            nc.vector.tensor_copy(xq[:, j0:j1], xw[:].indirect(offs_t[:, j0 // 16 : j1 // 16]))
+            first_product(0, j0, j1)
+        first_product_block(1, nc.vector.tensor_copy)
 
-        def weighted_sums(name, a, window, lists, weights, w0, c0, c1, sums):
+        def turned_sums(window, lists, weights, c0, c1):
+            sums = bank("sums", 3)
+            n_sub = (c1 - c0) // P
             for d in range(D):
-                term = keep.tile([P, c1 - c0], F32, name="term", tag="term", bufs=6, align_bytes=64)
+                term = keep.tile([P, c1 - c0], F32, name="term", tag="term", bufs=TERM_TILES, align_bytes=64)
                 nc.vector.tensor_tensor(
-                    term[:], window[:].indirect(lists[d][:, c0 // 16 : c1 // 16]), weights[:, d, w0 : w0 + c1 - c0], MULT
+                    term[:], window[:].indirect(lists[d][:, c0 // 16 : c1 // 16]), weights[d][:, c0:c1], MULT
                 )
-                for s, dst in enumerate(sums):
-                    nc.tensor.matmul(
-                        dst, lhsT=term[:, s * P : (s + 1) * P], rhs=ident[:],
-                        start=(d == 0), stop=(d == D - 1), is_transpose=True,
-                    )
-
-        def hop1_chunk(c, between):
-            v0, v1 = V_CHUNKS[c]
-            last = c == len(V_CHUNKS) - 1
-            n_sub = (v1 - v0) // P
-            banks = [bank("sums", 3) for s in range(n_sub)]
-            zt = [sb("zt_%d_%d" % (c, s), [P, 2, P, 2], BF16) for s in range(n_sub)]
-            for a in range(BLOCKS):
-                if last and a == BLOCKS - 1:
-                    nc.scalar.copy(zt[0][:, :, 0:96, :], banks[0][:, 0:384].rearrange("v (p u e) -> v u p e", u=2, e=2))
-                    banks = [bank("sums", 3)]
-                weighted_sums("term1_%d" % c, a, h[a], pos_t, gate_t[c], 0, v0, v1, [b[:, a * P : (a + 1) * P] for b in banks])
-                between(a)
-            if last:
-                nc.vector.tensor_copy(zt[0][:, :, 96:128, :], banks[0][:, 384:512].rearrange("v (p u e) -> v u p e", u=2, e=2))
-            else:
                 for s in range(n_sub):
-                    nc.scalar.copy(zt[s][:], banks[s][:].rearrange("v (p u e) -> v u p e", u=2, e=2))
-            zb = sb("zb_%d" % c, [P, v1 - v0, PACK], BF16)
-            for s in range(n_sub):
-                back = bank("back", 2)
-                words = zt[s][:].rearrange("v u p e -> v (u p e)").bitcast(F32)
-                for u in range(2):
-                    nc.tensor.transpose(back[:, u * P : (u + 1) * P], words[:, u * P : (u + 1) * P], ident[:])
-                dst = zb[:, s * P : (s + 1) * P, :].rearrange("p v t -> p (v t)").bitcast(F32).rearrange("p (v u) -> p v u", u=2)
-                src = back[:, 0 : 2 * P].rearrange("p (u v) -> p v u", u=2)
-                if last:
-                    nc.vector.tensor_copy(dst, src)
-                else:
-                    nc.scalar.copy(dst, src)
-            return zb
+                    nc.tensor.matmul(
+                        sums[:, s * P : (s + 1) * P], lhsT=term[:, s * P : (s + 1) * P], rhs=ident[:],
+                        start=(d == 0 and s == 0), stop=(d == D - 1 and s == n_sub - 1), is_transpose=True,
+                    )
+            return sums[:, 0 : c1 - c0]
 
-        def second_product(c, zb):
-            v0, v1 = V_CHUNKS[c]
-            last = c == len(V_CHUNKS) - 1
-            zq = sb("zq_%d" % c, [P, v1 - v0], U32)
-            zs = sb("zs_%d" % c, [P, v1 - v0], U8)
-            nc.vector.quantize_mx(zq[:].bitcast(FP8X4), zs[:], zb[:].rearrange("p v t -> p (v t)"))
-            for a in range(BLOCKS):
-                acc = bank("product", 3)
-                nc.tensor.matmul_mx(
-                    acc[:, 0 : v1 - v0], lhsT=w2w[:, 2 * P * a : 2 * P * (a + 1)].bitcast(FP4X4),
-                    lhsT_scale=w2s[:, P * a : P * (a + 1)],
-                    rhs=zq[:].bitcast(FP8X4), rhs_scale=zs[:], start=True, stop=True,
-                )
-                if last and a == 0:
-                    nc.vector.tensor_scalar(g[a][:, v0:v1], acc[:, 0 : v1 - v0], 0.0, None, MAX)
-                else:
-                    nc.scalar.activation(g[a][:, v0:v1], acc[:, 0 : v1 - v0], RELU)
+        zt = sb("zt", [P, V // P, 2, P, 2], BF16)
+        zb = sb("zb", [P, V, PACK], BF16)
+        zq = sb("zq", [P, V], U32)
+        zs = sb("zs", [P, V], U8)
 
-        def next_h(a):
+        def hop1(a, v0, v1, copy):
+            sums = turned_sums(h[a], pos_t, gate_t, v0, v1)
+            copy(
+                zt[:, v0 // P : v1 // P, :, a * QUARTER : (a + 1) * QUARTER, :],
+                sums.rearrange("v (s p u e) -> v s u p e", p=QUARTER, u=2, e=2),
+            )
+
+        def second_product(a, v0, v1):
+            product(g[a], w2w[:, 2 * P * a : 2 * P * (a + 1)].bitcast(FP4X4), w2s[:, P * a : P * (a + 1)], zq, zs, v0, v1)
+
+        def quantise_z(v0, v1):
+            back = bank("back", 2)
+            pairs = zt[:].rearrange("v s u p e -> v (s u p e)").bitcast(F32)
+            for n in range(2 * (v1 - v0) // P):
+                first = 2 * v0 + n * P
+                nc.tensor.transpose(back[:, n * P : (n + 1) * P], pairs[:, first : first + P], ident[:])
+            nc.scalar.copy(
+                zb[:, v0:v1, :].rearrange("p v t -> p (v t)").bitcast(F32).rearrange("p (s v u) -> p s v u", v=P, u=2),
+                back[:, 0 : 2 * (v1 - v0)].rearrange("p (s u v) -> p s v u", v=P, u=2),
+            )
+            nc.vector.quantize_mx(zq[:, v0:v1].bitcast(FP8X4), zs[:, v0:v1], zb[:, v0:v1, :].rearrange("p v t -> p (v t)"))
+
+        for a in range(BLOCKS - 1):
             if a + 2 < BLOCKS:
-                round_w1(a + 2)
-                quantise_w1(a + 2)
-            if a + 2 < BLOCKS:
-                for j0 in (0, 512):
-                    first_product(a + 2, j0, j0 + 512)
+                first_product_block(a + 2, nc.scalar.copy)
+            hop1(a, 0, V, nc.scalar.copy)
+        for v0, v1 in V_PIECES:
+            hop1(BLOCKS - 1, v0, v1, nc.vector.tensor_copy if v1 == V else nc.scalar.copy)
+        for v0, v1 in V_PIECES:
+            quantise_z(v0, v1)
+            second_product(0, v0, v1)
+        for a in range(1, BLOCKS):
+            second_product(a, 0, V)
 
-        for j0 in (0, 512):
-            first_product(1, j0, j0 + 512)
-        zb_prev = hop1_chunk(0, next_h)
-        for c in range(1, len(V_CHUNKS)):
-            zb_prev = hop1_chunk(c, lambda a, c=c, zb=zb_prev: second_product(c - 1, zb) if a == 1 else None)
-        second_product(len(V_CHUNKS) - 1, zb_prev)
-
+        yt = sb("yt", [P, U // P, PACK, P], F32)
         codes = sb("codes", [P, U], U32)
         scales = sb("scales", [P, U], U8)
         out_rows = out_0.rearrange("(p t) r -> p t r", t=PACK)
         code_rows = out_1[0].rearrange("p r t -> p (r t)").bitcast(I32)
 
-        def hop2_chunk(c, between):
-            r0, r1 = R_CHUNKS[c]
-            last = c == len(R_CHUNKS) - 1
-            sums = bank("sums", 3)
-            ot = sb("ot_%d" % c, [P, PACK, P], F32)
-            for a in range(BLOCKS):
-                if last and a == BLOCKS - 1:
-                    nc.scalar.copy(ot[:, :, 0:96], sums[:, 0:384].rearrange("r (p t) -> r t p", t=PACK))
-                    sums = bank("sums", 3)
-                weighted_sums("term2_%d" % c, a, g[a], nxt_t, gate2_t, r0, r0, r1, [sums[:, a * P : (a + 1) * P]])
-                between(a)
-            if last:
-                nc.vector.tensor_copy(ot[:, :, 96:128], sums[:, 384:512].rearrange("r (p t) -> r t p", t=PACK))
-            else:
-                nc.scalar.copy(ot[:], sums[:].rearrange("r (p t) -> r t p", t=PACK))
-            y = sb("y_%d" % c, [P, PACK, P], F32)
-            yb = sb("yb_%d" % c, [P, P, PACK], BF16)
-            if last:
-                for half in range(2):
-                    back = bank("back", 2)
-                    for t in range(2):
-                        nc.tensor.transpose(back[:, t * P : (t + 1) * P], ot[:, 2 * half + t, :], ident[:])
-                    dst = y[:, 2 * half : 2 * half + 2, :].rearrange("p t r -> p (t r)")
-                    if half == 0:
-                        nc.scalar.copy(dst, back[:, 0 : 2 * P])
-                    else:
-                        nc.vector.tensor_copy(dst, back[:, 0 : 2 * P])
-                nc.sync.dma_start(out_rows[:, :, r0:r1], y[:])
-                nc.vector.tensor_copy(yb[:], y[:].rearrange("p t r -> p r t"))
-            else:
-                back = bank("back", 2)
-                for t in range(PACK):
-                    nc.tensor.transpose(back[:, t * P : (t + 1) * P], ot[:, t, :], ident[:])
-                nc.scalar.copy(y[:].rearrange("p t r -> p (t r)"), back[:])
-                nc.sync.dma_start(out_rows[:, :, r0:r1], y[:])
-                nc.scalar.copy(yb[:], y[:].rearrange("p t r -> p r t"))
-            return yb
+        def hop2(a, r0, r1, copy):
+            sums = turned_sums(g[a], nxt_t, gate2_t, r0, r1)
+            copy(
+                yt[:, r0 // P : r1 // P, :, a * QUARTER : (a + 1) * QUARTER],
+                sums.rearrange("r (s p t) -> r s t p", p=QUARTER, t=PACK),
+            )
 
-        def planes(c, yb):
-            r0, r1 = R_CHUNKS[c]
+        def hand_out(r0, r1, second_copy):
+            y = sb("y_%d" % r0, [P, PACK, P], F32)
+            yb = sb("yb_%d" % r0, [P, P, PACK], BF16)
+            for half, copy in enumerate((nc.scalar.copy, second_copy)):
+                back = bank("back", 2)
+                for t in range(2):
+                    nc.tensor.transpose(back[:, t * P : (t + 1) * P], yt[:, r0 // P, 2 * half + t, :], ident[:])
+                copy(y[:, 2 * half : 2 * half + 2, :].rearrange("p t r -> p (t r)"), back[:, 0 : 2 * P])
+            nc.sync.dma_start(out_rows[:, :, r0:r1], y[:])
+            second_copy(yb[:], y[:].rearrange("p t r -> p r t"))
             nc.vector.quantize_mx(codes[:, r0:r1].bitcast(FP8X4), scales[:, r0:r1], yb[:].rearrange("p r t -> p (r t)"))
             nc.sync.dma_start(code_rows[:, r0:r1], codes[:, r0:r1].bitcast(I32))
 
-        yb_prev = hop2_chunk(0, lambda a: None)
-        yb_last = hop2_chunk(1, lambda a: planes(0, yb_prev) if a == 2 else None)
-        planes(1, yb_last)
+        for a in range(BLOCKS - 1):
+            hop2(a, 0, U, nc.scalar.copy)
+        for r0, r1 in R_PIECES:
+            hop2(BLOCKS - 1, r0, r1, nc.vector.tensor_copy if r1 == U else nc.scalar.copy)
+        for r0, r1 in R_PIECES:
+            hand_out(r0, r1, nc.vector.tensor_copy if r1 == U else nc.scalar.copy)
         for q in range(4):
             queue = nc.scalar if q % 2 else nc.sync
             queue.dma_start(out_2[0, 4 * q : 4 * q + 4, :].bitcast(I32), scales[32 * q : 32 * q + 4, :].bitcast(I32))

@@ -16,6 +16,7 @@ FP4X4 = mybir.dt.float4_e2m1fn_x4
 ABS = mybir.ActivationFunctionType.Abs
 RELU = mybir.ActivationFunctionType.Relu
 MULT = mybir.AluOpType.mult
+ADD = mybir.AluOpType.add
 
 P = 128
 PACK = 4
@@ -25,7 +26,7 @@ BANK = 512
 X_PIECES = ((0, 512), (512, 768), (768, 1024))
 V_PIECES = ((0, 256), (256, 384), (384, 512))
 R_PIECES = ((0, 128), (128, 256))
-TERM_TILES = 6
+TERM_TILES = 18
 
 
 def tile_picked_hop2_relu_po_kernel(
@@ -36,6 +37,7 @@ def tile_picked_hop2_relu_po_kernel(
     with ExitStack() as ctx:
         keep = ctx.enter_context(tc.tile_pool(name="keep", bufs=1))
         psum = ctx.enter_context(tc.psum_pool(name="psum", bufs=1))
+        reuse = ctx.enter_context(tc.tile_pool(name="reuse", bufs=1))
 
         def sb(name, shape, dtype):
             return keep.tile(shape, dtype, name=name, align_bytes=64)
@@ -53,11 +55,11 @@ def tile_picked_hop2_relu_po_kernel(
             nc.sync.dma_start(dst[:], src)
             return dst
 
-        def load_scale_rows(plane, rows):
+        def load_scale_rows(queue, plane, rows):
             for q in range(4):
-                nc.sync.dma_start(plane[32 * q : 32 * q + 4, :].bitcast(I32), rows[4 * q : 4 * q + 4, :].bitcast(I32))
+                queue.dma_start(plane[32 * q : 32 * q + 4, :].bitcast(I32), rows[4 * q : 4 * q + 4, :].bitcast(I32))
 
-        xs = sb("xs", [P, T], U8)
+        xs = reuse.tile([P, T], U8, name="xs", offset=4096, align_bytes=64)
         nc.gpsimd.memset(xs[:].bitcast(I32), 0)
         w2s = sb("w2s", [P, H], U8)
         nc.vector.memset(w2s[:].bitcast(I32), 0)
@@ -71,26 +73,27 @@ def tile_picked_hop2_relu_po_kernel(
         w1_rows = w1.rearrange("(p j) c -> p j c", j=PACK)
         offs_t = load_list("offs_t", offs)
         pos_t = [load_list("pos1_t", pos1)]
-        load_scale_rows(xs, x_scales[0])
+        load_scale_rows(nc.sync, xs, x_scales[0])
         w1_b0 = load("w1_b0", w1_rows[:, :, 0:P])
         xw = sb("xw", [P, T], U32)
         nc.sync.dma_start(xw[:].bitcast(I32), x_words[0].rearrange("p n t -> p (n t)").bitcast(I32))
-        gate_t = [load("gate_0", gate[0])]
         w1_b1 = load("w1_b1", w1_rows[:, :, P : 2 * P])
+        gate_t = [load("gate_0", gate[0])]
         pos_t.append(load_list("pos2_t", pos2))
         pos_t.append(load_list("pos3_t", pos3))
         gate_t.append(load("gate_1", gate[1]))
         w1_b23 = load("w1_b23", w1_rows[:, :, 2 * P : H])
-        gate_t.append(load("gate_2", gate[2]))
+        gate_t.append(reuse.tile([P, V], F32, name="gate_2", offset=0, align_bytes=64))
+        nc.sync.dma_start(gate_t[2][:], gate[2])
         w2w = sb("w2w", [P, 2 * H], U8)
         nc.sync.dma_start(w2w[:].bitcast(I32), w2_words[0].bitcast(I32))
-        load_scale_rows(w2s, w2_scales[0])
+        load_scale_rows(nc.sync, w2s, w2_scales[0])
         nxt_t = [load_list("nxt%d_t" % d, src) for d, src in enumerate((nxt1, nxt2, nxt3))]
         gate2_all = load("gate2_all", gate2.rearrange("d p r -> p d r"))
         gate2_t = [gate2_all[:, d, :] for d in range(D)]
         w1_raw = [w1_b0[:], w1_b1[:], w1_b23[:, :, 0:P], w1_b23[:, :, P : 2 * P]]
 
-        xq = sb("xq", [P, S], U32)
+        xq = reuse.tile([P, S], U32, name="xq", offset=4096, align_bytes=64)
         xqs = sb("xqs", [P, S], U8)
         w1_bf = [sb("w1_bf%d" % a, [P, P, PACK], BF16) for a in range(BLOCKS)]
         w1q = [sb("w1q%d" % a, [P, P], U32) for a in range(BLOCKS)]
@@ -123,16 +126,22 @@ def tile_picked_hop2_relu_po_kernel(
         for j0, j1 in X_PIECES:
             nc.vector.tensor_copy(xq[:, j0:j1], xw[:].indirect(offs_t[:, j0 // 16 : j1 // 16]))
             first_product(0, j0, j1)
-        first_product_block(1, nc.vector.tensor_copy)
+        first_product_block(1, nc.scalar.copy)
 
-        def turned_sums(window, lists, weights, c0, c1):
-            sums = bank("sums", 3)
+        def weighted_gather(term, window, lists, weights, d, c0, c1):
+            nc.vector.tensor_tensor(
+                term[:], window[:].indirect(lists[d][:, c0 // 16 : c1 // 16]), weights[d][:, c0:c1], MULT
+            )
+
+        def turned_sums(window, lists, weights, c0, c1, last_term=None):
+            sums = bank("sums", 2)
             n_sub = (c1 - c0) // P
             for d in range(D):
-                term = keep.tile([P, c1 - c0], F32, name="term", tag="term", bufs=TERM_TILES, align_bytes=64)
-                nc.vector.tensor_tensor(
-                    term[:], window[:].indirect(lists[d][:, c0 // 16 : c1 // 16]), weights[d][:, c0:c1], MULT
-                )
+                if d == D - 1 and last_term is not None:
+                    term = last_term
+                else:
+                    term = keep.tile([P, c1 - c0], F32, name="term", tag="term", bufs=TERM_TILES, align_bytes=64)
+                weighted_gather(term, window, lists, weights, d, c0, c1)
                 for s in range(n_sub):
                     nc.tensor.matmul(
                         sums[:, s * P : (s + 1) * P], lhsT=term[:, s * P : (s + 1) * P], rhs=ident[:],
@@ -141,76 +150,109 @@ def tile_picked_hop2_relu_po_kernel(
             return sums[:, 0 : c1 - c0]
 
         zt = sb("zt", [P, V // P, 2, P, 2], BF16)
-        zb = sb("zb", [P, V, PACK], BF16)
+        zb = reuse.tile([P, V, PACK], BF16, name="zb", offset=8192, align_bytes=64)
         zq = sb("zq", [P, V], U32)
         zs = sb("zs", [P, V], U8)
 
-        def hop1(a, v0, v1, copy):
-            sums = turned_sums(h[a], pos_t, gate_t, v0, v1)
+        def hop1(a, v0, v1, copy, last_term=None):
+            sums = turned_sums(h[a], pos_t, gate_t, v0, v1, last_term)
             copy(
                 zt[:, v0 // P : v1 // P, :, a * QUARTER : (a + 1) * QUARTER, :],
                 sums.rearrange("v (s p u e) -> v s u p e", p=QUARTER, u=2, e=2),
             )
 
         def second_product(a, v0, v1):
-            product(g[a], w2w[:, 2 * P * a : 2 * P * (a + 1)].bitcast(FP4X4), w2s[:, P * a : P * (a + 1)], zq, zs, v0, v1)
+            product(g[a], w2_dealt[a][0].bitcast(FP4X4), w2_dealt[a][1], zq, zs, v0, v1)
 
-        def quantise_z(v0, v1):
-            back = bank("back", 2)
+        def turn_back_z(v0, v1, copy):
+            back = bank("back", 3)
             pairs = zt[:].rearrange("v s u p e -> v (s u p e)").bitcast(F32)
             for n in range(2 * (v1 - v0) // P):
                 first = 2 * v0 + n * P
                 nc.tensor.transpose(back[:, n * P : (n + 1) * P], pairs[:, first : first + P], ident[:])
-            nc.scalar.copy(
+            copy(
                 zb[:, v0:v1, :].rearrange("p v t -> p (v t)").bitcast(F32).rearrange("p (s v u) -> p s v u", v=P, u=2),
                 back[:, 0 : 2 * (v1 - v0)].rearrange("p (s u v) -> p s v u", v=P, u=2),
             )
+
+        def quantise_z(v0, v1):
             nc.vector.quantize_mx(zq[:, v0:v1].bitcast(FP8X4), zs[:, v0:v1], zb[:, v0:v1, :].rearrange("p v t -> p (v t)"))
+
+        w2w_by_t = w2w[:].rearrange("p (m t b) -> p t m b", t=PACK, b=2)
+        w2s_by_t = w2s[:].rearrange("p (m t) -> p t m", t=PACK)
+        w2_dealt = []
+
+        def deal_w2(t0, t1, offset):
+            n = t1 - t0
+            words = reuse.tile([P, n, P, 2], U8, name="w2w_%d" % t0, offset=offset + n * P, align_bytes=64)
+            plane = reuse.tile([P, n, P], U8, name="w2s_%d" % t0, offset=offset, align_bytes=64)
+            nc.vector.tensor_copy(words[:], w2w_by_t[:, t0:t1])
+            nc.vector.tensor_copy(plane[:], w2s_by_t[:, t0:t1])
+            for t in range(n):
+                w2_dealt.append((words[:, t].rearrange("p m b -> p (m b)"), plane[:, t]))
 
         for a in range(BLOCKS - 1):
             if a + 2 < BLOCKS:
                 first_product_block(a + 2, nc.scalar.copy)
             hop1(a, 0, V, nc.scalar.copy)
-        for v0, v1 in V_PIECES:
-            hop1(BLOCKS - 1, v0, v1, nc.vector.tensor_copy if v1 == V else nc.scalar.copy)
+        first, second, last = V_PIECES
+        hop1(BLOCKS - 1, *first, nc.scalar.copy)
+        hop1(BLOCKS - 1, *second, nc.scalar.copy)
+        turn_back_z(*first, nc.scalar.copy)
+        lt = reuse.tile([P, P], F32, name="last_term", offset=2048, align_bytes=64)
+        hop1(BLOCKS - 1, *last, nc.vector.tensor_copy, lt)
+        deal_w2(0, 1, 0)
+        turn_back_z(*second, nc.scalar.copy)
+        turn_back_z(*last, nc.vector.tensor_copy)
         for v0, v1 in V_PIECES:
             quantise_z(v0, v1)
             second_product(0, v0, v1)
+        deal_w2(1, 2, 2048)
+        deal_w2(2, 4, 8192)
         for a in range(1, BLOCKS):
             second_product(a, 0, V)
 
-        yt = sb("yt", [P, U // P, PACK, P], F32)
+        y = [sb("y_%d" % u, [P, 2, U], F32) for u in range(2)]
+        yb = sb("yb", [P, U, PACK], BF16)
         codes = sb("codes", [P, U], U32)
         scales = sb("scales", [P, U], U8)
         out_rows = out_0.rearrange("(p t) r -> p t r", t=PACK)
         code_rows = out_1[0].rearrange("p r t -> p (r t)").bitcast(I32)
 
-        def hop2(a, r0, r1, copy):
-            sums = turned_sums(g[a], nxt_t, gate2_t, r0, r1)
-            copy(
-                yt[:, r0 // P : r1 // P, :, a * QUARTER : (a + 1) * QUARTER],
-                sums.rearrange("r (s p t) -> r s t p", p=QUARTER, t=PACK),
+        def hop2(t):
+            sums = turned_sums(g[t], nxt_t, gate2_t, 0, U)
+            turned = keep.tile([P, U], F32, name="turned", tag="turned", bufs=2, align_bytes=64)
+            nc.scalar.copy(turned[:], sums)
+            back = bank("back", 3)
+            for s in range(U // P):
+                nc.tensor.transpose(back[:, s * P : (s + 1) * P], turned[:, s * P : (s + 1) * P], ident[:])
+            nc.scalar.copy(y[t // 2][:, t % 2, :], back[:, 0:U])
+
+        def round_pair(copy, u, r0, r1):
+            copy(yb[:, r0:r1, 2 * u : 2 * u + 2], y[u][:, :, r0:r1].rearrange("p e r -> p r e"))
+
+        hop2(0)
+        hop2(1)
+        nc.sync.dma_start(out_rows[:, 0:2, :], y[0][:])
+        hop2(2)
+        nc.sync.dma_start(out_rows[:, 2, :], y[1][:, 0, :])
+        round_pair(nc.scalar.copy, 0, 0, U)
+
+        terms = [sb("last_term_%d" % d, [P, U], F32) for d in range(D)]
+        partial = sb("partial", [P, U], F32)
+        for d in range(D):
+            weighted_gather(terms[d], g[PACK - 1], nxt_t, gate2_t, d, 0, U)
+        nc.vector.tensor_tensor(partial[:], terms[0][:], terms[1][:], ADD)
+        for r0, r1 in R_PIECES:
+            nc.vector.tensor_tensor(y[1][:, 1, r0:r1], partial[:, r0:r1], terms[2][:, r0:r1], ADD)
+        nc.sync.dma_start(out_rows[:, 3, :], y[1][:, 1, :])
+        for r0, r1 in R_PIECES:
+            round_pair(nc.vector.tensor_copy, 1, r0, r1)
+        for r0, r1 in R_PIECES:
+            nc.vector.quantize_mx(
+                codes[:, r0:r1].bitcast(FP8X4), scales[:, r0:r1], yb[:, r0:r1, :].rearrange("p r t -> p (r t)")
             )
-
-        def hand_out(r0, r1, second_copy):
-            y = sb("y_%d" % r0, [P, PACK, P], F32)
-            yb = sb("yb_%d" % r0, [P, P, PACK], BF16)
-            for half, copy in enumerate((nc.scalar.copy, second_copy)):
-                back = bank("back", 2)
-                for t in range(2):
-                    nc.tensor.transpose(back[:, t * P : (t + 1) * P], yt[:, r0 // P, 2 * half + t, :], ident[:])
-                copy(y[:, 2 * half : 2 * half + 2, :].rearrange("p t r -> p (t r)"), back[:, 0 : 2 * P])
-            nc.sync.dma_start(out_rows[:, :, r0:r1], y[:])
-            second_copy(yb[:], y[:].rearrange("p t r -> p r t"))
-            nc.vector.quantize_mx(codes[:, r0:r1].bitcast(FP8X4), scales[:, r0:r1], yb[:].rearrange("p r t -> p (r t)"))
-            nc.sync.dma_start(code_rows[:, r0:r1], codes[:, r0:r1].bitcast(I32))
-
-        for a in range(BLOCKS - 1):
-            hop2(a, 0, U, nc.scalar.copy)
-        for r0, r1 in R_PIECES:
-            hop2(BLOCKS - 1, r0, r1, nc.vector.tensor_copy if r1 == U else nc.scalar.copy)
-        for r0, r1 in R_PIECES:
-            hand_out(r0, r1, nc.vector.tensor_copy if r1 == U else nc.scalar.copy)
+        nc.sync.dma_start(code_rows, codes[:].bitcast(I32))
         for q in range(4):
             queue = nc.scalar if q % 2 else nc.sync
             queue.dma_start(out_2[0, 4 * q : 4 * q + 4, :].bitcast(I32), scales[32 * q : 32 * q + 4, :].bitcast(I32))

@@ -20,13 +20,11 @@ ADD = mybir.AluOpType.add
 
 P = 128
 PACK = 4
-BLOCKS = H // P
-QUARTER = P // BLOCKS
 BANK = 512
-X_PIECES = ((0, 512), (512, 768), (768, 1024))
-V_PIECES = ((0, 256), (256, 384), (384, 512))
-R_PIECES = ((0, 128), (128, 256))
-TERM_TILES = 18
+HALF = V // 2
+KB = 1024
+EARLY = 512
+X_SPLIT = 768
 
 
 def tile_picked_hop2_relu_po_kernel(
@@ -42,8 +40,11 @@ def tile_picked_hop2_relu_po_kernel(
         def sb(name, shape, dtype):
             return keep.tile(shape, dtype, name=name, align_bytes=64)
 
-        def bank(tag, bufs):
-            return psum.tile([P, BANK], F32, name=tag, tag=tag, bufs=bufs)
+        def shared(name, shape, dtype, offset):
+            return reuse.tile(shape, dtype, name=name, offset=offset, align_bytes=64)
+
+        def bank(tag):
+            return psum.tile([P, BANK], F32, name=tag, tag=tag, bufs={"product": 3, "sums": 2, "back": 3}[tag])
 
         def load_list(name, src):
             lst = keep.tile(list(src.shape), U16, name=name)
@@ -55,11 +56,11 @@ def tile_picked_hop2_relu_po_kernel(
             nc.sync.dma_start(dst[:], src)
             return dst
 
-        def load_scale_rows(queue, plane, rows):
+        def load_scale_rows(queues, plane, rows):
             for q in range(4):
-                queue.dma_start(plane[32 * q : 32 * q + 4, :].bitcast(I32), rows[4 * q : 4 * q + 4, :].bitcast(I32))
+                queues[q % len(queues)].dma_start(plane[32 * q : 32 * q + 4, :].bitcast(I32), rows[4 * q : 4 * q + 4, :].bitcast(I32))
 
-        xs = reuse.tile([P, T], U8, name="xs", offset=4096, align_bytes=64)
+        xs = sb("xs", [P, T], U8)
         nc.gpsimd.memset(xs[:].bitcast(I32), 0)
         w2s = sb("w2s", [P, H], U8)
         nc.vector.memset(w2s[:].bitcast(I32), 0)
@@ -71,76 +72,119 @@ def tile_picked_hop2_relu_po_kernel(
         nc.scalar.activation(ident[:], distance[:], RELU, bias=1.0, scale=-1.0)
 
         w1_rows = w1.rearrange("(p j) c -> p j c", j=PACK)
+        word_rows = x_words[0].rearrange("p n t -> p (n t)").bitcast(I32)
         offs_t = load_list("offs_t", offs)
-        pos_t = [load_list("pos1_t", pos1)]
-        load_scale_rows(nc.sync, xs, x_scales[0])
-        w1_b0 = load("w1_b0", w1_rows[:, :, 0:P])
         xw = sb("xw", [P, T], U32)
-        nc.sync.dma_start(xw[:].bitcast(I32), x_words[0].rearrange("p n t -> p (n t)").bitcast(I32))
-        w1_b1 = load("w1_b1", w1_rows[:, :, P : 2 * P])
-        gate_t = [load("gate_0", gate[0])]
-        pos_t.append(load_list("pos2_t", pos2))
-        pos_t.append(load_list("pos3_t", pos3))
-        gate_t.append(load("gate_1", gate[1]))
-        w1_b23 = load("w1_b23", w1_rows[:, :, 2 * P : H])
-        gate_t.append(reuse.tile([P, V], F32, name="gate_2", offset=0, align_bytes=64))
-        nc.sync.dma_start(gate_t[2][:], gate[2])
+        nc.sync.dma_start(xw[:, 0:EARLY].bitcast(I32), word_rows[:, 0:EARLY])
+        load_scale_rows((nc.sync,), xs, x_scales[0])
+        nc.sync.dma_start(xw[:, EARLY:T].bitcast(I32), word_rows[:, EARLY:T])
+        w1_low = load("w1_low", w1_rows[:, :, 0 : H // 2])
+        pos_t = [load_list("pos%d_t" % d, src) for d, src in enumerate((pos1, pos2, pos3))]
+        w1_high = load("w1_high", w1_rows[:, :, H // 2 : H])
+        gate_t = [load("gate_%d" % d, gate[d]) for d in range(D)]
         w2w = sb("w2w", [P, 2 * H], U8)
         nc.sync.dma_start(w2w[:].bitcast(I32), w2_words[0].bitcast(I32))
-        load_scale_rows(nc.sync, w2s, w2_scales[0])
+        load_scale_rows((nc.sync,), w2s, w2_scales[0])
         nxt_t = [load_list("nxt%d_t" % d, src) for d, src in enumerate((nxt1, nxt2, nxt3))]
         gate2_all = load("gate2_all", gate2.rearrange("d p r -> p d r"))
         gate2_t = [gate2_all[:, d, :] for d in range(D)]
-        w1_raw = [w1_b0[:], w1_b1[:], w1_b23[:, :, 0:P], w1_b23[:, :, P : 2 * P]]
 
-        xq = reuse.tile([P, S], U32, name="xq", offset=4096, align_bytes=64)
+        xq = sb("xq", [P, X_SPLIT], U32)
+        xq_last = shared("xq_last", [P, S - X_SPLIT], U32, KB)
         xqs = sb("xqs", [P, S], U8)
-        w1_bf = [sb("w1_bf%d" % a, [P, P, PACK], BF16) for a in range(BLOCKS)]
-        w1q = [sb("w1q%d" % a, [P, P], U32) for a in range(BLOCKS)]
-        w1s = [sb("w1s%d" % a, [P, P], U8) for a in range(BLOCKS)]
-        h = [sb("h%d" % a, [P, S], F32) for a in range(BLOCKS)]
-        g = [sb("g%d" % a, [P, V], F32) for a in range(BLOCKS)]
+        w1_by_t = [half[:].rearrange("k j (p t) -> k p t j", t=PACK) for half in (w1_low, w1_high)]
+        w1_pairs = [shared("w1_pairs0", [P, 64, 2, PACK], BF16, KB), sb("w1_pairs1", [P, 64, 2, PACK], BF16)]
+        w1_odd = sb("w1_odd", [P, 2, P, PACK], BF16)
+        w1_bf = [
+            w1_pairs[0][:].rearrange("k p t j -> k (p t j)"),
+            w1_pairs[1][:].rearrange("k p t j -> k (p t j)"),
+            w1_odd[:, 0].rearrange("k p j -> k (p j)"),
+            w1_odd[:, 1].rearrange("k p j -> k (p j)"),
+        ]
+        w1q = [sb("w1q%d" % a, [P, P], U32) for a in range(PACK)]
+        w1s = [sb("w1s%d" % a, [P, P], U8) for a in range(PACK)]
+        h = [sb("h%d" % a, [P, S], F32) for a in range(PACK)]
+        g = [sb("g%d" % a, [P, V], F32) for a in range(PACK)]
 
-        def quantise_w1(a, copy):
-            copy(w1_bf[a][:], w1_raw[a].rearrange("p j c -> p c j"))
-            nc.vector.quantize_mx(w1q[a][:].bitcast(FP8X4), w1s[a][:], w1_bf[a][:].rearrange("p c j -> p (c j)"))
+        def round_pairs(half, copy):
+            copy(w1_pairs[half][:], w1_by_t[half][:, :, 0:2, :])
 
-        def product(dst, lhsT, lhsT_scale, rhs, rhs_scale, c0, c1):
-            acc = bank("product", 3)
-            nc.tensor.matmul_mx(
-                acc[:, 0 : c1 - c0], lhsT=lhsT, lhsT_scale=lhsT_scale,
-                rhs=rhs[:, c0:c1].bitcast(FP8X4), rhs_scale=rhs_scale[:, c0:c1], start=True, stop=True,
+        def round_odd(half, copy):
+            copy(
+                w1_odd[:, :, 64 * half : 64 * (half + 1), :].rearrange("k t p j -> k p t j"), w1_by_t[half][:, :, 2:4, :]
             )
+
+        def quantise_w1(a):
+            nc.vector.quantize_mx(w1q[a][:].bitcast(FP8X4), w1s[a][:], w1_bf[a])
+
+        def product(dst, tag, lhsT, lhsT_scale, rhs, rhs_scale, cuts):
+            acc = bank(tag)
+            c0, c1 = cuts[0], cuts[-1]
+            for j0, j1 in zip(cuts, cuts[1:]):
+                nc.tensor.matmul_mx(
+                    acc[:, j0 - c0 : j1 - c0], lhsT=lhsT, lhsT_scale=lhsT_scale,
+                    rhs=rhs(j0, j1).bitcast(FP8X4), rhs_scale=rhs_scale[:, j0:j1], start=True, stop=True,
+                )
             nc.scalar.activation(dst[:, c0:c1], acc[:, 0 : c1 - c0], RELU)
 
-        def first_product(a, j0, j1):
-            product(h[a], w1q[a][:].bitcast(FP8X4), w1s[a][:], xq, xqs, j0, j1)
+        def picked(j0, j1):
+            return xq[:, j0:j1] if j1 <= X_SPLIT else xq_last[:]
 
-        def first_product_block(a, copy):
-            quantise_w1(a, copy)
-            for j0 in range(0, S, BANK):
-                first_product(a, j0, j0 + BANK)
+        def first_product(a, tag, cuts):
+            product(h[a], tag, w1q[a][:].bitcast(FP8X4), w1s[a][:], picked, xqs, cuts)
+
+        def gather_words(j0, j1):
+            nc.vector.tensor_copy(picked(j0, j1), xw[:].indirect(offs_t[:, j0 // 16 : j1 // 16]))
 
         nc.vector.tensor_copy(xqs[:], xs[:].indirect(offs_t[:]))
-        quantise_w1(0, nc.scalar.copy)
-        for j0, j1 in X_PIECES:
-            nc.vector.tensor_copy(xq[:, j0:j1], xw[:].indirect(offs_t[:, j0 // 16 : j1 // 16]))
-            first_product(0, j0, j1)
-        first_product_block(1, nc.scalar.copy)
+        round_pairs(0, nc.scalar.copy)
+        gather_words(0, X_SPLIT)
+        quantise_w1(0)
+        gather_words(X_SPLIT, S)
+        round_odd(0, nc.scalar.copy)
+        for n, tag in enumerate(("product", "product", "product", "back")):
+            first_product(0, tag, (256 * n, 256 * (n + 1)))
+        round_pairs(1, nc.vector.tensor_copy)
+        round_odd(1, nc.vector.tensor_copy)
+        for a in range(1, PACK):
+            quantise_w1(a)
+            first_product(a, "product", (0, 512))
+            first_product(a, "product", (512, 768, 1024))
+
+        w2_words_by_t = w2w[:].rearrange("p (m t b) -> p t m b", t=PACK, b=2)
+        w2_plane_by_t = w2s[:].rearrange("p (m t) -> p t m", t=PACK)
+        w2_dealt = []
+
+        def deal_w2(t0, t1, place):
+            n = t1 - t0
+            plane = shared("w2_plane%d" % t0, [P, n, P], U8, place)
+            words = shared("w2_words%d" % t0, [P, n, P, 2], U8, place + n * P)
+            nc.vector.tensor_copy(plane[:], w2_plane_by_t[:, t0:t1])
+            nc.vector.tensor_copy(words[:], w2_words_by_t[:, t0:t1])
+            for t in range(n):
+                w2_dealt.append((words[:, t].rearrange("p m b -> p (m b)").bitcast(FP4X4), plane[:, t]))
+
+        deal_w2(0, 1, 0)
 
         def weighted_gather(term, window, lists, weights, d, c0, c1):
             nc.vector.tensor_tensor(
                 term[:], window[:].indirect(lists[d][:, c0 // 16 : c1 // 16]), weights[d][:, c0:c1], MULT
             )
 
-        def turned_sums(window, lists, weights, c0, c1, last_term=None):
-            sums = bank("sums", 2)
+        def term_tile(name, d, width):
+            return sb("%s_%d" % (name, d), [P, width], F32)
+
+        def gather_terms(name, window, lists, weights, c0, c1):
+            terms = [term_tile(name, d, c1 - c0) for d in range(D)]
+            for d in range(D):
+                weighted_gather(terms[d], window, lists, weights, d, c0, c1)
+            return terms
+
+        def turned_sums(name, window, lists, weights, c0, c1):
+            sums = bank("sums")
             n_sub = (c1 - c0) // P
             for d in range(D):
-                if d == D - 1 and last_term is not None:
-                    term = last_term
-                else:
-                    term = keep.tile([P, c1 - c0], F32, name="term", tag="term", bufs=TERM_TILES, align_bytes=64)
+                term = term_tile(name, d, c1 - c0)
                 weighted_gather(term, window, lists, weights, d, c0, c1)
                 for s in range(n_sub):
                     nc.tensor.matmul(
@@ -149,68 +193,82 @@ def tile_picked_hop2_relu_po_kernel(
                     )
             return sums[:, 0 : c1 - c0]
 
-        zt = sb("zt", [P, V // P, 2, P, 2], BF16)
-        zb = reuse.tile([P, V, PACK], BF16, name="zb", offset=8192, align_bytes=64)
+        def turned_halves(terms):
+            halves = [bank("sums")[:, 0:P], bank("product")[:, 0:P]]
+            for d in range(D):
+                for s in range(2):
+                    nc.tensor.matmul(
+                        halves[s], lhsT=terms[d][:, s * P : (s + 1) * P], rhs=ident[:],
+                        start=(d == 0), stop=(d == D - 1), is_transpose=True,
+                    )
+            return halves
+
+        def turn(dst, src):
+            for s in range(src.shape[1] // P):
+                nc.tensor.transpose(dst[:, s * P : (s + 1) * P], src[:, s * P : (s + 1) * P], ident[:])
+
+        def add_in_halves(name, dst, terms):
+            width = dst.shape[1] // 2
+            partial = sb(name, list(dst.shape), F32)
+            for n in range(2):
+                cols = slice(n * width, (n + 1) * width)
+                nc.vector.tensor_tensor(partial[:, cols], terms[0][:, cols], terms[1][:, cols], ADD)
+            for n in range(2):
+                cols = slice(n * width, (n + 1) * width)
+                nc.vector.tensor_tensor(dst[:, cols], partial[:, cols], terms[2][:, cols], ADD)
+
+        zt01 = sb("zt01", [P, V // P, P, 2], BF16)
+        zt23 = sb("zt23", [P, HALF // P, P, 2], BF16)
+        zb = shared("zb", [P, V, PACK], BF16, 4096)
+        zb_words = zb[:].rearrange("p v t -> p (v t)").bitcast(F32).rearrange("p (v u) -> p v u", u=2)
+        z23 = sb("z23", [P, 2, HALF], F32)
         zq = sb("zq", [P, V], U32)
         zs = sb("zs", [P, V], U8)
 
-        def hop1(a, v0, v1, copy, last_term=None):
-            sums = turned_sums(h[a], pos_t, gate_t, v0, v1, last_term)
-            copy(
-                zt[:, v0 // P : v1 // P, :, a * QUARTER : (a + 1) * QUARTER, :],
-                sums.rearrange("v (s p u e) -> v s u p e", p=QUARTER, u=2, e=2),
-            )
+        def words_of(pairs):
+            return pairs.rearrange("v s p e -> v (s p e)").bitcast(F32)
 
-        def second_product(a, v0, v1):
-            product(g[a], w2_dealt[a][0].bitcast(FP4X4), w2_dealt[a][1], zq, zs, v0, v1)
+        for half in range(2):
+            sums = turned_sums("pair%d" % half, h[half], pos_t, gate_t, 0, V)
+            nc.scalar.copy(zt01[:, :, 64 * half : 64 * (half + 1), :], sums.rearrange("v (s p e) -> v s p e", p=64, e=2))
+        back = bank("back")
+        turn(back, words_of(zt01[:, 2:4]))
+        nc.scalar.copy(zb_words[:, HALF:V, 0], back[:, 0:HALF])
 
-        def turn_back_z(v0, v1, copy):
-            back = bank("back", 3)
-            pairs = zt[:].rearrange("v s u p e -> v (s u p e)").bitcast(F32)
-            for n in range(2 * (v1 - v0) // P):
-                first = 2 * v0 + n * P
-                nc.tensor.transpose(back[:, n * P : (n + 1) * P], pairs[:, first : first + P], ident[:])
-            copy(
-                zb[:, v0:v1, :].rearrange("p v t -> p (v t)").bitcast(F32).rearrange("p (s v u) -> p s v u", v=P, u=2),
-                back[:, 0 : 2 * (v1 - v0)].rearrange("p (s u v) -> p s v u", v=P, u=2),
-            )
+        sums = turned_sums("third", h[2], pos_t, gate_t, 0, V)
+        nc.scalar.copy(zt23[:, :, :, 0], sums[:, 0:HALF].rearrange("v (s p) -> v s p", p=P))
+        turned2 = sb("turned2", [P, HALF], F32)
+        nc.scalar.copy(turned2[:], sums[:, HALF:V])
+        back = bank("back")
+        turn(back, turned2[:])
+        nc.scalar.copy(z23[:, 0, :], back[:, 0:HALF])
 
-        def quantise_z(v0, v1):
+        backs = [bank("back") for s in range(2)]
+        for s in range(2):
+            turn(backs[s][:, 0:P], words_of(zt01[:, s : s + 1]))
+        halves = turned_halves(gather_terms("fourth", h[3], pos_t, gate_t, 0, HALF))
+        for s in range(2):
+            nc.scalar.copy(zt23[:, s, :, 1], halves[s])
+        for s in range(2):
+            turn(backs[s][:, P : 2 * P], words_of(zt23[:, s : s + 1]))
+            nc.scalar.copy(zb_words[:, s * P : (s + 1) * P, :], backs[s][:, 0 : 2 * P].rearrange("p (u v) -> p v u", u=2))
+
+        terms = gather_terms("last", h[3], pos_t, gate_t, HALF, V)
+        add_in_halves("partial_z", z23[:, 1, :], terms)
+        for v0 in (HALF, HALF + P):
+            nc.vector.tensor_copy(zb[:, v0 : v0 + P, 2:4], z23[:, :, v0 - HALF : v0 - HALF + P].rearrange("p e v -> p v e"))
+
+        def second_product(t, tag, v0, v1):
+            product(g[t], tag, w2_dealt[t][0], w2_dealt[t][1], lambda j0, j1: zq[:, j0:j1], zs, (v0, v1))
+
+        for n, tag in enumerate(("product", "product", "product", "sums")):
+            v0, v1 = n * P, (n + 1) * P
             nc.vector.quantize_mx(zq[:, v0:v1].bitcast(FP8X4), zs[:, v0:v1], zb[:, v0:v1, :].rearrange("p v t -> p (v t)"))
-
-        w2w_by_t = w2w[:].rearrange("p (m t b) -> p t m b", t=PACK, b=2)
-        w2s_by_t = w2s[:].rearrange("p (m t) -> p t m", t=PACK)
-        w2_dealt = []
-
-        def deal_w2(t0, t1, offset):
-            n = t1 - t0
-            words = reuse.tile([P, n, P, 2], U8, name="w2w_%d" % t0, offset=offset + n * P, align_bytes=64)
-            plane = reuse.tile([P, n, P], U8, name="w2s_%d" % t0, offset=offset, align_bytes=64)
-            nc.vector.tensor_copy(words[:], w2w_by_t[:, t0:t1])
-            nc.vector.tensor_copy(plane[:], w2s_by_t[:, t0:t1])
-            for t in range(n):
-                w2_dealt.append((words[:, t].rearrange("p m b -> p (m b)"), plane[:, t]))
-
-        for a in range(BLOCKS - 1):
-            if a + 2 < BLOCKS:
-                first_product_block(a + 2, nc.scalar.copy)
-            hop1(a, 0, V, nc.scalar.copy)
-        first, second, last = V_PIECES
-        hop1(BLOCKS - 1, *first, nc.scalar.copy)
-        hop1(BLOCKS - 1, *second, nc.scalar.copy)
-        turn_back_z(*first, nc.scalar.copy)
-        lt = reuse.tile([P, P], F32, name="last_term", offset=2048, align_bytes=64)
-        hop1(BLOCKS - 1, *last, nc.vector.tensor_copy, lt)
-        deal_w2(0, 1, 0)
-        turn_back_z(*second, nc.scalar.copy)
-        turn_back_z(*last, nc.vector.tensor_copy)
-        for v0, v1 in V_PIECES:
-            quantise_z(v0, v1)
-            second_product(0, v0, v1)
-        deal_w2(1, 2, 2048)
-        deal_w2(2, 4, 8192)
-        for a in range(1, BLOCKS):
-            second_product(a, 0, V)
+            second_product(0, tag, v0, v1)
+        deal_w2(1, 2, 4 * KB)
+        deal_w2(2, 4, 5 * KB)
+        for t in range(1, PACK):
+            second_product(t, "product", 0, V)
 
         y = [sb("y_%d" % u, [P, 2, U], F32) for u in range(2)]
         yb = sb("yb", [P, U, PACK], BF16)
@@ -220,12 +278,11 @@ def tile_picked_hop2_relu_po_kernel(
         code_rows = out_1[0].rearrange("p r t -> p (r t)").bitcast(I32)
 
         def hop2(t):
-            sums = turned_sums(g[t], nxt_t, gate2_t, 0, U)
+            sums = turned_sums("root%d" % t, g[t], nxt_t, gate2_t, 0, U)
             turned = keep.tile([P, U], F32, name="turned", tag="turned", bufs=2, align_bytes=64)
             nc.scalar.copy(turned[:], sums)
-            back = bank("back", 3)
-            for s in range(U // P):
-                nc.tensor.transpose(back[:, s * P : (s + 1) * P], turned[:, s * P : (s + 1) * P], ident[:])
+            back = bank("back")
+            turn(back, turned[:])
             nc.scalar.copy(y[t // 2][:, t % 2, :], back[:, 0:U])
 
         def round_pair(copy, u, r0, r1):
@@ -234,23 +291,26 @@ def tile_picked_hop2_relu_po_kernel(
         hop2(0)
         hop2(1)
         nc.sync.dma_start(out_rows[:, 0:2, :], y[0][:])
-        hop2(2)
-        nc.sync.dma_start(out_rows[:, 2, :], y[1][:, 0, :])
         round_pair(nc.scalar.copy, 0, 0, U)
+        halves = turned_halves(gather_terms("root2", g[2], nxt_t, gate2_t, 0, U))
+        turned = [sb("turned_half%d" % s, [P, P], F32) for s in range(2)]
+        for s in range(2):
+            nc.scalar.copy(turned[s][:], halves[s])
+        for s in range(2):
+            back = bank("back")
+            turn(back, turned[s][:])
+            nc.scalar.copy(y[1][:, 0, s * P : (s + 1) * P], back[:, 0:P])
+        nc.sync.dma_start(out_rows[:, 2, :], y[1][:, 0, :])
 
-        terms = [sb("last_term_%d" % d, [P, U], F32) for d in range(D)]
-        partial = sb("partial", [P, U], F32)
-        for d in range(D):
-            weighted_gather(terms[d], g[PACK - 1], nxt_t, gate2_t, d, 0, U)
-        nc.vector.tensor_tensor(partial[:], terms[0][:], terms[1][:], ADD)
-        for r0, r1 in R_PIECES:
-            nc.vector.tensor_tensor(y[1][:, 1, r0:r1], partial[:, r0:r1], terms[2][:, r0:r1], ADD)
+        terms = gather_terms("root3", g[PACK - 1], nxt_t, gate2_t, 0, U)
+        add_in_halves("partial_y", y[1][:, 1, :], terms)
         nc.sync.dma_start(out_rows[:, 3, :], y[1][:, 1, :])
-        for r0, r1 in R_PIECES:
-            round_pair(nc.vector.tensor_copy, 1, r0, r1)
-        for r0, r1 in R_PIECES:
+        for r0 in (0, P):
+            round_pair(nc.vector.tensor_copy, 1, r0, r0 + P)
+        for r0 in (0, P):
             nc.vector.quantize_mx(
-                codes[:, r0:r1].bitcast(FP8X4), scales[:, r0:r1], yb[:, r0:r1, :].rearrange("p r t -> p (r t)")
+                codes[:, r0 : r0 + P].bitcast(FP8X4), scales[:, r0 : r0 + P],
+                yb[:, r0 : r0 + P, :].rearrange("p r t -> p (r t)"),
             )
         nc.sync.dma_start(code_rows, codes[:].bitcast(I32))
         for q in range(4):

@@ -151,18 +151,18 @@ def tile_picked_hop2_relu_po_kernel(
             first_product(a, "product", (0, 512))
             first_product(a, "product", (512, 768, 1024))
 
-        w2_words_by_t = w2w[:].rearrange("p (m t b) -> p t m b", t=PACK, b=2)
+        w2_words_by_t = w2w[:].bitcast(U16).rearrange("p (m t) -> p t m", t=PACK)
         w2_plane_by_t = w2s[:].rearrange("p (m t) -> p t m", t=PACK)
         w2_dealt = []
 
         def deal_w2(t0, t1, place):
             n = t1 - t0
             plane = shared("w2_plane%d" % t0, [P, n, P], U8, place)
-            words = shared("w2_words%d" % t0, [P, n, P, 2], U8, place + n * P)
+            words = shared("w2_words%d" % t0, [P, n, 2 * P], U8, place + n * P)
             nc.vector.tensor_copy(plane[:], w2_plane_by_t[:, t0:t1])
-            nc.vector.tensor_copy(words[:], w2_words_by_t[:, t0:t1])
+            nc.vector.tensor_copy(words[:].bitcast(U16), w2_words_by_t[:, t0:t1])
             for t in range(n):
-                w2_dealt.append((words[:, t].rearrange("p m b -> p (m b)").bitcast(FP4X4), plane[:, t]))
+                w2_dealt.append((words[:, t].bitcast(FP4X4), plane[:, t]))
 
         deal_w2(0, 1, 0)
 

@@ -79,9 +79,12 @@ def tile_picked_hop2_relu_po_kernel(
         load_scale_rows((nc.sync,), xs, x_scales[0])
         nc.sync.dma_start(xw[:, EARLY:T].bitcast(I32), word_rows[:, EARLY:T])
         w1_low = load("w1_low", w1_rows[:, :, 0 : H // 2])
-        pos_t = [load_list("pos%d_t" % d, src) for d, src in enumerate((pos1, pos2, pos3))]
         w1_high = load("w1_high", w1_rows[:, :, H // 2 : H])
-        gate_t = [load("gate_%d" % d, gate[d]) for d in range(D)]
+        pos_t = [load_list("pos0_t", pos1)]
+        gate_t = [load("gate_0", gate[0])]
+        for d, src in ((1, pos2), (2, pos3)):
+            pos_t.append(load_list("pos%d_t" % d, src))
+            gate_t.append(load("gate_%d" % d, gate[d]))
         w2w = sb("w2w", [P, 2 * H], U8)
         nc.sync.dma_start(w2w[:].bitcast(I32), w2_words[0].bitcast(I32))
         load_scale_rows((nc.sync,), w2s, w2_scales[0])
@@ -90,24 +93,25 @@ def tile_picked_hop2_relu_po_kernel(
         gate2_t = [gate2_all[:, d, :] for d in range(D)]
 
         xq = sb("xq", [P, X_SPLIT], U32)
-        xq_last = shared("xq_last", [P, S - X_SPLIT], U32, KB)
+        xq_last = shared("xq_last", [P, S - X_SPLIT], U32, KB // 2)
         xqs = sb("xqs", [P, S], U8)
         w1_by_t = [half[:].rearrange("k j (p t) -> k p t j", t=PACK) for half in (w1_low, w1_high)]
-        w1_pairs = [shared("w1_pairs0", [P, 64, 2, PACK], BF16, KB), sb("w1_pairs1", [P, 64, 2, PACK], BF16)]
-        w1_odd = sb("w1_odd", [P, 2, P, PACK], BF16)
+        w1_bf0 = shared("w1_bf0", [P, P, PACK], BF16, KB)
+        w1_rest = shared("w1_rest", [P, 3, P, PACK], BF16, 3 * KB // 2)
+        w1_pairs = [t.rearrange("k (p t) j -> k p t j", t=2) for t in (w1_bf0[:], w1_rest[:, 0])]
+        w1_odd = w1_rest[:, 1:3]
         w1_bf = [
-            w1_pairs[0][:].rearrange("k p t j -> k (p t j)"),
-            w1_pairs[1][:].rearrange("k p t j -> k (p t j)"),
-            w1_odd[:, 0].rearrange("k p j -> k (p j)"),
-            w1_odd[:, 1].rearrange("k p j -> k (p j)"),
+            w1_bf0[:].rearrange("k m j -> k (m j)"),
+            w1_rest[:, 0].rearrange("k m j -> k (m j)"),
+            w1_odd.rearrange("k t p j -> k (t p j)"),
         ]
-        w1q = [sb("w1q%d" % a, [P, P], U32) for a in range(PACK)]
-        w1s = [sb("w1s%d" % a, [P, P], U8) for a in range(PACK)]
+        w1q = sb("w1q", [P, H], U32)
+        w1s = sb("w1s", [P, H], U8)
         h = [sb("h%d" % a, [P, S], F32) for a in range(PACK)]
         g = [sb("g%d" % a, [P, V], F32) for a in range(PACK)]
 
         def round_pairs(half, copy):
-            copy(w1_pairs[half][:], w1_by_t[half][:, :, 0:2, :])
+            copy(w1_pairs[half], w1_by_t[half][:, :, 0:2, :])
 
         def round_odd(half, copy):
             copy(
@@ -115,7 +119,8 @@ def tile_picked_hop2_relu_po_kernel(
             )
 
         def quantise_w1(a):
-            nc.vector.quantize_mx(w1q[a][:].bitcast(FP8X4), w1s[a][:], w1_bf[a])
+            cols = slice(a * P, a * P + w1_bf[a].shape[1] // PACK)
+            nc.vector.quantize_mx(w1q[:, cols].bitcast(FP8X4), w1s[:, cols], w1_bf[a])
 
         def product(dst, tag, lhsT, lhsT_scale, rhs, rhs_scale, cuts):
             acc = bank(tag)
@@ -131,7 +136,8 @@ def tile_picked_hop2_relu_po_kernel(
             return xq[:, j0:j1] if j1 <= X_SPLIT else xq_last[:]
 
         def first_product(a, tag, cuts):
-            product(h[a], tag, w1q[a][:].bitcast(FP8X4), w1s[a][:], picked, xqs, cuts)
+            cols = slice(a * P, (a + 1) * P)
+            product(h[a], tag, w1q[:, cols].bitcast(FP8X4), w1s[:, cols], picked, xqs, cuts)
 
         def gather_words(j0, j1):
             nc.vector.tensor_copy(picked(j0, j1), xw[:].indirect(offs_t[:, j0 // 16 : j1 // 16]))
@@ -146,21 +152,22 @@ def tile_picked_hop2_relu_po_kernel(
             first_product(0, tag, (256 * n, 256 * (n + 1)))
         round_pairs(1, nc.vector.tensor_copy)
         round_odd(1, nc.vector.tensor_copy)
+        quantise_w1(1)
+        quantise_w1(2)
         for a in range(1, PACK):
-            quantise_w1(a)
             first_product(a, "product", (0, 512))
             first_product(a, "product", (512, 768, 1024))
 
-        w2_words_by_t = w2w[:].bitcast(U16).rearrange("p (m t) -> p t m", t=PACK)
-        w2_plane_by_t = w2s[:].rearrange("p (m t) -> p t m", t=PACK)
+        w2_words_by_t = w2w[:].bitcast(U16).rearrange("p (h m t) -> p h t m", h=2, t=PACK)
+        w2_plane_by_t = w2s[:].rearrange("p (h m t) -> p h t m", h=2, t=PACK)
         w2_dealt = []
 
         def deal_w2(t0, t1, place):
             n = t1 - t0
             plane = shared("w2_plane%d" % t0, [P, n, P], U8, place)
             words = shared("w2_words%d" % t0, [P, n, 2 * P], U8, place + n * P)
-            nc.vector.tensor_copy(plane[:], w2_plane_by_t[:, t0:t1])
-            nc.vector.tensor_copy(words[:].bitcast(U16), w2_words_by_t[:, t0:t1])
+            nc.vector.tensor_copy(plane[:].rearrange("p t (h m) -> p h t m", h=2), w2_plane_by_t[:, :, t0:t1])
+            nc.vector.tensor_copy(words[:].bitcast(U16).rearrange("p t (h m) -> p h t m", h=2), w2_words_by_t[:, :, t0:t1])
             for t in range(n):
                 w2_dealt.append((words[:, t].bitcast(FP4X4), plane[:, t]))
 
@@ -219,7 +226,7 @@ def tile_picked_hop2_relu_po_kernel(
 
         zt01 = sb("zt01", [P, V // P, P, 2], BF16)
         zt23 = sb("zt23", [P, HALF // P, P, 2], BF16)
-        zb = shared("zb", [P, V, PACK], BF16, 4096)
+        zb = shared("zb", [P, V, PACK], BF16, 5 * KB)
         zb_words = zb[:].rearrange("p v t -> p (v t)").bitcast(F32).rearrange("p (v u) -> p v u", u=2)
         z23 = sb("z23", [P, 2, HALF], F32)
         zq = sb("zq", [P, V], U32)
@@ -265,8 +272,7 @@ def tile_picked_hop2_relu_po_kernel(
             v0, v1 = n * P, (n + 1) * P
             nc.vector.quantize_mx(zq[:, v0:v1].bitcast(FP8X4), zs[:, v0:v1], zb[:, v0:v1, :].rearrange("p v t -> p (v t)"))
             second_product(0, tag, v0, v1)
-        deal_w2(1, 2, 4 * KB)
-        deal_w2(2, 4, 5 * KB)
+        deal_w2(1, PACK, 5 * KB)
         for t in range(1, PACK):
             second_product(t, "product", 0, V)
 

@@ -14,6 +14,7 @@ U8 = mybir.dt.uint8
 FP8X4 = mybir.dt.float8_e4m3fn_x4
 FP4X4 = mybir.dt.float4_e2m1fn_x4
 ABS = mybir.ActivationFunctionType.Abs
+COPY = mybir.ActivationFunctionType.Copy
 RELU = mybir.ActivationFunctionType.Relu
 MULT = mybir.AluOpType.mult
 ADD = mybir.AluOpType.add
@@ -154,7 +155,8 @@ def tile_picked_hop2_relu_po_kernel(
         round_odd(1, nc.vector.tensor_copy)
         quantise_w1(1)
         quantise_w1(2)
-        for a in range(1, PACK):
+
+        def whole_product(a):
             first_product(a, "product", (0, 512))
             first_product(a, "product", (512, 768, 1024))
 
@@ -173,32 +175,28 @@ def tile_picked_hop2_relu_po_kernel(
 
         deal_w2(0, 1, 0)
 
-        def weighted_gather(term, window, lists, weights, d, c0, c1):
-            nc.vector.tensor_tensor(
-                term[:], window[:].indirect(lists[d][:, c0 // 16 : c1 // 16]), weights[d][:, c0:c1], MULT
-            )
+        def weighted(name, window, lst, weight, c0, c1):
+            term = sb(name, [P, c1 - c0], F32)
+            nc.vector.tensor_tensor(term[:], window[:].indirect(lst[:, c0 // 16 : c1 // 16]), weight[:, c0:c1], MULT)
+            return term
 
-        def term_tile(name, d, width):
-            return sb("%s_%d" % (name, d), [P, width], F32)
+        def fetched(name, window, lst, c0, c1):
+            raw = sb(name, [P, c1 - c0], F32)
+            nc.scalar.activation(raw[:], window[:].indirect(lst[:, c0 // 16 : c1 // 16]), COPY)
+            return raw
 
-        def gather_terms(name, window, lists, weights, c0, c1):
-            terms = [term_tile(name, d, c1 - c0) for d in range(D)]
-            for d in range(D):
-                weighted_gather(terms[d], window, lists, weights, d, c0, c1)
-            return terms
+        def weigh(name, raw, weight):
+            term = sb(name, list(raw.shape), F32)
+            nc.vector.tensor_tensor(term[:], raw, weight, MULT)
+            return term
 
-        def turned_sums(name, window, lists, weights, c0, c1):
-            sums = bank("sums")
-            n_sub = (c1 - c0) // P
-            for d in range(D):
-                term = term_tile(name, d, c1 - c0)
-                weighted_gather(term, window, lists, weights, d, c0, c1)
-                for s in range(n_sub):
-                    nc.tensor.matmul(
-                        sums[:, s * P : (s + 1) * P], lhsT=term[:, s * P : (s + 1) * P], rhs=ident[:],
-                        start=(d == 0 and s == 0), stop=(d == D - 1 and s == n_sub - 1), is_transpose=True,
-                    )
-            return sums[:, 0 : c1 - c0]
+        def add_turned(sums, term, first, last):
+            n_sub = term.shape[1] // P
+            for s in range(n_sub):
+                nc.tensor.matmul(
+                    sums[:, s * P : (s + 1) * P], lhsT=term[:, s * P : (s + 1) * P], rhs=ident[:],
+                    start=(first and s == 0), stop=(last and s == n_sub - 1), is_transpose=True,
+                )
 
         def turned_halves(terms):
             halves = [bank("sums")[:, 0:P], bank("product")[:, 0:P]]
@@ -235,17 +233,38 @@ def tile_picked_hop2_relu_po_kernel(
         def words_of(pairs):
             return pairs.rearrange("v s p e -> v (s p e)").bitcast(F32)
 
-        for half in range(2):
-            sums = turned_sums("pair%d" % half, h[half], pos_t, gate_t, 0, V)
-            nc.scalar.copy(zt01[:, :, 64 * half : 64 * (half + 1), :], sums.rearrange("v (s p e) -> v s p e", p=64, e=2))
+        def sort_pairs(half, sums):
+            nc.scalar.copy(zt01[:, :, 64 * half : 64 * (half + 1), :], sums[:].rearrange("v (s p e) -> v s p e", p=64, e=2))
+
+        whole_product(1)
+        sums0 = bank("sums")
+        for d in range(2):
+            add_turned(sums0, weighted("z0_%d" % d, h[0], pos_t[d], gate_t[d], 0, V), d == 0, False)
+        raw0 = fetched("raw0", h[0], pos_t[2], 0, V)
+        whole_product(2)
+        sums1 = bank("sums")
+        add_turned(sums1, weighted("z1_0", h[1], pos_t[0], gate_t[0], 0, V), True, False)
+        add_turned(sums0, weigh("z0_2", raw0[:], gate_t[2][:]), False, True)
+        raw1 = fetched("raw1", h[1], pos_t[2], 0, V)
+        whole_product(3)
+        add_turned(sums1, weighted("z1_1", h[1], pos_t[1], gate_t[1], 0, V), False, False)
+        add_turned(sums1, weigh("z1_2", raw1[:], gate_t[2][:]), False, True)
+        raw2 = fetched("raw2", h[2], pos_t[2], 0, V)
+        sort_pairs(0, sums0)
+        raw3 = fetched("raw3", h[3], pos_t[2], 0, V)
+        sums2 = bank("sums")
+        for d in range(2):
+            add_turned(sums2, weighted("z2_%d" % d, h[2], pos_t[d], gate_t[d], 0, V), d == 0, False)
+        add_turned(sums2, weigh("z2_2", raw2[:], gate_t[2][:]), False, True)
+        sort_pairs(1, sums1)
+        raw3a = fetched("raw3a", h[3], pos_t[1], 0, HALF)
         back = bank("back")
         turn(back, words_of(zt01[:, 2:4]))
         nc.scalar.copy(zb_words[:, HALF:V, 0], back[:, 0:HALF])
 
-        sums = turned_sums("third", h[2], pos_t, gate_t, 0, V)
-        nc.scalar.copy(zt23[:, :, :, 0], sums[:, 0:HALF].rearrange("v (s p) -> v s p", p=P))
+        nc.scalar.copy(zt23[:, :, :, 0], sums2[:, 0:HALF].rearrange("v (s p) -> v s p", p=P))
         turned2 = sb("turned2", [P, HALF], F32)
-        nc.scalar.copy(turned2[:], sums[:, HALF:V])
+        nc.scalar.copy(turned2[:], sums2[:, HALF:V])
         back = bank("back")
         turn(back, turned2[:])
         nc.scalar.copy(z23[:, 0, :], back[:, 0:HALF])
@@ -253,15 +272,18 @@ def tile_picked_hop2_relu_po_kernel(
         backs = [bank("back") for s in range(2)]
         for s in range(2):
             turn(backs[s][:, 0:P], words_of(zt01[:, s : s + 1]))
-        halves = turned_halves(gather_terms("fourth", h[3], pos_t, gate_t, 0, HALF))
+        z3a_0 = weighted("z3a_0", h[3], pos_t[0], gate_t[0], 0, HALF)
+        z3_2 = weigh("z3_2", raw3[:], gate_t[2][:])
+        z3a_1 = weigh("z3a_1", raw3a[:], gate_t[1][:, 0:HALF])
+        halves = turned_halves([z3a_0, z3_2, z3a_1])
         for s in range(2):
             nc.scalar.copy(zt23[:, s, :, 1], halves[s])
         for s in range(2):
             turn(backs[s][:, P : 2 * P], words_of(zt23[:, s : s + 1]))
             nc.scalar.copy(zb_words[:, s * P : (s + 1) * P, :], backs[s][:, 0 : 2 * P].rearrange("p (u v) -> p v u", u=2))
 
-        terms = gather_terms("last", h[3], pos_t, gate_t, HALF, V)
-        add_in_halves("partial_z", z23[:, 1, :], terms)
+        terms = [weighted("z3b_%d" % d, h[3], pos_t[d], gate_t[d], HALF, V)[:] for d in range(2)]
+        add_in_halves("partial_z", z23[:, 1, :], [z3_2[:, HALF:V]] + terms)
         for v0 in (HALF, HALF + P):
             nc.vector.tensor_copy(zb[:, v0 : v0 + P, 2:4], z23[:, :, v0 - HALF : v0 - HALF + P].rearrange("p e v -> p v e"))
 
@@ -273,8 +295,6 @@ def tile_picked_hop2_relu_po_kernel(
             nc.vector.quantize_mx(zq[:, v0:v1].bitcast(FP8X4), zs[:, v0:v1], zb[:, v0:v1, :].rearrange("p v t -> p (v t)"))
             second_product(0, tag, v0, v1)
         deal_w2(1, PACK, 5 * KB)
-        for t in range(1, PACK):
-            second_product(t, "product", 0, V)
 
         y = [sb("y_%d" % u, [P, 2, U], F32) for u in range(2)]
         yb = sb("yb", [P, U, PACK], BF16)
@@ -283,10 +303,9 @@ def tile_picked_hop2_relu_po_kernel(
         out_rows = out_0.rearrange("(p t) r -> p t r", t=PACK)
         code_rows = out_1[0].rearrange("p r t -> p (r t)").bitcast(I32)
 
-        def hop2(t):
-            sums = turned_sums("root%d" % t, g[t], nxt_t, gate2_t, 0, U)
+        def bring_back(t, sums):
             turned = keep.tile([P, U], F32, name="turned", tag="turned", bufs=2, align_bytes=64)
-            nc.scalar.copy(turned[:], sums)
+            nc.scalar.copy(turned[:], sums[:, 0:U])
             back = bank("back")
             turn(back, turned[:])
             nc.scalar.copy(y[t // 2][:, t % 2, :], back[:, 0:U])
@@ -294,11 +313,27 @@ def tile_picked_hop2_relu_po_kernel(
         def round_pair(copy, u, r0, r1):
             copy(yb[:, r0:r1, 2 * u : 2 * u + 2], y[u][:, :, r0:r1].rearrange("p e r -> p r e"))
 
-        hop2(0)
-        hop2(1)
+        second_product(1, "product", 0, V)
+        sums0 = bank("sums")
+        for d in range(2):
+            add_turned(sums0, weighted("y0_%d" % d, g[0], nxt_t[d], gate2_t[d], 0, U), d == 0, False)
+        raw0 = fetched("root0", g[0], nxt_t[2], 0, U)
+        second_product(2, "product", 0, V)
+        sums1 = bank("sums")
+        add_turned(sums1, weighted("y1_0", g[1], nxt_t[0], gate2_t[0], 0, U), True, False)
+        add_turned(sums0, weigh("y0_2", raw0[:], gate2_t[2]), False, True)
+        raw1 = fetched("root1", g[1], nxt_t[2], 0, U)
+        second_product(3, "product", 0, V)
+        add_turned(sums1, weighted("y1_1", g[1], nxt_t[1], gate2_t[1], 0, U), False, False)
+        add_turned(sums1, weigh("y1_2", raw1[:], gate2_t[2]), False, True)
+        raw2 = fetched("root2", g[2], nxt_t[2], 0, U)
+        raw3 = fetched("root3", g[3], nxt_t[2], 0, U)
+        terms2 = [weighted("y2_%d" % d, g[2], nxt_t[d], gate2_t[d], 0, U) for d in range(2)]
+        terms2.append(weigh("y2_2", raw2[:], gate2_t[2]))
+        bring_back(0, sums0)
+        bring_back(1, sums1)
         nc.sync.dma_start(out_rows[:, 0:2, :], y[0][:])
-        round_pair(nc.scalar.copy, 0, 0, U)
-        halves = turned_halves(gather_terms("root2", g[2], nxt_t, gate2_t, 0, U))
+        halves = turned_halves(terms2)
         turned = [sb("turned_half%d" % s, [P, P], F32) for s in range(2)]
         for s in range(2):
             nc.scalar.copy(turned[s][:], halves[s])
@@ -308,8 +343,11 @@ def tile_picked_hop2_relu_po_kernel(
             nc.scalar.copy(y[1][:, 0, s * P : (s + 1) * P], back[:, 0:P])
         nc.sync.dma_start(out_rows[:, 2, :], y[1][:, 0, :])
 
-        terms = gather_terms("root3", g[PACK - 1], nxt_t, gate2_t, 0, U)
-        add_in_halves("partial_y", y[1][:, 1, :], terms)
+        y3_0 = weighted("y3_0", g[3], nxt_t[0], gate2_t[0], 0, U)
+        y3_2 = weigh("y3_2", raw3[:], gate2_t[2])
+        y3_1 = weighted("y3_1", g[3], nxt_t[1], gate2_t[1], 0, U)
+        add_in_halves("partial_y", y[1][:, 1, :], [y3_0, y3_2, y3_1])
+        round_pair(nc.vector.tensor_copy, 0, 0, U)
         nc.sync.dma_start(out_rows[:, 3, :], y[1][:, 1, :])
         for r0 in (0, P):
             round_pair(nc.vector.tensor_copy, 1, r0, r0 + P)

@@ -81,11 +81,13 @@ def tile_picked_hop2_relu_po_kernel(
         nc.sync.dma_start(xw[:, EARLY:T].bitcast(I32), word_rows[:, EARLY:T])
         w1_low = load("w1_low", w1_rows[:, :, 0 : H // 2])
         w1_high = load("w1_high", w1_rows[:, :, H // 2 : H])
-        pos_t = [load_list("pos0_t", pos1)]
-        gate_t = [load("gate_0", gate[0])]
-        for d, src in ((1, pos2), (2, pos3)):
+        third_list = load_list("pos2_t", pos3)
+        pos_t, gate_t = [], []
+        for d, src in enumerate((pos1, pos2)):
             pos_t.append(load_list("pos%d_t" % d, src))
             gate_t.append(load("gate_%d" % d, gate[d]))
+        pos_t.append(third_list)
+        gate_t.append(load("gate_2", gate[2]))
         w2w = sb("w2w", [P, 2 * H], U8)
         nc.sync.dma_start(w2w[:].bitcast(I32), w2_words[0].bitcast(I32))
         load_scale_rows((nc.sync,), w2s, w2_scales[0])
@@ -97,13 +99,12 @@ def tile_picked_hop2_relu_po_kernel(
         xq_last = shared("xq_last", [P, S - X_SPLIT], U32, KB // 2)
         xqs = sb("xqs", [P, S], U8)
         w1_by_t = [half[:].rearrange("k j (p t) -> k p t j", t=PACK) for half in (w1_low, w1_high)]
-        w1_bf0 = shared("w1_bf0", [P, P, PACK], BF16, KB)
         w1_rest = shared("w1_rest", [P, 3, P, PACK], BF16, 3 * KB // 2)
-        w1_pairs = [t.rearrange("k (p t) j -> k p t j", t=2) for t in (w1_bf0[:], w1_rest[:, 0])]
+        w1_pairs = [shared("w1_first", [P, 64, 2, PACK], BF16, KB)[:], w1_rest[:, 0].rearrange("k (p t) j -> k p t j", t=2)]
         w1_odd = w1_rest[:, 1:3]
         w1_bf = [
-            w1_bf0[:].rearrange("k m j -> k (m j)"),
-            w1_rest[:, 0].rearrange("k m j -> k (m j)"),
+            w1_pairs[0].rearrange("k p t j -> k (p t j)"),
+            w1_pairs[1].rearrange("k p t j -> k (p t j)"),
             w1_odd.rearrange("k t p j -> k (t p j)"),
         ]
         w1q = sb("w1q", [P, H], U32)
@@ -123,22 +124,26 @@ def tile_picked_hop2_relu_po_kernel(
             cols = slice(a * P, a * P + w1_bf[a].shape[1] // PACK)
             nc.vector.quantize_mx(w1q[:, cols].bitcast(FP8X4), w1s[:, cols], w1_bf[a])
 
-        def product(dst, tag, lhsT, lhsT_scale, rhs, rhs_scale, cuts):
+        def empty_scalar(dst, src):
+            nc.scalar.activation(dst, src, RELU)
+
+        def product(dst, tag, lhsT, lhsT_scale, parts, rhs_scale, empty):
             acc = bank(tag)
-            c0, c1 = cuts[0], cuts[-1]
-            for j0, j1 in zip(cuts, cuts[1:]):
+            c0, c1 = parts[0][0], parts[-1][1]
+            for j0, j1, words in parts:
                 nc.tensor.matmul_mx(
                     acc[:, j0 - c0 : j1 - c0], lhsT=lhsT, lhsT_scale=lhsT_scale,
-                    rhs=rhs(j0, j1).bitcast(FP8X4), rhs_scale=rhs_scale[:, j0:j1], start=True, stop=True,
+                    rhs=words.bitcast(FP8X4), rhs_scale=rhs_scale[:, j0:j1], start=True, stop=True,
                 )
-            nc.scalar.activation(dst[:, c0:c1], acc[:, 0 : c1 - c0], RELU)
+            empty(dst[:, c0:c1], acc[:, 0 : c1 - c0])
 
         def picked(j0, j1):
             return xq[:, j0:j1] if j1 <= X_SPLIT else xq_last[:]
 
         def first_product(a, tag, cuts):
             cols = slice(a * P, (a + 1) * P)
-            product(h[a], tag, w1q[:, cols].bitcast(FP8X4), w1s[:, cols], picked, xqs, cuts)
+            parts = [(j0, j1, picked(j0, j1)) for j0, j1 in zip(cuts, cuts[1:])]
+            product(h[a], tag, w1q[:, cols].bitcast(FP8X4), w1s[:, cols], parts, xqs, empty_scalar)
 
         def gather_words(j0, j1):
             nc.vector.tensor_copy(picked(j0, j1), xw[:].indirect(offs_t[:, j0 // 16 : j1 // 16]))
@@ -156,9 +161,9 @@ def tile_picked_hop2_relu_po_kernel(
         quantise_w1(1)
         quantise_w1(2)
 
-        def whole_product(a):
-            first_product(a, "product", (0, 512))
-            first_product(a, "product", (512, 768, 1024))
+        def whole_product(a, tags):
+            first_product(a, tags[0], (0, 512))
+            first_product(a, tags[1], (512, 768, 1024))
 
         w2_words_by_t = w2w[:].bitcast(U16).rearrange("p (h m t) -> p h t m", h=2, t=PACK)
         w2_plane_by_t = w2s[:].rearrange("p (h m t) -> p h t m", h=2, t=PACK)
@@ -173,127 +178,119 @@ def tile_picked_hop2_relu_po_kernel(
             for t in range(n):
                 w2_dealt.append((words[:, t].bitcast(FP4X4), plane[:, t]))
 
-        deal_w2(0, 1, 0)
+        def weighted(dst, window, lst, weight, c0, c1):
+            nc.vector.tensor_tensor(dst, window[:].indirect(lst[:, c0 // 16 : c1 // 16]), weight[:, c0:c1], MULT)
+            return dst
 
-        def weighted(name, window, lst, weight, c0, c1):
-            term = sb(name, [P, c1 - c0], F32)
-            nc.vector.tensor_tensor(term[:], window[:].indirect(lst[:, c0 // 16 : c1 // 16]), weight[:, c0:c1], MULT)
-            return term
+        def fetched(dst, window, lst, c0, c1):
+            nc.scalar.activation(dst, window[:].indirect(lst[:, c0 // 16 : c1 // 16]), COPY)
+            return dst
 
-        def fetched(name, window, lst, c0, c1):
-            raw = sb(name, [P, c1 - c0], F32)
-            nc.scalar.activation(raw[:], window[:].indirect(lst[:, c0 // 16 : c1 // 16]), COPY)
-            return raw
+        def weigh(dst, raw, weight):
+            nc.vector.tensor_tensor(dst, raw, weight, MULT)
+            return dst
 
-        def weigh(name, raw, weight):
-            term = sb(name, list(raw.shape), F32)
-            nc.vector.tensor_tensor(term[:], raw, weight, MULT)
-            return term
+        def term(name, width):
+            return sb(name, [P, width], F32)[:]
 
-        def add_turned(sums, term, first, last):
-            n_sub = term.shape[1] // P
-            for s in range(n_sub):
+        def add_turned(sums, src, first, last):
+            for s in range(len(sums)):
                 nc.tensor.matmul(
-                    sums[:, s * P : (s + 1) * P], lhsT=term[:, s * P : (s + 1) * P], rhs=ident[:],
-                    start=(first and s == 0), stop=(last and s == n_sub - 1), is_transpose=True,
+                    sums[s], lhsT=src[:, s * P : (s + 1) * P], rhs=ident[:],
+                    start=(first and s == 0), stop=(last and s == len(sums) - 1), is_transpose=True,
                 )
 
-        def turned_halves(terms):
-            halves = [bank("sums")[:, 0:P], bank("product")[:, 0:P]]
-            for d in range(D):
-                for s in range(2):
-                    nc.tensor.matmul(
-                        halves[s], lhsT=terms[d][:, s * P : (s + 1) * P], rhs=ident[:],
-                        start=(d == 0), stop=(d == D - 1), is_transpose=True,
-                    )
-            return halves
+        def pieces(acc, n):
+            return [acc[:, s * P : (s + 1) * P] for s in range(n)]
 
         def turn(dst, src):
             for s in range(src.shape[1] // P):
                 nc.tensor.transpose(dst[:, s * P : (s + 1) * P], src[:, s * P : (s + 1) * P], ident[:])
 
-        def add_in_halves(name, dst, terms):
-            width = dst.shape[1] // 2
-            partial = sb(name, list(dst.shape), F32)
-            for n in range(2):
-                cols = slice(n * width, (n + 1) * width)
-                nc.vector.tensor_tensor(partial[:, cols], terms[0][:, cols], terms[1][:, cols], ADD)
-            for n in range(2):
-                cols = slice(n * width, (n + 1) * width)
-                nc.vector.tensor_tensor(dst[:, cols], partial[:, cols], terms[2][:, cols], ADD)
-
         zt01 = sb("zt01", [P, V // P, P, 2], BF16)
         zt23 = sb("zt23", [P, HALF // P, P, 2], BF16)
-        zb = shared("zb", [P, V, PACK], BF16, 5 * KB)
-        zb_words = zb[:].rearrange("p v t -> p (v t)").bitcast(F32).rearrange("p (v u) -> p v u", u=2)
-        z23 = sb("z23", [P, 2, HALF], F32)
+        zb = [sb("zb0", [P, HALF, PACK], BF16), sb("zb1", [P, P, PACK], BF16), shared("zb2", [P, P, PACK], BF16, 5 * KB)]
+        late = [sb("late%d" % n, [P, 2, P], F32) for n in range(2)]
         zq = sb("zq", [P, V], U32)
         zs = sb("zs", [P, V], U8)
 
         def words_of(pairs):
             return pairs.rearrange("v s p e -> v (s p e)").bitcast(F32)
 
+        def as_words(t):
+            return t[:].rearrange("p v t -> p (v t)").bitcast(F32).rearrange("p (v u) -> p v u", u=2)
+
         def sort_pairs(half, sums):
             nc.scalar.copy(zt01[:, :, 64 * half : 64 * (half + 1), :], sums[:].rearrange("v (s p e) -> v s p e", p=64, e=2))
 
-        whole_product(1)
+        def quantise_z(n, v0):
+            v1 = v0 + zb[n].shape[1]
+            nc.vector.quantize_mx(zq[:, v0:v1].bitcast(FP8X4), zs[:, v0:v1], zb[n][:].rearrange("p v t -> p (v t)"))
+
+        def second_product(t, tag, v0, v1, empty=empty_scalar):
+            product(g[t], tag, w2_dealt[t][0], w2_dealt[t][1], [(v0, v1, zq[:, v0:v1])], zs, empty)
+
+        whole_product(1, ("back", "back"))
         sums0 = bank("sums")
         for d in range(2):
-            add_turned(sums0, weighted("z0_%d" % d, h[0], pos_t[d], gate_t[d], 0, V), d == 0, False)
-        raw0 = fetched("raw0", h[0], pos_t[2], 0, V)
-        whole_product(2)
+            add_turned(pieces(sums0, 4), weighted(term("z0_%d" % d, V), h[0], pos_t[d], gate_t[d], 0, V), d == 0, False)
+        raw0 = fetched(term("raw0", V), h[0], pos_t[2], 0, V)
+        whole_product(2, ("product", "product"))
         sums1 = bank("sums")
-        add_turned(sums1, weighted("z1_0", h[1], pos_t[0], gate_t[0], 0, V), True, False)
-        add_turned(sums0, weigh("z0_2", raw0[:], gate_t[2][:]), False, True)
-        raw1 = fetched("raw1", h[1], pos_t[2], 0, V)
-        whole_product(3)
-        add_turned(sums1, weighted("z1_1", h[1], pos_t[1], gate_t[1], 0, V), False, False)
-        add_turned(sums1, weigh("z1_2", raw1[:], gate_t[2][:]), False, True)
-        raw2 = fetched("raw2", h[2], pos_t[2], 0, V)
+        add_turned(pieces(sums1, 4), weighted(term("z1_0", V), h[1], pos_t[0], gate_t[0], 0, V), True, False)
+        add_turned(pieces(sums0, 4), weigh(term("z0_2", V), raw0, gate_t[2][:]), False, True)
+        raw1 = fetched(term("raw1", V), h[1], pos_t[2], 0, V)
+        whole_product(3, ("product", "back"))
+        add_turned(pieces(sums1, 4), weighted(term("z1_1", V), h[1], pos_t[1], gate_t[1], 0, V), False, False)
+        add_turned(pieces(sums1, 4), weigh(term("z1_2", V), raw1, gate_t[2][:]), False, True)
+
+        raw23 = [fetched(shared("raw%d" % a, [P, V], F32, (4 + 2 * a) * KB)[:], h[a], pos_t[2], 0, V) for a in (2, 3)]
+        third = sb("third", [P, 2, V], F32)
+        sums23 = bank("back")
+        by_tile = sums23[:].rearrange("v (s e p) -> v s e p", s=2, e=2)
+        for e in range(2):
+            places = [by_tile[:, s, e, :] for s in range(2)]
+            for d in range(2):
+                src = weighted(term("z%d_%d" % (2 + e, d), HALF), h[2 + e], pos_t[d], gate_t[d], 0, HALF)
+                add_turned(places, src, e == 0 and d == 0, False)
+            add_turned(places, weigh(third[:, e, :], raw23[e], gate_t[2][:]), False, e == 1)
         sort_pairs(0, sums0)
-        raw3 = fetched("raw3", h[3], pos_t[2], 0, V)
-        sums2 = bank("sums")
-        for d in range(2):
-            add_turned(sums2, weighted("z2_%d" % d, h[2], pos_t[d], gate_t[d], 0, V), d == 0, False)
-        add_turned(sums2, weigh("z2_2", raw2[:], gate_t[2][:]), False, True)
         sort_pairs(1, sums1)
-        raw3a = fetched("raw3a", h[3], pos_t[1], 0, HALF)
+        late_raw = sb("late_raw", [P, 2, HALF], F32)
+        for e in range(2):
+            fetched(late_raw[:, e, :], h[2 + e], pos_t[1], HALF, V)
         back = bank("back")
         turn(back, words_of(zt01[:, 2:4]))
-        nc.scalar.copy(zb_words[:, HALF:V, 0], back[:, 0:HALF])
-
-        nc.scalar.copy(zt23[:, :, :, 0], sums2[:, 0:HALF].rearrange("v (s p) -> v s p", p=P))
-        turned2 = sb("turned2", [P, HALF], F32)
-        nc.scalar.copy(turned2[:], sums2[:, HALF:V])
+        for n in range(2):
+            nc.scalar.copy(late[n][:, 0, :], back[:, n * P : (n + 1) * P])
+        nc.scalar.copy(zt23[:], by_tile.rearrange("v s e p -> v s p e"))
         back = bank("back")
-        turn(back, turned2[:])
-        nc.scalar.copy(z23[:, 0, :], back[:, 0:HALF])
+        turn(back[:, 0:HALF], words_of(zt01[:, 0:2]))
+        turn(back[:, HALF:V], words_of(zt23[:]))
+        nc.scalar.copy(as_words(zb[0]), back[:].rearrange("p (u v) -> p v u", u=2))
 
-        backs = [bank("back") for s in range(2)]
-        for s in range(2):
-            turn(backs[s][:, 0:P], words_of(zt01[:, s : s + 1]))
-        z3a_0 = weighted("z3a_0", h[3], pos_t[0], gate_t[0], 0, HALF)
-        z3_2 = weigh("z3_2", raw3[:], gate_t[2][:])
-        z3a_1 = weigh("z3a_1", raw3a[:], gate_t[1][:, 0:HALF])
-        halves = turned_halves([z3a_0, z3_2, z3a_1])
-        for s in range(2):
-            nc.scalar.copy(zt23[:, s, :, 1], halves[s])
-        for s in range(2):
-            turn(backs[s][:, P : 2 * P], words_of(zt23[:, s : s + 1]))
-            nc.scalar.copy(zb_words[:, s * P : (s + 1) * P, :], backs[s][:, 0 : 2 * P].rearrange("p (u v) -> p v u", u=2))
-
-        terms = [weighted("z3b_%d" % d, h[3], pos_t[d], gate_t[d], HALF, V)[:] for d in range(2)]
-        add_in_halves("partial_z", z23[:, 1, :], [z3_2[:, HALF:V]] + terms)
-        for v0 in (HALF, HALF + P):
-            nc.vector.tensor_copy(zb[:, v0 : v0 + P, 2:4], z23[:, :, v0 - HALF : v0 - HALF + P].rearrange("p e v -> p v e"))
-
-        def second_product(t, tag, v0, v1):
-            product(g[t], tag, w2_dealt[t][0], w2_dealt[t][1], lambda j0, j1: zq[:, j0:j1], zs, (v0, v1))
-
-        for n, tag in enumerate(("product", "product", "product", "sums")):
-            v0, v1 = n * P, (n + 1) * P
-            nc.vector.quantize_mx(zq[:, v0:v1].bitcast(FP8X4), zs[:, v0:v1], zb[:, v0:v1, :].rearrange("p v t -> p (v t)"))
-            second_product(0, tag, v0, v1)
+        late_first = shared("late_first", [P, 2, HALF], F32, 10 * KB)
+        for e in range(2):
+            weighted(late_first[:, e, :], h[2 + e], pos_t[0], gate_t[0], HALF, V)
+        late_second = sb("late_second", [P, 2, HALF], F32)
+        weigh(late_second[:], late_raw[:], gate_t[1][:, HALF:V].unsqueeze(1).to_broadcast([P, 2, HALF]))
+        partial = sb("partial_z", [P, 2, HALF], F32)
+        nc.vector.tensor_tensor(partial[:], late_first[:], third[:, :, HALF:V], ADD)
+        deal_w2(0, 1, 0)
+        for n in range(2):
+            cols = slice(n * P, (n + 1) * P)
+            nc.vector.tensor_tensor(
+                late[n][:, 1, :].bitcast(BF16).rearrange("p (v e) -> p v e", e=2),
+                partial[:, :, cols].rearrange("p e v -> p v e"), late_second[:, :, cols].rearrange("p e v -> p v e"), ADD,
+            )
+        quantise_z(0, 0)
+        second_product(0, "product", 0, HALF)
+        for n in range(2):
+            nc.vector.tensor_copy(as_words(zb[1 + n]), late[n][:].rearrange("p u v -> p v u"))
+        for n in range(2):
+            v0 = HALF + n * P
+            quantise_z(1 + n, v0)
+            second_product(0, "product", v0, v0 + P)
         deal_w2(1, PACK, 5 * KB)
 
         y = [sb("y_%d" % u, [P, 2, U], F32) for u in range(2)]
@@ -303,51 +300,57 @@ def tile_picked_hop2_relu_po_kernel(
         out_rows = out_0.rearrange("(p t) r -> p t r", t=PACK)
         code_rows = out_1[0].rearrange("p r t -> p (r t)").bitcast(I32)
 
-        def bring_back(t, sums):
-            turned = keep.tile([P, U], F32, name="turned", tag="turned", bufs=2, align_bytes=64)
-            nc.scalar.copy(turned[:], sums[:, 0:U])
+        def take_turned(t, sums):
+            turned = term("turned%d" % t, U)
+            nc.scalar.copy(turned, sums[:, 0:U])
             back = bank("back")
-            turn(back, turned[:])
+            turn(back, turned)
+            return back
+
+        def take_back(t, back):
             nc.scalar.copy(y[t // 2][:, t % 2, :], back[:, 0:U])
 
         def round_pair(copy, u, r0, r1):
             copy(yb[:, r0:r1, 2 * u : 2 * u + 2], y[u][:, :, r0:r1].rearrange("p e r -> p r e"))
 
-        second_product(1, "product", 0, V)
+        second_product(1, "sums", 0, V)
         sums0 = bank("sums")
         for d in range(2):
-            add_turned(sums0, weighted("y0_%d" % d, g[0], nxt_t[d], gate2_t[d], 0, U), d == 0, False)
-        raw0 = fetched("root0", g[0], nxt_t[2], 0, U)
-        second_product(2, "product", 0, V)
-        sums1 = bank("sums")
-        add_turned(sums1, weighted("y1_0", g[1], nxt_t[0], gate2_t[0], 0, U), True, False)
-        add_turned(sums0, weigh("y0_2", raw0[:], gate2_t[2]), False, True)
-        raw1 = fetched("root1", g[1], nxt_t[2], 0, U)
-        second_product(3, "product", 0, V)
-        add_turned(sums1, weighted("y1_1", g[1], nxt_t[1], gate2_t[1], 0, U), False, False)
-        add_turned(sums1, weigh("y1_2", raw1[:], gate2_t[2]), False, True)
-        raw2 = fetched("root2", g[2], nxt_t[2], 0, U)
-        raw3 = fetched("root3", g[3], nxt_t[2], 0, U)
-        terms2 = [weighted("y2_%d" % d, g[2], nxt_t[d], gate2_t[d], 0, U) for d in range(2)]
-        terms2.append(weigh("y2_2", raw2[:], gate2_t[2]))
-        bring_back(0, sums0)
-        bring_back(1, sums1)
+            add_turned(pieces(sums0, 2), weighted(term("y0_%d" % d, U), g[0], nxt_t[d], gate2_t[d], 0, U), d == 0, False)
+        raw0 = fetched(term("root0", U), g[0], nxt_t[2], 0, U)
+        second_product(2, "back", 0, V)
+        sums1 = bank("product")
+        add_turned(pieces(sums1, 2), weighted(term("y1_0", U), g[1], nxt_t[0], gate2_t[0], 0, U), True, False)
+        add_turned(pieces(sums0, 2), weigh(term("y0_2", U), raw0, gate2_t[2]), False, True)
+        raw1 = fetched(term("root1", U), g[1], nxt_t[2], 0, U)
+        second_product(3, "back", 0, V)
+        add_turned(pieces(sums1, 2), weighted(term("y1_1", U), g[1], nxt_t[1], gate2_t[1], 0, U), False, False)
+        add_turned(pieces(sums1, 2), weigh(term("y1_2", U), raw1, gate2_t[2]), False, True)
+        raw2 = [fetched(term("root2_%d" % d, U), g[2], nxt_t[d], 0, U) for d in (1, 2)]
+        raw3 = fetched(term("root3", U), g[3], nxt_t[2], 0, U)
+        sums2 = bank("product")
+        add_turned(pieces(sums2, 2), weighted(term("y2_0", U), g[2], nxt_t[0], gate2_t[0], 0, U), True, False)
+        for d in (1, 2):
+            add_turned(pieces(sums2, 2), weigh(term("y2_%d" % d, U), raw2[d - 1], gate2_t[d]), False, d == 2)
+        back0 = take_turned(0, sums0)
+        back1 = take_turned(1, sums1)
+        take_back(0, back0)
+        back2 = take_turned(2, sums2)
+        take_back(1, back1)
         nc.sync.dma_start(out_rows[:, 0:2, :], y[0][:])
-        halves = turned_halves(terms2)
-        turned = [sb("turned_half%d" % s, [P, P], F32) for s in range(2)]
-        for s in range(2):
-            nc.scalar.copy(turned[s][:], halves[s])
-        for s in range(2):
-            back = bank("back")
-            turn(back, turned[s][:])
-            nc.scalar.copy(y[1][:, 0, s * P : (s + 1) * P], back[:, 0:P])
+        take_back(2, back2)
         nc.sync.dma_start(out_rows[:, 2, :], y[1][:, 0, :])
+        round_pair(nc.scalar.copy, 0, 0, U)
 
-        y3_0 = weighted("y3_0", g[3], nxt_t[0], gate2_t[0], 0, U)
-        y3_2 = weigh("y3_2", raw3[:], gate2_t[2])
-        y3_1 = weighted("y3_1", g[3], nxt_t[1], gate2_t[1], 0, U)
-        add_in_halves("partial_y", y[1][:, 1, :], [y3_0, y3_2, y3_1])
-        round_pair(nc.vector.tensor_copy, 0, 0, U)
+        y3_0 = weighted(term("y3_0", U), g[3], nxt_t[0], gate2_t[0], 0, U)
+        y3_2 = weigh(term("y3_2", U), raw3, gate2_t[2])
+        y3_1 = weighted(term("y3_1a", P), g[3], nxt_t[1], gate2_t[1], 0, P)
+        partial = term("partial_y", U)
+        nc.vector.tensor_tensor(partial, y3_0, y3_2, ADD)
+        y3_1 = [y3_1, weighted(term("y3_1b", P), g[3], nxt_t[1], gate2_t[1], P, U)]
+        for n in range(2):
+            cols = slice(n * P, (n + 1) * P)
+            nc.vector.tensor_tensor(y[1][:, 1, cols], partial[:, cols], y3_1[n], ADD)
         nc.sync.dma_start(out_rows[:, 3, :], y[1][:, 1, :])
         for r0 in (0, P):
             round_pair(nc.vector.tensor_copy, 1, r0, r0 + P)

@@ -44,8 +44,8 @@ def tile_picked_hop2_relu_po_kernel(
         def shared(name, shape, dtype, offset):
             return reuse.tile(shape, dtype, name=name, offset=offset, align_bytes=64)
 
-        def bank(tag):
-            return psum.tile([P, BANK], F32, name=tag, tag=tag, bufs={"product": 3, "sums": 2, "back": 3}[tag])
+        def bank(n):
+            return psum.tile([P, BANK], F32, name="bank%d" % n, tag="bank%d" % n, bufs=1)
 
         def load_list(name, src):
             lst = keep.tile(list(src.shape), U16, name=name)
@@ -110,7 +110,7 @@ def tile_picked_hop2_relu_po_kernel(
         w1q = sb("w1q", [P, H], U32)
         w1s = sb("w1s", [P, H], U8)
         h = [sb("h%d" % a, [P, S], F32) for a in range(PACK)]
-        g = [sb("g%d" % a, [P, V], F32) for a in range(PACK)]
+        g = [shared("g%d" % a, [P, V], F32, (12 + 2 * a) * KB) for a in range(PACK)]
 
         def round_pairs(half, copy):
             copy(w1_pairs[half], w1_by_t[half][:, :, 0:2, :])
@@ -154,8 +154,8 @@ def tile_picked_hop2_relu_po_kernel(
         quantise_w1(0)
         gather_words(X_SPLIT, S)
         round_odd(0, nc.scalar.copy)
-        for n, tag in enumerate(("product", "product", "product", "back")):
-            first_product(0, tag, (256 * n, 256 * (n + 1)))
+        for n in range(4):
+            first_product(0, n, (256 * n, 256 * (n + 1)))
         round_pairs(1, nc.vector.tensor_copy)
         round_odd(1, nc.vector.tensor_copy)
         quantise_w1(1)
@@ -230,23 +230,23 @@ def tile_picked_hop2_relu_po_kernel(
         def second_product(t, tag, v0, v1, empty=empty_scalar):
             product(g[t], tag, w2_dealt[t][0], w2_dealt[t][1], [(v0, v1, zq[:, v0:v1])], zs, empty)
 
-        whole_product(1, ("back", "back"))
-        sums0 = bank("sums")
+        whole_product(1, (4, 5))
+        sums0 = bank(2)
         for d in range(2):
             add_turned(pieces(sums0, 4), weighted(term("z0_%d" % d, V), h[0], pos_t[d], gate_t[d], 0, V), d == 0, False)
         raw0 = fetched(term("raw0", V), h[0], pos_t[2], 0, V)
-        whole_product(2, ("product", "product"))
-        sums1 = bank("sums")
+        whole_product(2, (6, 7))
+        sums1 = bank(3)
         add_turned(pieces(sums1, 4), weighted(term("z1_0", V), h[1], pos_t[0], gate_t[0], 0, V), True, False)
         add_turned(pieces(sums0, 4), weigh(term("z0_2", V), raw0, gate_t[2][:]), False, True)
         raw1 = fetched(term("raw1", V), h[1], pos_t[2], 0, V)
-        whole_product(3, ("product", "back"))
+        whole_product(3, (0, 1))
         add_turned(pieces(sums1, 4), weighted(term("z1_1", V), h[1], pos_t[1], gate_t[1], 0, V), False, False)
         add_turned(pieces(sums1, 4), weigh(term("z1_2", V), raw1, gate_t[2][:]), False, True)
 
         raw23 = [fetched(shared("raw%d" % a, [P, V], F32, (4 + 2 * a) * KB)[:], h[a], pos_t[2], 0, V) for a in (2, 3)]
         third = sb("third", [P, 2, V], F32)
-        sums23 = bank("back")
+        sums23 = bank(4)
         by_tile = sums23[:].rearrange("v (s e p) -> v s e p", s=2, e=2)
         for e in range(2):
             places = [by_tile[:, s, e, :] for s in range(2)]
@@ -259,12 +259,12 @@ def tile_picked_hop2_relu_po_kernel(
         late_raw = sb("late_raw", [P, 2, HALF], F32)
         for e in range(2):
             fetched(late_raw[:, e, :], h[2 + e], pos_t[1], HALF, V)
-        back = bank("back")
+        back = bank(5)
         turn(back, words_of(zt01[:, 2:4]))
         for n in range(2):
             nc.scalar.copy(late[n][:, 0, :], back[:, n * P : (n + 1) * P])
         nc.scalar.copy(zt23[:], by_tile.rearrange("v s e p -> v s p e"))
-        back = bank("back")
+        back = bank(6)
         turn(back[:, 0:HALF], words_of(zt01[:, 0:2]))
         turn(back[:, HALF:V], words_of(zt23[:]))
         nc.scalar.copy(as_words(zb[0]), back[:].rearrange("p (u v) -> p v u", u=2))
@@ -284,13 +284,13 @@ def tile_picked_hop2_relu_po_kernel(
                 partial[:, :, cols].rearrange("p e v -> p v e"), late_second[:, :, cols].rearrange("p e v -> p v e"), ADD,
             )
         quantise_z(0, 0)
-        second_product(0, "product", 0, HALF)
+        second_product(0, 7, 0, HALF)
         for n in range(2):
             nc.vector.tensor_copy(as_words(zb[1 + n]), late[n][:].rearrange("p u v -> p v u"))
         for n in range(2):
             v0 = HALF + n * P
             quantise_z(1 + n, v0)
-            second_product(0, "product", v0, v0 + P)
+            second_product(0, n, v0, v0 + P)
         deal_w2(1, PACK, 5 * KB)
 
         y = [sb("y_%d" % u, [P, 2, U], F32) for u in range(2)]
@@ -303,7 +303,7 @@ def tile_picked_hop2_relu_po_kernel(
         def take_turned(t, sums):
             turned = term("turned%d" % t, U)
             nc.scalar.copy(turned, sums[:, 0:U])
-            back = bank("back")
+            back = bank(t)
             turn(back, turned)
             return back
 
@@ -313,25 +313,26 @@ def tile_picked_hop2_relu_po_kernel(
         def round_pair(copy, u, r0, r1):
             copy(yb[:, r0:r1, 2 * u : 2 * u + 2], y[u][:, :, r0:r1].rearrange("p e r -> p r e"))
 
-        second_product(1, "sums", 0, V)
-        sums0 = bank("sums")
+        second_product(1, 2, 0, V)
+        sums0 = bank(5)
         for d in range(2):
             add_turned(pieces(sums0, 2), weighted(term("y0_%d" % d, U), g[0], nxt_t[d], gate2_t[d], 0, U), d == 0, False)
         raw0 = fetched(term("root0", U), g[0], nxt_t[2], 0, U)
-        second_product(2, "back", 0, V)
-        sums1 = bank("product")
+        second_product(2, 3, 0, V)
+        sums1 = bank(6)
         add_turned(pieces(sums1, 2), weighted(term("y1_0", U), g[1], nxt_t[0], gate2_t[0], 0, U), True, False)
         add_turned(pieces(sums0, 2), weigh(term("y0_2", U), raw0, gate2_t[2]), False, True)
         raw1 = fetched(term("root1", U), g[1], nxt_t[2], 0, U)
-        second_product(3, "back", 0, V)
+        second_product(3, 4, 0, V)
         add_turned(pieces(sums1, 2), weighted(term("y1_1", U), g[1], nxt_t[1], gate2_t[1], 0, U), False, False)
         add_turned(pieces(sums1, 2), weigh(term("y1_2", U), raw1, gate2_t[2]), False, True)
-        raw2 = [fetched(term("root2_%d" % d, U), g[2], nxt_t[d], 0, U) for d in (1, 2)]
+        raw2 = fetched(term("root2", U), g[2], nxt_t[2], 0, U)
         raw3 = fetched(term("root3", U), g[3], nxt_t[2], 0, U)
-        sums2 = bank("product")
-        add_turned(pieces(sums2, 2), weighted(term("y2_0", U), g[2], nxt_t[0], gate2_t[0], 0, U), True, False)
-        for d in (1, 2):
-            add_turned(pieces(sums2, 2), weigh(term("y2_%d" % d, U), raw2[d - 1], gate2_t[d]), False, d == 2)
+        sums2 = bank(7)
+        first2 = shared("y2_0", [P, U], F32, 14 * KB)[:]
+        add_turned(pieces(sums2, 2), weighted(first2, g[2], nxt_t[0], gate2_t[0], 0, U), True, False)
+        add_turned(pieces(sums2, 2), weighted(shared("y2_1", [P, U], F32, 15 * KB)[:], g[2], nxt_t[1], gate2_t[1], 0, U), False, False)
+        add_turned(pieces(sums2, 2), weigh(term("y2_2", U), raw2, gate2_t[2]), False, True)
         back0 = take_turned(0, sums0)
         back1 = take_turned(1, sums1)
         take_back(0, back0)
@@ -342,12 +343,12 @@ def tile_picked_hop2_relu_po_kernel(
         nc.sync.dma_start(out_rows[:, 2, :], y[1][:, 0, :])
         round_pair(nc.scalar.copy, 0, 0, U)
 
-        y3_0 = weighted(term("y3_0", U), g[3], nxt_t[0], gate2_t[0], 0, U)
+        y3_0 = weighted(shared("y3_0", [P, U], F32, 16 * KB)[:], g[3], nxt_t[0], gate2_t[0], 0, U)
         y3_2 = weigh(term("y3_2", U), raw3, gate2_t[2])
-        y3_1 = weighted(term("y3_1a", P), g[3], nxt_t[1], gate2_t[1], 0, P)
+        y3_1 = weighted(shared("y3_1a", [P, P], F32, 17 * KB)[:], g[3], nxt_t[1], gate2_t[1], 0, P)
         partial = term("partial_y", U)
         nc.vector.tensor_tensor(partial, y3_0, y3_2, ADD)
-        y3_1 = [y3_1, weighted(term("y3_1b", P), g[3], nxt_t[1], gate2_t[1], P, U)]
+        y3_1 = [y3_1, weighted(shared("y3_1b", [P, P], F32, 17 * KB + KB // 2)[:], g[3], nxt_t[1], gate2_t[1], P, U)]
         for n in range(2):
             cols = slice(n * P, (n + 1) * P)
             nc.vector.tensor_tensor(y[1][:, 1, cols], partial[:, cols], y3_1[n], ADD)

@@ -244,38 +244,51 @@ def tile_picked_hop2_relu_po_kernel(
         add_turned(pieces(sums1, 4), weighted(term("z1_1", V), h[1], pos_t[1], gate_t[1], 0, V), False, False)
         add_turned(pieces(sums1, 4), weigh(term("z1_2", V), raw1, gate_t[2][:]), False, True)
 
-        raw23 = [fetched(shared("raw%d" % a, [P, V], F32, (4 + 2 * a) * KB)[:], h[a], pos_t[2], 0, V) for a in (2, 3)]
-        third = sb("third", [P, 2, V], F32)
+        raw23 = [
+            fetched(shared("raw2", [P, HALF], F32, 8 * KB)[:], h[2], pos_t[2], 0, HALF),
+            fetched(term("raw3", HALF), h[3], pos_t[2], 0, HALF),
+        ]
         sums23 = bank(4)
         by_tile = sums23[:].rearrange("v (s e p) -> v s e p", s=2, e=2)
+        places = [[by_tile[:, s, e, :] for s in range(2)] for e in range(2)]
         for e in range(2):
-            places = [by_tile[:, s, e, :] for s in range(2)]
             for d in range(2):
                 src = weighted(term("z%d_%d" % (2 + e, d), HALF), h[2 + e], pos_t[d], gate_t[d], 0, HALF)
-                add_turned(places, src, e == 0 and d == 0, False)
-            add_turned(places, weigh(third[:, e, :], raw23[e], gate_t[2][:]), False, e == 1)
-        sort_pairs(0, sums0)
-        sort_pairs(1, sums1)
-        late_raw = sb("late_raw", [P, 2, HALF], F32)
+                add_turned(places[e], src, e == 0 and d == 0, False)
         for e in range(2):
-            fetched(late_raw[:, e, :], h[2 + e], pos_t[1], HALF, V)
-        back = bank(5)
-        turn(back, words_of(zt01[:, 2:4]))
-        for n in range(2):
-            nc.scalar.copy(late[n][:, 0, :], back[:, n * P : (n + 1) * P])
+            add_turned(places[e], weigh(term("z%d_2" % (2 + e), HALF), raw23[e], gate_t[2][:, 0:HALF]), False, e == 1)
+
+        def fetch_late(d):
+            raw = sb("late_raw%d" % d, [P, 2, HALF], F32)
+            for e in range(2):
+                fetched(raw[:, e, :], h[2 + e], pos_t[d], HALF, V)
+            return raw
+
+        def weigh_late(d, raw):
+            weight = gate_t[d][:, HALF:V].unsqueeze(1).to_broadcast([P, 2, HALF])
+            return weigh(sb("late_term%d" % d, [P, 2, HALF], F32)[:], raw[:], weight)
+
+        sort_pairs(0, sums0)
+        late_raw2 = fetch_late(2)
+        sort_pairs(1, sums1)
         nc.scalar.copy(zt23[:], by_tile.rearrange("v s e p -> v s p e"))
+        late_raw1 = fetch_late(1)
         back = bank(6)
         turn(back[:, 0:HALF], words_of(zt01[:, 0:2]))
         turn(back[:, HALF:V], words_of(zt23[:]))
         nc.scalar.copy(as_words(zb[0]), back[:].rearrange("p (u v) -> p v u", u=2))
+        back = bank(5)
+        turn(back, words_of(zt01[:, 2:4]))
+        for n in range(2):
+            nc.scalar.copy(late[n][:, 0, :], back[:, n * P : (n + 1) * P])
 
-        late_first = shared("late_first", [P, 2, HALF], F32, 10 * KB)
+        late_first = shared("late_first", [P, 2, HALF], F32, 8 * KB)
         for e in range(2):
             weighted(late_first[:, e, :], h[2 + e], pos_t[0], gate_t[0], HALF, V)
-        late_second = sb("late_second", [P, 2, HALF], F32)
-        weigh(late_second[:], late_raw[:], gate_t[1][:, HALF:V].unsqueeze(1).to_broadcast([P, 2, HALF]))
+        late_third = weigh_late(2, late_raw2)
+        late_second = weigh_late(1, late_raw1)
         partial = sb("partial_z", [P, 2, HALF], F32)
-        nc.vector.tensor_tensor(partial[:], late_first[:], third[:, :, HALF:V], ADD)
+        nc.vector.tensor_tensor(partial[:], late_first[:], late_third, ADD)
         deal_w2(0, 1, 0)
         for n in range(2):
             cols = slice(n * P, (n + 1) * P)
@@ -323,16 +336,15 @@ def tile_picked_hop2_relu_po_kernel(
         add_turned(pieces(sums1, 2), weighted(term("y1_0", U), g[1], nxt_t[0], gate2_t[0], 0, U), True, False)
         add_turned(pieces(sums0, 2), weigh(term("y0_2", U), raw0, gate2_t[2]), False, True)
         raw1 = fetched(term("root1", U), g[1], nxt_t[2], 0, U)
+        raw2 = [fetched(term("root2_%d" % d, U), g[2], nxt_t[d], 0, U) for d in (2, 1)]
         second_product(3, 4, 0, V)
         add_turned(pieces(sums1, 2), weighted(term("y1_1", U), g[1], nxt_t[1], gate2_t[1], 0, U), False, False)
         add_turned(pieces(sums1, 2), weigh(term("y1_2", U), raw1, gate2_t[2]), False, True)
-        raw2 = fetched(term("root2", U), g[2], nxt_t[2], 0, U)
-        raw3 = fetched(term("root3", U), g[3], nxt_t[2], 0, U)
         sums2 = bank(7)
         first2 = shared("y2_0", [P, U], F32, 14 * KB)[:]
         add_turned(pieces(sums2, 2), weighted(first2, g[2], nxt_t[0], gate2_t[0], 0, U), True, False)
-        add_turned(pieces(sums2, 2), weighted(shared("y2_1", [P, U], F32, 15 * KB)[:], g[2], nxt_t[1], gate2_t[1], 0, U), False, False)
-        add_turned(pieces(sums2, 2), weigh(term("y2_2", U), raw2, gate2_t[2]), False, True)
+        for n, d in enumerate((2, 1)):
+            add_turned(pieces(sums2, 2), weigh(term("y2_%d" % d, U), raw2[n], gate2_t[d]), False, d == 1)
         back0 = take_turned(0, sums0)
         back1 = take_turned(1, sums1)
         take_back(0, back0)
@@ -344,7 +356,7 @@ def tile_picked_hop2_relu_po_kernel(
         round_pair(nc.scalar.copy, 0, 0, U)
 
         y3_0 = weighted(shared("y3_0", [P, U], F32, 16 * KB)[:], g[3], nxt_t[0], gate2_t[0], 0, U)
-        y3_2 = weigh(term("y3_2", U), raw3, gate2_t[2])
+        y3_2 = weighted(shared("y3_2", [P, U], F32, 15 * KB)[:], g[3], nxt_t[2], gate2_t[2], 0, U)
         y3_1 = weighted(shared("y3_1a", [P, P], F32, 17 * KB)[:], g[3], nxt_t[1], gate2_t[1], 0, P)
         partial = term("partial_y", U)
         nc.vector.tensor_tensor(partial, y3_0, y3_2, ADD)

@@ -282,6 +282,11 @@ def tile_picked_hop2_relu_po_kernel(
         for n in range(2):
             nc.scalar.copy(late[n][:, 0, :], back[:, n * P : (n + 1) * P])
 
+        weights = bank(3)
+        turn(weights, gate2_all[:, 1:3, :].rearrange("p d r -> p (d r)"))
+        root_weight = sb("root_weight", [P, 4], F32)
+        nc.scalar.copy(root_weight[:], weights[:, 0:BANK:P])
+
         late_first = shared("late_first", [P, 2, HALF], F32, 8 * KB)
         for e in range(2):
             weighted(late_first[:, e, :], h[2 + e], pos_t[0], gate_t[0], HALF, V)
@@ -336,26 +341,32 @@ def tile_picked_hop2_relu_po_kernel(
         add_turned(pieces(sums1, 2), weighted(term("y1_0", U), g[1], nxt_t[0], gate2_t[0], 0, U), True, False)
         add_turned(pieces(sums0, 2), weigh(term("y0_2", U), raw0, gate2_t[2]), False, True)
         raw1 = fetched(term("root1", U), g[1], nxt_t[2], 0, U)
-        raw2 = [fetched(term("root2_%d" % d, U), g[2], nxt_t[d], 0, U) for d in (2, 1)]
+        turned2 = [bank(7), bank(3)]
+        turn(turned2[0], fetched(term("root2_1", U), g[2], nxt_t[1], 0, U))
         second_product(3, 4, 0, V)
+        turn(turned2[1], fetched(term("root2_2", U), g[2], nxt_t[2], 0, U))
         add_turned(pieces(sums1, 2), weighted(term("y1_1", U), g[1], nxt_t[1], gate2_t[1], 0, U), False, False)
         add_turned(pieces(sums1, 2), weigh(term("y1_2", U), raw1, gate2_t[2]), False, True)
-        sums2 = bank(7)
-        first2 = shared("y2_0", [P, U], F32, 14 * KB)[:]
-        add_turned(pieces(sums2, 2), weighted(first2, g[2], nxt_t[0], gate2_t[0], 0, U), True, False)
-        for n, d in enumerate((2, 1)):
-            add_turned(pieces(sums2, 2), weigh(term("y2_%d" % d, U), raw2[n], gate2_t[d]), False, d == 1)
+        first2 = weighted(shared("y2_0", [P, U], F32, 14 * KB)[:], g[2], nxt_t[0], gate2_t[0], 0, U)
+        sums2 = bank(2)
+
+        def weigh_turned(d):
+            for s in range(2):
+                scaled = term("root2_scaled%d%d" % (d, s), P)
+                weight = root_weight[:, 2 * d + s : 2 * d + s + 1]
+                nc.scalar.activation(scaled, turned2[d][:, s * P : (s + 1) * P], COPY, scale=weight)
+                add_turned([sums2[:, s * P : (s + 1) * P]], scaled, d + s == 0, d + s == 2)
+
+        weigh_turned(0)
         back0 = take_turned(0, sums0)
         back1 = take_turned(1, sums1)
+        weigh_turned(1)
         take_back(0, back0)
-        back2 = take_turned(2, sums2)
         take_back(1, back1)
         nc.sync.dma_start(out_rows[:, 0:2, :], y[0][:])
-        take_back(2, back2)
-        nc.sync.dma_start(out_rows[:, 2, :], y[1][:, 0, :])
         round_pair(nc.scalar.copy, 0, 0, U)
 
-        y3_0 = weighted(shared("y3_0", [P, U], F32, 16 * KB)[:], g[3], nxt_t[0], gate2_t[0], 0, U)
+        y3_0 = weighted(term("y3_0", U), g[3], nxt_t[0], gate2_t[0], 0, U)
         y3_2 = weighted(shared("y3_2", [P, U], F32, 15 * KB)[:], g[3], nxt_t[2], gate2_t[2], 0, U)
         y3_1 = weighted(shared("y3_1a", [P, P], F32, 17 * KB)[:], g[3], nxt_t[1], gate2_t[1], 0, P)
         partial = term("partial_y", U)
@@ -365,6 +376,8 @@ def tile_picked_hop2_relu_po_kernel(
             cols = slice(n * P, (n + 1) * P)
             nc.vector.tensor_tensor(y[1][:, 1, cols], partial[:, cols], y3_1[n], ADD)
         nc.sync.dma_start(out_rows[:, 3, :], y[1][:, 1, :])
+        nc.vector.tensor_tensor(y[1][:, 0, :], sums2[:, 0:U], first2, ADD)
+        nc.sync.dma_start(out_rows[:, 2, :], y[1][:, 0, :])
         for r0 in (0, P):
             round_pair(nc.vector.tensor_copy, 1, r0, r0 + P)
         for r0 in (0, P):

@@ -209,7 +209,7 @@ def tile_picked_hop2_relu_po_kernel(
 
         zt01 = sb("zt01", [P, V // P, P, 2], BF16)
         zt23 = sb("zt23", [P, HALF // P, P, 2], BF16)
-        zb = [sb("zb0", [P, HALF, PACK], BF16), sb("zb1", [P, P, PACK], BF16), shared("zb2", [P, P, PACK], BF16, 5 * KB)]
+        zb = [sb("zb0", [P, HALF, PACK], BF16), shared("zb1", [P, P, PACK], BF16, 5 * KB), sb("zb2", [P, P, PACK], BF16)]
         late = [sb("late%d" % n, [P, 2, P], F32) for n in range(2)]
         zq = sb("zq", [P, V], U32)
         zs = sb("zs", [P, V], U8)
@@ -372,12 +372,11 @@ def tile_picked_hop2_relu_po_kernel(
         partial = term("partial_y", U)
         nc.vector.tensor_tensor(partial, y3_0, y3_2, ADD)
         y3_1 = [y3_1, weighted(shared("y3_1b", [P, P], F32, 17 * KB + KB // 2)[:], g[3], nxt_t[1], gate2_t[1], P, U)]
-        for n in range(2):
-            cols = slice(n * P, (n + 1) * P)
-            nc.vector.tensor_tensor(y[1][:, 1, cols], partial[:, cols], y3_1[n], ADD)
-        nc.sync.dma_start(out_rows[:, 3, :], y[1][:, 1, :])
+        nc.vector.tensor_tensor(y[1][:, 1, 0:P], partial[:, 0:P], y3_1[0], ADD)
         nc.vector.tensor_tensor(y[1][:, 0, :], sums2[:, 0:U], first2, ADD)
         nc.sync.dma_start(out_rows[:, 2, :], y[1][:, 0, :])
+        nc.vector.tensor_tensor(y[1][:, 1, P:U], partial[:, P:U], y3_1[1], ADD)
+        nc.sync.dma_start(out_rows[:, 3, :], y[1][:, 1, :])
         for r0 in (0, P):
             round_pair(nc.vector.tensor_copy, 1, r0, r0 + P)
         for r0 in (0, P):

@@ -209,7 +209,7 @@ def tile_picked_hop2_relu_po_kernel(
 
         zt01 = sb("zt01", [P, V // P, P, 2], BF16)
         zt23 = sb("zt23", [P, HALF // P, P, 2], BF16)
-        zb = [sb("zb0", [P, HALF, PACK], BF16), shared("zb1", [P, P, PACK], BF16, 5 * KB), sb("zb2", [P, P, PACK], BF16)]
+        zb = [sb("zb0", [P, HALF, PACK], BF16), sb("zb1", [P, P, PACK], BF16), shared("zb2", [P, P, PACK], BF16, 5 * KB)]
         late = [sb("late%d" % n, [P, 2, P], F32) for n in range(2)]
         zq = sb("zq", [P, V], U32)
         zs = sb("zs", [P, V], U8)
@@ -258,28 +258,35 @@ def tile_picked_hop2_relu_po_kernel(
         for e in range(2):
             add_turned(places[e], weigh(term("z%d_2" % (2 + e), HALF), raw23[e], gate_t[2][:, 0:HALF]), False, e == 1)
 
-        def fetch_late(d):
-            raw = sb("late_raw%d" % d, [P, 2, HALF], F32)
+        mid, end = slice(HALF, HALF + P), slice(HALF + P, V)
+        weights = bank(5)
+        for d in (1, 2):
+            turn(weights[:, (d - 1) * P : d * P], gate_t[d][:, mid])
+        mid_weight = sb("mid_weight", [P, 2], F32)
+        nc.scalar.copy(mid_weight[:], weights[:, 0:HALF:P])
+        mid_turned = [bank(6), bank(7)]
+        for d in (1, 2):
             for e in range(2):
-                fetched(raw[:, e, :], h[2 + e], pos_t[d], HALF, V)
-            return raw
-
-        def weigh_late(d, raw):
-            weight = gate_t[d][:, HALF:V].unsqueeze(1).to_broadcast([P, 2, HALF])
-            return weigh(sb("late_term%d" % d, [P, 2, HALF], F32)[:], raw[:], weight)
-
+                raw = fetched(term("mid_raw%d%d" % (d, e), P), h[2 + e], pos_t[d], mid.start, mid.stop)
+                turn(mid_turned[d - 1][:, e * P : (e + 1) * P], raw)
+        end_raw = sb("end_raw", [P, 2, P], F32)
+        for e in range(2):
+            fetched(end_raw[:, e, :], h[2 + e], pos_t[2], end.start, end.stop)
         sort_pairs(0, sums0)
-        late_raw2 = fetch_late(2)
         sort_pairs(1, sums1)
         nc.scalar.copy(zt23[:], by_tile.rearrange("v s e p -> v s p e"))
-        late_raw1 = fetch_late(1)
-        back = bank(6)
+        mid_sums = bank(0)
+        for d in range(2):
+            scaled = term("mid_scaled%d" % d, HALF)
+            nc.scalar.activation(scaled, mid_turned[d][:, 0:HALF], COPY, scale=mid_weight[:, d : d + 1])
+            add_turned(pieces(mid_sums, 2), scaled, d == 0, d == 1)
+        back = bank(1)
         turn(back[:, 0:HALF], words_of(zt01[:, 0:2]))
         turn(back[:, HALF:V], words_of(zt23[:]))
         nc.scalar.copy(as_words(zb[0]), back[:].rearrange("p (u v) -> p v u", u=2))
         back = bank(5)
         turn(back, words_of(zt01[:, 2:4]))
-        for n in range(2):
+        for n in (1, 0):
             nc.scalar.copy(late[n][:, 0, :], back[:, n * P : (n + 1) * P])
 
         weights = bank(3)
@@ -287,28 +294,33 @@ def tile_picked_hop2_relu_po_kernel(
         root_weight = sb("root_weight", [P, 4], F32)
         nc.scalar.copy(root_weight[:], weights[:, 0:BANK:P])
 
-        late_first = shared("late_first", [P, 2, HALF], F32, 8 * KB)
+        late_first = shared("late_first", [P, 2, HALF], F32, 8 * KB + KB // 2)
         for e in range(2):
             weighted(late_first[:, e, :], h[2 + e], pos_t[0], gate_t[0], HALF, V)
-        late_third = weigh_late(2, late_raw2)
-        late_second = weigh_late(1, late_raw1)
-        partial = sb("partial_z", [P, 2, HALF], F32)
-        nc.vector.tensor_tensor(partial[:], late_first[:], late_third, ADD)
+        end_second = shared("end_second", [P, 2, P], F32, 8 * KB - KB // 2)
+        for e in range(2):
+            weighted(end_second[:, e, :], h[2 + e], pos_t[1], gate_t[1], end.start, end.stop)
+        end_third = weigh(sb("end_third", [P, 2, P], F32)[:], end_raw[:], gate_t[2][:, end].unsqueeze(1).to_broadcast([P, 2, P]))
+        partial = sb("partial_z", [P, 2, P], F32)
+        nc.vector.tensor_tensor(partial[:], late_first[:, :, P:HALF], end_second[:], ADD)
         deal_w2(0, 1, 0)
-        for n in range(2):
-            cols = slice(n * P, (n + 1) * P)
+
+        def add_pairs(n, left, right):
             nc.vector.tensor_tensor(
                 late[n][:, 1, :].bitcast(BF16).rearrange("p (v e) -> p v e", e=2),
-                partial[:, :, cols].rearrange("p e v -> p v e"), late_second[:, :, cols].rearrange("p e v -> p v e"), ADD,
+                left.rearrange("p e v -> p v e"), right.rearrange("p e v -> p v e"), ADD,
             )
+
+        add_pairs(1, partial[:], end_third)
         quantise_z(0, 0)
         second_product(0, 7, 0, HALF)
-        for n in range(2):
+        add_pairs(0, mid_sums[:, 0:HALF].rearrange("p (e v) -> p e v", e=2), late_first[:, :, 0:P])
+        for n in (1, 0):
             nc.vector.tensor_copy(as_words(zb[1 + n]), late[n][:].rearrange("p u v -> p v u"))
-        for n in range(2):
+        for n in (1, 0):
             v0 = HALF + n * P
             quantise_z(1 + n, v0)
-            second_product(0, n, v0, v0 + P)
+            second_product(0, 6 * n, v0, v0 + P)
         deal_w2(1, PACK, 5 * KB)
 
         y = [sb("y_%d" % u, [P, 2, U], F32) for u in range(2)]

@@ -265,13 +265,13 @@ def tile_picked_hop2_relu_po_kernel(
         mid_weight = sb("mid_weight", [P, 2], F32)
         nc.scalar.copy(mid_weight[:], weights[:, 0:HALF:P])
         mid_turned = [bank(6), bank(7)]
-        for d in (1, 2):
-            for e in range(2):
-                raw = fetched(term("mid_raw%d%d" % (d, e), P), h[2 + e], pos_t[d], mid.start, mid.stop)
-                turn(mid_turned[d - 1][:, e * P : (e + 1) * P], raw)
-        end_raw = sb("end_raw", [P, 2, P], F32)
+        late_raw = sb("late_raw", [P, 2, HALF], F32)
         for e in range(2):
-            fetched(end_raw[:, e, :], h[2 + e], pos_t[2], end.start, end.stop)
+            raw = fetched(term("mid_raw%d" % e, P), h[2 + e], pos_t[1], mid.start, mid.stop)
+            turn(mid_turned[0][:, e * P : (e + 1) * P], raw)
+        for e in range(2):
+            raw = fetched(late_raw[:, e, :], h[2 + e], pos_t[2], HALF, V)
+            turn(mid_turned[1][:, e * P : (e + 1) * P], raw[:, 0:P])
         sort_pairs(0, sums0)
         sort_pairs(1, sums1)
         nc.scalar.copy(zt23[:], by_tile.rearrange("v s e p -> v s p e"))
@@ -300,7 +300,7 @@ def tile_picked_hop2_relu_po_kernel(
         end_second = shared("end_second", [P, 2, P], F32, 8 * KB - KB // 2)
         for e in range(2):
             weighted(end_second[:, e, :], h[2 + e], pos_t[1], gate_t[1], end.start, end.stop)
-        end_third = weigh(sb("end_third", [P, 2, P], F32)[:], end_raw[:], gate_t[2][:, end].unsqueeze(1).to_broadcast([P, 2, P]))
+        end_third = weigh(sb("end_third", [P, 2, P], F32)[:], late_raw[:, :, P:HALF], gate_t[2][:, end].unsqueeze(1).to_broadcast([P, 2, P]))
         partial = sb("partial_z", [P, 2, P], F32)
         nc.vector.tensor_tensor(partial[:], late_first[:, :, P:HALF], end_second[:], ADD)
         deal_w2(0, 1, 0)
@@ -376,18 +376,18 @@ def tile_picked_hop2_relu_po_kernel(
         take_back(0, back0)
         take_back(1, back1)
         nc.sync.dma_start(out_rows[:, 0:2, :], y[0][:])
-        round_pair(nc.scalar.copy, 0, 0, U)
+        for r0 in (0, P):
+            round_pair(nc.scalar.copy, 0, r0, r0 + P)
 
         y3_0 = weighted(term("y3_0", U), g[3], nxt_t[0], gate2_t[0], 0, U)
         y3_2 = weighted(shared("y3_2", [P, U], F32, 15 * KB)[:], g[3], nxt_t[2], gate2_t[2], 0, U)
-        y3_1 = weighted(shared("y3_1a", [P, P], F32, 17 * KB)[:], g[3], nxt_t[1], gate2_t[1], 0, P)
+        y3_1 = weighted(shared("y3_1", [P, U], F32, 17 * KB)[:], g[3], nxt_t[1], gate2_t[1], 0, U)
         partial = term("partial_y", U)
         nc.vector.tensor_tensor(partial, y3_0, y3_2, ADD)
-        y3_1 = [y3_1, weighted(shared("y3_1b", [P, P], F32, 17 * KB + KB // 2)[:], g[3], nxt_t[1], gate2_t[1], P, U)]
-        nc.vector.tensor_tensor(y[1][:, 1, 0:P], partial[:, 0:P], y3_1[0], ADD)
         nc.vector.tensor_tensor(y[1][:, 0, :], sums2[:, 0:U], first2, ADD)
         nc.sync.dma_start(out_rows[:, 2, :], y[1][:, 0, :])
-        nc.vector.tensor_tensor(y[1][:, 1, P:U], partial[:, P:U], y3_1[1], ADD)
+        for r0 in (0, P):
+            nc.vector.tensor_tensor(y[1][:, 1, r0 : r0 + P], partial[:, r0 : r0 + P], y3_1[:, r0 : r0 + P], ADD)
         nc.sync.dma_start(out_rows[:, 3, :], y[1][:, 1, :])
         for r0 in (0, P):
             round_pair(nc.vector.tensor_copy, 1, r0, r0 + P)

@@ -99,9 +99,8 @@ def tile_picked_hop2_relu_po_kernel(
         xq_last = shared("xq_last", [P, S - X_SPLIT], U32, KB // 2)
         xqs = sb("xqs", [P, S], U8)
         w1_by_t = [half[:].rearrange("k j (p t) -> k p t j", t=PACK) for half in (w1_low, w1_high)]
-        w1_rest = shared("w1_rest", [P, 3, P, PACK], BF16, 3 * KB // 2)
-        w1_pairs = [shared("w1_first", [P, 64, 2, PACK], BF16, KB)[:], w1_rest[:, 0].rearrange("k (p t) j -> k p t j", t=2)]
-        w1_odd = w1_rest[:, 1:3]
+        w1_pairs = [shared("w1_first", [P, 64, 2, PACK], BF16, KB)[:], shared("w1_second", [P, 64, 2, PACK], BF16, 3 * KB // 2)[:]]
+        w1_odd = shared("w1_odd", [P, 2, P, PACK], BF16, 7 * KB // 2)[:]
         w1_bf = [
             w1_pairs[0].rearrange("k p t j -> k (p t j)"),
             w1_pairs[1].rearrange("k p t j -> k (p t j)"),
@@ -150,10 +149,10 @@ def tile_picked_hop2_relu_po_kernel(
 
         nc.vector.tensor_copy(xqs[:], xs[:].indirect(offs_t[:]))
         round_pairs(0, nc.scalar.copy)
+        round_odd(0, nc.scalar.copy)
         gather_words(0, X_SPLIT)
         quantise_w1(0)
         gather_words(X_SPLIT, S)
-        round_odd(0, nc.scalar.copy)
         for n in range(4):
             first_product(0, n, (256 * n, 256 * (n + 1)))
         round_pairs(1, nc.vector.tensor_copy)

@@ -82,12 +82,13 @@ def tile_picked_hop2_relu_po_kernel(
         w1_low = load("w1_low", w1_rows[:, :, 0 : H // 2])
         w1_high = load("w1_high", w1_rows[:, :, H // 2 : H])
         third_list = load_list("pos2_t", pos3)
-        pos_t, gate_t = [], []
-        for d, src in enumerate((pos1, pos2)):
-            pos_t.append(load_list("pos%d_t" % d, src))
-            gate_t.append(load("gate_%d" % d, gate[d]))
+        pos_t = [load_list("pos0_t", pos1)]
+        gate_t = [load("gate_0", gate[0])]
+        pos_t.append(load_list("pos1_t", pos2))
         pos_t.append(third_list)
-        gate_t.append(load("gate_2", gate[2]))
+        other_gates = load("other_gates", gate[1:D].rearrange("d p v -> p d v"))
+        gate_t.extend(other_gates[:, d, :] for d in range(D - 1))
+        root_runs = load("root_runs", gate2.rearrange("d p (c k) -> (d p c) k", k=P)[0 : (P - 1) * 5 + 1 : 5, :])
         w2w = sb("w2w", [P, 2 * H], U8)
         nc.sync.dma_start(w2w[:].bitcast(I32), w2_words[0].bitcast(I32))
         load_scale_rows((nc.sync,), w2s, w2_scales[0])
@@ -237,11 +238,11 @@ def tile_picked_hop2_relu_po_kernel(
         whole_product(2, (6, 7))
         sums1 = bank(3)
         add_turned(pieces(sums1, 4), weighted(term("z1_0", V), h[1], pos_t[0], gate_t[0], 0, V), True, False)
-        add_turned(pieces(sums0, 4), weigh(term("z0_2", V), raw0, gate_t[2][:]), False, True)
+        add_turned(pieces(sums0, 4), weigh(term("z0_2", V), raw0, gate_t[2]), False, True)
         raw1 = fetched(term("raw1", V), h[1], pos_t[2], 0, V)
         whole_product(3, (0, 1))
         add_turned(pieces(sums1, 4), weighted(term("z1_1", V), h[1], pos_t[1], gate_t[1], 0, V), False, False)
-        add_turned(pieces(sums1, 4), weigh(term("z1_2", V), raw1, gate_t[2][:]), False, True)
+        add_turned(pieces(sums1, 4), weigh(term("z1_2", V), raw1, gate_t[2]), False, True)
 
         raw23 = [
             fetched(shared("raw2", [P, HALF], F32, 8 * KB)[:], h[2], pos_t[2], 0, HALF),
@@ -289,9 +290,9 @@ def tile_picked_hop2_relu_po_kernel(
             nc.scalar.copy(late[n][:, 0, :], back[:, n * P : (n + 1) * P])
 
         weights = bank(3)
-        turn(weights, gate2_all[:, 1:3, :].rearrange("p d r -> p (d r)"))
-        root_weight = sb("root_weight", [P, 4], F32)
-        nc.scalar.copy(root_weight[:], weights[:, 0:BANK:P])
+        turn(weights, root_runs[:])
+        root_weight = sb("root_weight", [P, 2, 2], F32)
+        nc.scalar.copy(root_weight[:], weights[:, 52:156].rearrange("p (d x) -> p d x", d=2)[:, :, 0:2])
 
         late_first = shared("late_first", [P, 2, HALF], F32, 8 * KB + KB // 2)
         for e in range(2):
@@ -364,8 +365,7 @@ def tile_picked_hop2_relu_po_kernel(
         def weigh_turned(d):
             for s in range(2):
                 scaled = term("root2_scaled%d%d" % (d, s), P)
-                weight = root_weight[:, 2 * d + s : 2 * d + s + 1]
-                nc.scalar.activation(scaled, turned2[d][:, s * P : (s + 1) * P], COPY, scale=weight)
+                nc.scalar.activation(scaled, turned2[d][:, s * P : (s + 1) * P], COPY, scale=root_weight[:, d, s : s + 1])
                 add_turned([sums2[:, s * P : (s + 1) * P]], scaled, d + s == 0, d + s == 2)
 
         weigh_turned(0)

@@ -15,6 +15,8 @@ FP8X4 = mybir.dt.float8_e4m3fn_x4
 FP4X4 = mybir.dt.float4_e2m1fn_x4
 ABS = mybir.ActivationFunctionType.Abs
 COPY = mybir.ActivationFunctionType.Copy
+IDENTITY = mybir.ActivationFunctionType.Identity
+SIGN = mybir.ActivationFunctionType.Sign
 RELU = mybir.ActivationFunctionType.Relu
 MULT = mybir.AluOpType.mult
 ADD = mybir.AluOpType.add
@@ -26,6 +28,10 @@ HALF = V // 2
 KB = 1024
 EARLY = 512
 X_SPLIT = 768
+CHUNKS = V // P
+TURNED = 3 * P
+NUDGE = 2.0 ** -60
+TINY = 2.0 ** -120
 
 
 def tile_picked_hop2_relu_po_kernel(
@@ -74,6 +80,11 @@ def tile_picked_hop2_relu_po_kernel(
 
         w1_rows = w1.rearrange("(p j) c -> p j c", j=PACK)
         word_rows = x_words[0].rearrange("p n t -> p (n t)").bitcast(I32)
+        def load_runs(name, src, step):
+            runs = src.rearrange("d p (c k) -> (d p c) k", k=P)
+            return load(name, runs[0 : (P - 1) * step + 1 : step, :])
+
+        gate_runs = load_runs("gate_runs", gate, 9)
         offs_t = load_list("offs_t", offs)
         xw = sb("xw", [P, T], U32)
         nc.sync.dma_start(xw[:, 0:EARLY].bitcast(I32), word_rows[:, 0:EARLY])
@@ -82,13 +93,9 @@ def tile_picked_hop2_relu_po_kernel(
         w1_low = load("w1_low", w1_rows[:, :, 0 : H // 2])
         w1_high = load("w1_high", w1_rows[:, :, H // 2 : H])
         third_list = load_list("pos2_t", pos3)
-        pos_t = [load_list("pos0_t", pos1)]
-        gate_t = [load("gate_0", gate[0])]
-        pos_t.append(load_list("pos1_t", pos2))
-        pos_t.append(third_list)
-        other_gates = load("other_gates", gate[1:D].rearrange("d p v -> p d v"))
-        gate_t.extend(other_gates[:, d, :] for d in range(D - 1))
-        root_runs = load("root_runs", gate2.rearrange("d p (c k) -> (d p c) k", k=P)[0 : (P - 1) * 5 + 1 : 5, :])
+        pos_t = [load_list("pos%d_t" % d, src) for d, src in enumerate((pos1, pos2))] + [third_list]
+        late_gate = load("late_gate", gate[:, :, TURNED:V].rearrange("d p v -> p d v"))
+        root_runs = load_runs("root_runs", gate2, 5)
         w2w = sb("w2w", [P, 2 * H], U8)
         nc.sync.dma_start(w2w[:].bitcast(I32), w2_words[0].bitcast(I32))
         load_scale_rows((nc.sync,), w2s, w2_scales[0])
@@ -96,9 +103,44 @@ def tile_picked_hop2_relu_po_kernel(
         gate2_all = load("gate2_all", gate2.rearrange("d p r -> p d r"))
         gate2_t = [gate2_all[:, d, :] for d in range(D)]
 
-        xq = sb("xq", [P, X_SPLIT], U32)
+        def turn(dst, src):
+            for s in range(src.shape[1] // P):
+                nc.tensor.transpose(dst[:, s * P : (s + 1) * P], src[:, s * P : (s + 1) * P], ident[:])
+
+        turned_runs = bank(0)
+        turn(turned_runs, gate_runs[:])
+        by_gate = turned_runs[:, 4 : 4 + D * 56].rearrange("p (d x) -> p d x", d=D)[:, :, 0:CHUNKS]
+        sign = sb("sign", [P, CHUNKS], F32)
+        nc.scalar.activation(sign[:], by_gate[:, 2], SIGN)
+        small = sb("small", [P, 2, CHUNKS], F32)
+        small_sum = sb("small_sum", [P, 1], F32)
+        nc.scalar.activation(small[:], by_gate[:, 0:2], ABS, scale=NUDGE, accum_out=small_sum[:])
+        side = sb("side", [P, CHUNKS], F32)
+        nc.scalar.activation(side[:], sign[:], SIGN, bias=0.5)
+        least = sb("least", [P, 1], F32)
+        nc.scalar.activation(least[:], small_sum[:], IDENTITY, bias=TINY)
+        third_weight = sb("third_weight", [P, CHUNKS], F32)
+        nc.scalar.copy(third_weight[:], by_gate[:, 2])
+        divisor = shared("divisor", [P, 32], F32, 20 * KB - 64)[:, 0:CHUNKS]
+        for c in range(CHUNKS):
+            nc.scalar.activation(divisor[:, c : c + 1], side[:, c : c + 1], IDENTITY, scale=least[:], bias=third_weight[:, c : c + 1])
+        factor = sb("factor", [P, CHUNKS], F32)
+        nc.scalar.copy(factor[:], divisor)
+        xqs = [shared("xqs_low", [P, BANK], U8, 20 * KB - BANK), sb("xqs_high", [P, BANK], U8)]
+        nc.vector.tensor_copy(xqs[1][:], xs[:].indirect(offs_t[:, BANK // 16 : S // 16]))
+        inverse = sb("inverse", [P, CHUNKS], F32)
+        nc.vector.reciprocal(inverse[:], divisor)
+        nc.vector.tensor_copy(xqs[0][:], xs[:].indirect(offs_t[:, 0 : BANK // 16]))
+        ratio = [shared("ratio%d" % n, [P, 2, 2], F32, place) for n, place in enumerate((KB, 7 * KB // 2))]
+        for c in range(CHUNKS):
+            nc.scalar.activation(ratio[c // 2][:, :, c % 2], by_gate[:, 0:2, c], COPY, scale=inverse[:, c : c + 1])
+        spread_banks = [bank(1), bank(2)]
+        for d in range(2):
+            for c in range(CHUNKS):
+                nc.tensor.transpose(spread_banks[d][:, c * P : (c + 1) * P], ratio[c // 2][:, d, c % 2 : c % 2 + 1].to_broadcast([P, P]), ident[:])
+
+        xq = shared("xq", [P, X_SPLIT], U32, 20 * KB)
         xq_last = shared("xq_last", [P, S - X_SPLIT], U32, KB // 2)
-        xqs = sb("xqs", [P, S], U8)
         w1_by_t = [half[:].rearrange("k j (p t) -> k p t j", t=PACK) for half in (w1_low, w1_high)]
         w1_pairs = [shared("w1_first", [P, 64, 2, PACK], BF16, KB)[:], shared("w1_second", [P, 64, 2, PACK], BF16, 3 * KB // 2)[:]]
         w1_odd = shared("w1_odd", [P, 2, P, PACK], BF16, 7 * KB // 2)[:]
@@ -133,29 +175,34 @@ def tile_picked_hop2_relu_po_kernel(
             for j0, j1, words in parts:
                 nc.tensor.matmul_mx(
                     acc[:, j0 - c0 : j1 - c0], lhsT=lhsT, lhsT_scale=lhsT_scale,
-                    rhs=words.bitcast(FP8X4), rhs_scale=rhs_scale[:, j0:j1], start=True, stop=True,
+                    rhs=words.bitcast(FP8X4), rhs_scale=rhs_scale(j0, j1), start=True, stop=True,
                 )
             empty(dst[:, c0:c1], acc[:, 0 : c1 - c0])
 
         def picked(j0, j1):
             return xq[:, j0:j1] if j1 <= X_SPLIT else xq_last[:]
 
+        def picked_scales(j0, j1):
+            return xqs[j0 // BANK][:, j0 % BANK : j0 % BANK + j1 - j0]
+
         def first_product(a, tag, cuts):
             cols = slice(a * P, (a + 1) * P)
             parts = [(j0, j1, picked(j0, j1)) for j0, j1 in zip(cuts, cuts[1:])]
-            product(h[a], tag, w1q[:, cols].bitcast(FP8X4), w1s[:, cols], parts, xqs, empty_scalar)
+            product(h[a], tag, w1q[:, cols].bitcast(FP8X4), w1s[:, cols], parts, picked_scales, empty_scalar)
 
         def gather_words(j0, j1):
             nc.vector.tensor_copy(picked(j0, j1), xw[:].indirect(offs_t[:, j0 // 16 : j1 // 16]))
 
-        nc.vector.tensor_copy(xqs[:], xs[:].indirect(offs_t[:]))
+        ratio_t = [sb("ratio_rows%d" % d, [P, V], F32) for d in range(2)]
+        nc.scalar.copy(ratio_t[0][:], spread_banks[0][:])
         round_pairs(0, nc.scalar.copy)
+        nc.scalar.copy(ratio_t[1][:], spread_banks[1][:])
         round_odd(0, nc.scalar.copy)
         gather_words(0, X_SPLIT)
         quantise_w1(0)
         gather_words(X_SPLIT, S)
         for n in range(4):
-            first_product(0, n, (256 * n, 256 * (n + 1)))
+            first_product(0, (0, 1, 4, 5)[n], (256 * n, 256 * (n + 1)))
         round_pairs(1, nc.vector.tensor_copy)
         round_odd(1, nc.vector.tensor_copy)
         quantise_w1(1)
@@ -203,125 +250,96 @@ def tile_picked_hop2_relu_po_kernel(
         def pieces(acc, n):
             return [acc[:, s * P : (s + 1) * P] for s in range(n)]
 
-        def turn(dst, src):
-            for s in range(src.shape[1] // P):
-                nc.tensor.transpose(dst[:, s * P : (s + 1) * P], src[:, s * P : (s + 1) * P], ident[:])
+        def add_marked(sums, src, first, last):
+            for s in range(len(sums)):
+                nc.tensor.matmul(
+                    sums[s], lhsT=src[:, s * P : (s + 1) * P], rhs=ident[:],
+                    start=s in first, stop=s in last, is_transpose=True,
+                )
 
-        zt01 = sb("zt01", [P, V // P, P, 2], BF16)
-        zt23 = sb("zt23", [P, HALF // P, P, 2], BF16)
-        zb = [sb("zb0", [P, HALF, PACK], BF16), sb("zb1", [P, P, PACK], BF16), shared("zb2", [P, P, PACK], BF16, 5 * KB)]
-        late = [sb("late%d" % n, [P, 2, P], F32) for n in range(2)]
+        zt01 = sb("zt01", [P, CHUNKS, 2 * P], BF16)
+        zt23 = sb("zt23", [P, CHUNKS - 1, P, 2], BF16)
+        zb = [sb("zb%d" % n, [P, HALF, PACK], BF16) for n in range(2)]
+        late = sb("late", [P, 2, P], F32)
         zq = sb("zq", [P, V], U32)
         zs = sb("zs", [P, V], U8)
 
-        def words_of(pairs):
-            return pairs.rearrange("v s p e -> v (s p e)").bitcast(F32)
+        def scaled(dst, src, c):
+            nc.scalar.activation(dst, src, COPY, scale=factor[:, c : c + 1])
 
         def as_words(t):
             return t[:].rearrange("p v t -> p (v t)").bitcast(F32).rearrange("p (v u) -> p v u", u=2)
-
-        def sort_pairs(half, sums):
-            nc.scalar.copy(zt01[:, :, 64 * half : 64 * (half + 1), :], sums[:].rearrange("v (s p e) -> v s p e", p=64, e=2))
 
         def quantise_z(n, v0):
             v1 = v0 + zb[n].shape[1]
             nc.vector.quantize_mx(zq[:, v0:v1].bitcast(FP8X4), zs[:, v0:v1], zb[n][:].rearrange("p v t -> p (v t)"))
 
         def second_product(t, tag, v0, v1, empty=empty_scalar):
-            product(g[t], tag, w2_dealt[t][0], w2_dealt[t][1], [(v0, v1, zq[:, v0:v1])], zs, empty)
+            product(g[t], tag, w2_dealt[t][0], w2_dealt[t][1], [(v0, v1, zq[:, v0:v1])], zs_cols, empty)
 
-        whole_product(1, (4, 5))
-        sums0 = bank(2)
-        for d in range(2):
-            add_turned(pieces(sums0, 4), weighted(term("z0_%d" % d, V), h[0], pos_t[d], gate_t[d], 0, V), d == 0, False)
-        raw0 = fetched(term("raw0", V), h[0], pos_t[2], 0, V)
-        whole_product(2, (6, 7))
-        sums1 = bank(3)
-        add_turned(pieces(sums1, 4), weighted(term("z1_0", V), h[1], pos_t[0], gate_t[0], 0, V), True, False)
-        add_turned(pieces(sums0, 4), weigh(term("z0_2", V), raw0, gate_t[2]), False, True)
-        raw1 = fetched(term("raw1", V), h[1], pos_t[2], 0, V)
-        whole_product(3, (0, 1))
-        add_turned(pieces(sums1, 4), weighted(term("z1_1", V), h[1], pos_t[1], gate_t[1], 0, V), False, False)
-        add_turned(pieces(sums1, 4), weigh(term("z1_2", V), raw1, gate_t[2]), False, True)
+        def zs_cols(j0, j1):
+            return zs[:, j0:j1]
 
-        raw23 = [
-            fetched(shared("raw2", [P, HALF], F32, 8 * KB)[:], h[2], pos_t[2], 0, HALF),
-            fetched(term("raw3", HALF), h[3], pos_t[2], 0, HALF),
-        ]
-        sums23 = bank(4)
-        by_tile = sums23[:].rearrange("v (s e p) -> v s e p", s=2, e=2)
-        places = [[by_tile[:, s, e, :] for s in range(2)] for e in range(2)]
+        whole_product(1, (2, 6))
+        pair_banks = [bank(4), bank(5)]
+        pair_places = [[pair_banks[c // 2][:, (2 * (c % 2) + a) * P : (2 * (c % 2) + a + 1) * P] for c in range(CHUNKS)] for a in range(2)]
+        for a in range(2):
+            add_marked(pair_places[a], weighted(term("z%d_0" % a, V), h[a], pos_t[0], ratio_t[0], 0, V), (0, 2) if a == 0 else (), ())
+            raw = fetched(term("raw%d" % a, V), h[a], pos_t[2], 0, V)
+            whole_product(2 + a, ((0, 7), (1, 2))[a])
+            second = weighted(term("z%d_1" % a, V), h[a], pos_t[1], ratio_t[1], 0, V)
+            add_marked(pair_places[a], raw, (), ())
+            add_marked(pair_places[a], second, (), (1, 3) if a == 1 else ())
+        plane_banks = [bank(6), bank(7)]
+        plane_places = [[plane_banks[c // 2][:, (2 * (c % 2) + e) * P : (2 * (c % 2) + e + 1) * P] for c in range(3)] for e in range(2)]
+        raw23 = sb("raw23", [P, 2, V], F32)
         for e in range(2):
-            for d in range(2):
-                src = weighted(term("z%d_%d" % (2 + e, d), HALF), h[2 + e], pos_t[d], gate_t[d], 0, HALF)
-                add_turned(places[e], src, e == 0 and d == 0, False)
-        for e in range(2):
-            add_turned(places[e], weigh(term("z%d_2" % (2 + e), HALF), raw23[e], gate_t[2][:, 0:HALF]), False, e == 1)
-
-        mid, end = slice(HALF, HALF + P), slice(HALF + P, V)
-        weights = bank(5)
-        for d in (1, 2):
-            turn(weights[:, (d - 1) * P : d * P], gate_t[d][:, mid])
-        mid_weight = sb("mid_weight", [P, 2], F32)
-        nc.scalar.copy(mid_weight[:], weights[:, 0:HALF:P])
-        mid_turned = [bank(6), bank(7)]
-        late_raw = sb("late_raw", [P, 2, HALF], F32)
-        for e in range(2):
-            raw = fetched(term("mid_raw%d" % e, P), h[2 + e], pos_t[1], mid.start, mid.stop)
-            turn(mid_turned[0][:, e * P : (e + 1) * P], raw)
-        for e in range(2):
-            raw = fetched(late_raw[:, e, :], h[2 + e], pos_t[2], HALF, V)
-            turn(mid_turned[1][:, e * P : (e + 1) * P], raw[:, 0:P])
-        sort_pairs(0, sums0)
-        sort_pairs(1, sums1)
-        nc.scalar.copy(zt23[:], by_tile.rearrange("v s e p -> v s p e"))
-        mid_sums = bank(0)
-        for d in range(2):
-            scaled = term("mid_scaled%d" % d, HALF)
-            nc.scalar.activation(scaled, mid_turned[d][:, 0:HALF], COPY, scale=mid_weight[:, d : d + 1])
-            add_turned(pieces(mid_sums, 2), scaled, d == 0, d == 1)
-        back = bank(1)
-        turn(back[:, 0:HALF], words_of(zt01[:, 0:2]))
-        turn(back[:, HALF:V], words_of(zt23[:]))
-        nc.scalar.copy(as_words(zb[0]), back[:].rearrange("p (u v) -> p v u", u=2))
-        back = bank(5)
-        turn(back, words_of(zt01[:, 2:4]))
-        for n in (1, 0):
-            nc.scalar.copy(late[n][:, 0, :], back[:, n * P : (n + 1) * P])
+            add_marked(plane_places[e], weighted(term("z%d_0" % (2 + e), TURNED), h[2 + e], pos_t[0], ratio_t[0], 0, TURNED), (0, 2) if e == 0 else (), ())
+            fetched(raw23[:, e, :], h[2 + e], pos_t[2], 0, V)
+            second = weighted(shared("z%d_1" % (2 + e), [P, TURNED], F32, (6 + 2 * e) * KB)[:], h[2 + e], pos_t[1], ratio_t[1], 0, TURNED)
+            add_marked(plane_places[e], raw23[:, e, 0:TURNED], (), ())
+            add_marked(plane_places[e], second, (), (1, 2) if e == 1 else ())
+        for c in range(CHUNKS):
+            scaled(zt01[:, c, :], pair_banks[c // 2][:, (c % 2) * HALF : (c % 2 + 1) * HALF], c)
+        back = [bank(0), bank(2)]
+        turn(back[0][:, 0:HALF], zt01[:, 0:2, :].rearrange("v c w -> v (c w)").bitcast(F32))
+        turn(back[1][:, 0:P], zt01[:, 2, :].bitcast(F32))
+        late_bank = bank(1)
+        turn(late_bank, zt01[:, 3, :].bitcast(F32))
+        nc.scalar.copy(late[:, 0, :], late_bank[:, 0:P])
+        for c in range(3):
+            sums = plane_banks[c // 2][:, (c % 2) * HALF : (c % 2 + 1) * HALF]
+            scaled(zt23[:, c], sums.rearrange("v (e p) -> v p e", e=2), c)
+        turn(back[0][:, HALF:V], zt23[:, 0:2].rearrange("v c p e -> v (c p e)").bitcast(F32))
+        turn(back[1][:, P:HALF], zt23[:, 2].rearrange("v p e -> v (p e)").bitcast(F32))
+        nc.scalar.copy(as_words(zb[0]), back[0][:].rearrange("p (u v) -> p v u", u=2))
+        nc.scalar.copy(as_words(zb[1])[:, 0:P], back[1][:, 0:HALF].rearrange("p (u v) -> p v u", u=2))
 
         weights = bank(3)
         turn(weights, root_runs[:])
         root_weight = sb("root_weight", [P, 2, 2], F32)
         nc.scalar.copy(root_weight[:], weights[:, 52:156].rearrange("p (d x) -> p d x", d=2)[:, :, 0:2])
-
-        late_first = shared("late_first", [P, 2, HALF], F32, 8 * KB + KB // 2)
+        late_terms = [shared("late_term%d" % d, [P, 2, P], F32, (6 + 4 * d) * KB) for d in range(2)]
         for e in range(2):
-            weighted(late_first[:, e, :], h[2 + e], pos_t[0], gate_t[0], HALF, V)
-        end_second = shared("end_second", [P, 2, P], F32, 8 * KB - KB // 2)
-        for e in range(2):
-            weighted(end_second[:, e, :], h[2 + e], pos_t[1], gate_t[1], end.start, end.stop)
-        end_third = weigh(sb("end_third", [P, 2, P], F32)[:], late_raw[:, :, P:HALF], gate_t[2][:, end].unsqueeze(1).to_broadcast([P, 2, P]))
+            nc.vector.tensor_tensor(late_terms[0][:, e, :], h[2 + e][:].indirect(pos_t[0][:, TURNED // 16 : V // 16]), late_gate[:, 0, :], MULT)
+        third = sb("late_third", [P, 2, P], F32)
+        nc.vector.tensor_tensor(third[:], raw23[:, :, TURNED:V], late_gate[:, 2, :].unsqueeze(1).to_broadcast([P, 2, P]), MULT)
+        nc.vector.tensor_tensor(late_terms[1][:, 0, :], h[2][:].indirect(pos_t[1][:, TURNED // 16 : V // 16]), late_gate[:, 1, :], MULT)
         partial = sb("partial_z", [P, 2, P], F32)
-        nc.vector.tensor_tensor(partial[:], late_first[:, :, P:HALF], end_second[:], ADD)
-        deal_w2(0, 1, 0)
-
-        def add_pairs(n, left, right):
-            nc.vector.tensor_tensor(
-                late[n][:, 1, :].bitcast(BF16).rearrange("p (v e) -> p v e", e=2),
-                left.rearrange("p e v -> p v e"), right.rearrange("p e v -> p v e"), ADD,
-            )
-
-        add_pairs(1, partial[:], end_third)
+        nc.vector.tensor_tensor(partial[:], late_terms[0][:], third[:], ADD)
+        nc.vector.tensor_tensor(late_terms[1][:, 1, :], h[3][:].indirect(pos_t[1][:, TURNED // 16 : V // 16]), late_gate[:, 1, :], MULT)
+        deal_w2(0, 1, 8 * KB)
+        nc.vector.tensor_tensor(
+            late[:, 1, :].bitcast(BF16).rearrange("p (v e) -> p v e", e=2),
+            partial[:].rearrange("p e v -> p v e"), late_terms[1][:].rearrange("p e v -> p v e"), ADD,
+        )
+        deal_w2(1, 2, 9 * KB)
+        nc.vector.tensor_copy(as_words(zb[1])[:, P:HALF], late[:].rearrange("p u v -> p v u"))
         quantise_z(0, 0)
-        second_product(0, 7, 0, HALF)
-        add_pairs(0, mid_sums[:, 0:HALF].rearrange("p (e v) -> p e v", e=2), late_first[:, :, 0:P])
-        for n in (1, 0):
-            nc.vector.tensor_copy(as_words(zb[1 + n]), late[n][:].rearrange("p u v -> p v u"))
-        for n in (1, 0):
-            v0 = HALF + n * P
-            quantise_z(1 + n, v0)
-            second_product(0, 6 * n, v0, v0 + P)
-        deal_w2(1, PACK, 5 * KB)
+        second_product(0, 4, 0, HALF)
+        quantise_z(1, HALF)
+        second_product(0, 5, HALF, V)
+        deal_w2(2, PACK, 10 * KB)
 
         y = [sb("y_%d" % u, [P, 2, U], F32) for u in range(2)]
         yb = sb("yb", [P, U, PACK], BF16)

@@ -110,22 +110,22 @@ def tile_picked_hop2_relu_po_kernel(
         turned_runs = bank(0)
         turn(turned_runs, gate_runs[:])
         by_gate = turned_runs[:, 4 : 4 + D * 56].rearrange("p (d x) -> p d x", d=D)[:, :, 0:CHUNKS]
-        sign = sb("sign", [P, CHUNKS], F32)
-        nc.scalar.activation(sign[:], by_gate[:, 2], SIGN)
+        size = sb("size", [P, CHUNKS], F32)
+        nc.scalar.activation(size[:], by_gate[:, 2], ABS)
         small = sb("small", [P, 2, CHUNKS], F32)
         small_sum = sb("small_sum", [P, 1], F32)
         nc.scalar.activation(small[:], by_gate[:, 0:2], ABS, scale=NUDGE, accum_out=small_sum[:])
-        side = sb("side", [P, CHUNKS], F32)
-        nc.scalar.activation(side[:], sign[:], SIGN, bias=0.5)
+        sign = sb("sign", [P, CHUNKS], F32)
+        nc.scalar.activation(sign[:], by_gate[:, 2], SIGN)
         least = sb("least", [P, 1], F32)
         nc.scalar.activation(least[:], small_sum[:], IDENTITY, bias=TINY)
-        third_weight = sb("third_weight", [P, CHUNKS], F32)
-        nc.scalar.copy(third_weight[:], by_gate[:, 2])
+        side = sb("side", [P, CHUNKS], F32)
+        nc.scalar.activation(side[:], sign[:], SIGN, bias=0.5)
         divisor = shared("divisor", [P, 32], F32, 20 * KB - 64)[:, 0:CHUNKS]
+        nc.scalar.activation(divisor, size[:], IDENTITY, bias=least[:])
+        signed = sb("signed", [P, 2, CHUNKS], F32)
         for c in range(CHUNKS):
-            nc.scalar.activation(divisor[:, c : c + 1], side[:, c : c + 1], IDENTITY, scale=least[:], bias=third_weight[:, c : c + 1])
-        factor = sb("factor", [P, CHUNKS], F32)
-        nc.scalar.copy(factor[:], divisor)
+            nc.scalar.activation(signed[:, :, c], by_gate[:, 0:2, c], COPY, scale=side[:, c : c + 1])
         xqs = [shared("xqs_low", [P, BANK], U8, 20 * KB - BANK), sb("xqs_high", [P, BANK], U8)]
         nc.vector.tensor_copy(xqs[1][:], xs[:].indirect(offs_t[:, BANK // 16 : S // 16]))
         inverse = sb("inverse", [P, CHUNKS], F32)
@@ -133,7 +133,12 @@ def tile_picked_hop2_relu_po_kernel(
         nc.vector.tensor_copy(xqs[0][:], xs[:].indirect(offs_t[:, 0 : BANK // 16]))
         ratio = [shared("ratio%d" % n, [P, 2, 2], F32, place) for n, place in enumerate((KB, 7 * KB // 2))]
         for c in range(CHUNKS):
-            nc.scalar.activation(ratio[c // 2][:, :, c % 2], by_gate[:, 0:2, c], COPY, scale=inverse[:, c : c + 1])
+            nc.scalar.activation(ratio[c // 2][:, :, c % 2], signed[:, :, c], COPY, scale=inverse[:, c : c + 1])
+        total = sb("total", [P, CHUNKS], F32)
+        nc.scalar.activation(total[:], size[:], IDENTITY, bias=least[:])
+        factor = sb("factor", [P, CHUNKS], F32)
+        for c in range(CHUNKS):
+            nc.scalar.activation(factor[:, c : c + 1], total[:, c : c + 1], COPY, scale=side[:, c : c + 1])
         spread_banks = [bank(1), bank(2)]
         for d in range(2):
             for c in range(CHUNKS):
@@ -197,16 +202,16 @@ def tile_picked_hop2_relu_po_kernel(
         nc.scalar.copy(ratio_t[0][:], spread_banks[0][:])
         round_pairs(0, nc.scalar.copy)
         nc.scalar.copy(ratio_t[1][:], spread_banks[1][:])
-        round_odd(0, nc.scalar.copy)
+        round_odd(1, nc.scalar.copy)
         gather_words(0, X_SPLIT)
+        round_odd(0, nc.vector.tensor_copy)
         quantise_w1(0)
         gather_words(X_SPLIT, S)
         for n in range(4):
             first_product(0, (0, 1, 4, 5)[n], (256 * n, 256 * (n + 1)))
         round_pairs(1, nc.vector.tensor_copy)
-        round_odd(1, nc.vector.tensor_copy)
-        quantise_w1(1)
         quantise_w1(2)
+        quantise_w1(1)
 
         def whole_product(a, tags):
             first_product(a, tags[0], (0, 512))

from contextlib import ExitStack

import concourse.mybir as mybir

K, T, S, D, V, H, U = 512, 2048, 1024, 3, 512, 512, 256
FLOPS = 2 * K * H * S + 2 * H * H * V

F32 = mybir.dt.float32
BF16 = mybir.dt.bfloat16
I32 = mybir.dt.int32
U32 = mybir.dt.uint32
U16 = mybir.dt.uint16
U8 = mybir.dt.uint8
FP8X4 = mybir.dt.float8_e4m3fn_x4
FP4X4 = mybir.dt.float4_e2m1fn_x4
ABS = mybir.ActivationFunctionType.Abs
COPY = mybir.ActivationFunctionType.Copy
IDENTITY = mybir.ActivationFunctionType.Identity
SIGN = mybir.ActivationFunctionType.Sign
RELU = mybir.ActivationFunctionType.Relu
MULT = mybir.AluOpType.mult
ADD = mybir.AluOpType.add

P = 128
PACK = 4
BANK = 512
HALF = V // 2
KB = 1024
EARLY = 512
X_SPLIT = 768
CHUNKS = V // P
TURNED = 3 * P
NUDGE = 2.0 ** -60
TINY = 2.0 ** -120


def tile_picked_hop2_relu_po_kernel(
    tc, x_words, x_scales, w1, w2_words, w2_scales, gate, gate2,
    offs, pos1, pos2, pos3, nxt1, nxt2, nxt3, out_0, out_1, out_2,
):
    nc = tc.nc
    with ExitStack() as ctx:
        keep = ctx.enter_context(tc.tile_pool(name="keep", bufs=1))
        psum = ctx.enter_context(tc.psum_pool(name="psum", bufs=1))
        reuse = ctx.enter_context(tc.tile_pool(name="reuse", bufs=1))

        def sb(name, shape, dtype):
            return keep.tile(shape, dtype, name=name, align_bytes=64)

        def shared(name, shape, dtype, offset):
            return reuse.tile(shape, dtype, name=name, offset=offset, align_bytes=64)

        def bank(n):
            return psum.tile([P, BANK], F32, name="bank%d" % n, tag="bank%d" % n, bufs=1)

        def load_list(name, src):
            lst = keep.tile(list(src.shape), U16, name=name)
            nc.sync.dma_start(lst[:], src)
            return lst

        def load(name, src):
            dst = sb(name, list(src.shape), F32)
            nc.sync.dma_start(dst[:], src)
            return dst

        def load_scale_rows(queues, plane, rows):
            for q in range(4):
                queues[q % len(queues)].dma_start(plane[32 * q : 32 * q + 4, :].bitcast(I32), rows[4 * q : 4 * q + 4, :].bitcast(I32))

        xs = sb("xs", [P, T], U8)
        nc.gpsimd.memset(xs[:].bitcast(I32), 0)
        w2s = sb("w2s", [P, H], U8)
        nc.vector.memset(w2s[:].bitcast(I32), 0)
        ident = sb("ident", [P, P], F32)
        row_less_column = sb("row_less_column", [P, P], F32)
        nc.gpsimd.iota(row_less_column[:], [[-1, P]], base=0, channel_multiplier=1, allow_small_or_imprecise_dtypes=True)
        distance = sb("distance", [P, P], F32)
        nc.scalar.activation(distance[:], row_less_column[:], ABS)
        nc.scalar.activation(ident[:], distance[:], RELU, bias=1.0, scale=-1.0)

        w1_rows = w1.rearrange("(p j) c -> p j c", j=PACK)
        word_rows = x_words[0].rearrange("p n t -> p (n t)").bitcast(I32)
        def load_runs(name, src, step):
            runs = src.rearrange("d p (c k) -> (d p c) k", k=P)
            return load(name, runs[0 : (P - 1) * step + 1 : step, :])

        gate_runs = load_runs("gate_runs", gate, 9)
        offs_t = load_list("offs_t", offs)
        xw = sb("xw", [P, T], U32)
        nc.sync.dma_start(xw[:, 0:EARLY].bitcast(I32), word_rows[:, 0:EARLY])
        load_scale_rows((nc.sync,), xs, x_scales[0])
        nc.sync.dma_start(xw[:, EARLY:T].bitcast(I32), word_rows[:, EARLY:T])
        w1_low = load("w1_low", w1_rows[:, :, 0 : H // 2])
        w1_high = load("w1_high", w1_rows[:, :, H // 2 : H])
        third_list = load_list("pos2_t", pos3)
        pos_t = [load_list("pos%d_t" % d, src) for d, src in enumerate((pos1, pos2))] + [third_list]
        late_gate = load("late_gate", gate[:, :, TURNED:V].rearrange("d p v -> p d v"))
        root_runs = load_runs("root_runs", gate2, 5)
        w2w = sb("w2w", [P, 2 * H], U8)
        nc.sync.dma_start(w2w[:].bitcast(I32), w2_words[0].bitcast(I32))
        load_scale_rows((nc.sync,), w2s, w2_scales[0])
        nxt_t = [load_list("nxt%d_t" % d, src) for d, src in enumerate((nxt1, nxt2, nxt3))]
        gate2_all = load("gate2_all", gate2.rearrange("d p r -> p d r"))
        gate2_t = [gate2_all[:, d, :] for d in range(D)]

        def turn(dst, src):
            for s in range(src.shape[1] // P):
                nc.tensor.transpose(dst[:, s * P : (s + 1) * P], src[:, s * P : (s + 1) * P], ident[:])

        turned_runs = bank(0)
        turn(turned_runs, gate_runs[:])
        by_gate = turned_runs[:, 4 : 4 + D * 56].rearrange("p (d x) -> p d x", d=D)[:, :, 0:CHUNKS]
        size = sb("size", [P, CHUNKS], F32)
        nc.scalar.activation(size[:], by_gate[:, 2], ABS)
        small = sb("small", [P, 2, CHUNKS], F32)
        small_sum = sb("small_sum", [P, 1], F32)
        nc.scalar.activation(small[:], by_gate[:, 0:2], ABS, scale=NUDGE, accum_out=small_sum[:])
        sign = sb("sign", [P, CHUNKS], F32)
        nc.scalar.activation(sign[:], by_gate[:, 2], SIGN)
        least = sb("least", [P, 1], F32)
        nc.scalar.activation(least[:], small_sum[:], IDENTITY, bias=TINY)
        side = sb("side", [P, CHUNKS], F32)
        nc.scalar.activation(side[:], sign[:], SIGN, bias=0.5)
        divisor = shared("divisor", [P, 32], F32, 20 * KB - 64)[:, 0:CHUNKS]
        nc.scalar.activation(divisor, size[:], IDENTITY, bias=least[:])
        signed = sb("signed", [P, 2, CHUNKS], F32)
        for c in range(CHUNKS):
            nc.scalar.activation(signed[:, :, c], by_gate[:, 0:2, c], COPY, scale=side[:, c : c + 1])
        xqs = [shared("xqs_low", [P, BANK], U8, 20 * KB - BANK), sb("xqs_high", [P, BANK], U8)]
        nc.vector.tensor_copy(xqs[1][:], xs[:].indirect(offs_t[:, BANK // 16 : S // 16]))
        inverse = sb("inverse", [P, CHUNKS], F32)
        nc.vector.reciprocal(inverse[:], divisor)
        nc.vector.tensor_copy(xqs[0][:], xs[:].indirect(offs_t[:, 0 : BANK // 16]))
        ratio = [shared("ratio%d" % n, [P, 2, 2], F32, place) for n, place in enumerate((KB, 7 * KB // 2))]
        for c in range(CHUNKS):
            nc.scalar.activation(ratio[c // 2][:, :, c % 2], signed[:, :, c], COPY, scale=inverse[:, c : c + 1])
        total = sb("total", [P, CHUNKS], F32)
        nc.scalar.activation(total[:], size[:], IDENTITY, bias=least[:])
        factor = sb("factor", [P, CHUNKS], F32)
        for c in range(CHUNKS):
            nc.scalar.activation(factor[:, c : c + 1], total[:, c : c + 1], COPY, scale=side[:, c : c + 1])
        spread_banks = [bank(1), bank(2)]
        for d in range(2):
            for c in range(CHUNKS):
                nc.tensor.transpose(spread_banks[d][:, c * P : (c + 1) * P], ratio[c // 2][:, d, c % 2 : c % 2 + 1].to_broadcast([P, P]), ident[:])

        xq = shared("xq", [P, X_SPLIT], U32, 20 * KB)
        xq_last = shared("xq_last", [P, S - X_SPLIT], U32, KB // 2)
        w1_by_t = [half[:].rearrange("k j (p t) -> k p t j", t=PACK) for half in (w1_low, w1_high)]
        w1_pairs = [shared("w1_first", [P, 64, 2, PACK], BF16, KB)[:], shared("w1_second", [P, 64, 2, PACK], BF16, 3 * KB // 2)[:]]
        w1_odd = shared("w1_odd", [P, 2, P, PACK], BF16, 7 * KB // 2)[:]
        w1_bf = [
            w1_pairs[0].rearrange("k p t j -> k (p t j)"),
            w1_pairs[1].rearrange("k p t j -> k (p t j)"),
            w1_odd.rearrange("k t p j -> k (t p j)"),
        ]
        w1q = sb("w1q", [P, H], U32)
        w1s = sb("w1s", [P, H], U8)
        h = [sb("h%d" % a, [P, S], F32) for a in range(PACK)]
        g = [shared("g%d" % a, [P, V], F32, (12 + 2 * a) * KB) for a in range(PACK)]

        def round_pairs(half, copy):
            copy(w1_pairs[half], w1_by_t[half][:, :, 0:2, :])

        def round_odd(half, copy):
            copy(
                w1_odd[:, :, 64 * half : 64 * (half + 1), :].rearrange("k t p j -> k p t j"), w1_by_t[half][:, :, 2:4, :]
            )

        def quantise_w1(a):
            cols = slice(a * P, a * P + w1_bf[a].shape[1] // PACK)
            nc.vector.quantize_mx(w1q[:, cols].bitcast(FP8X4), w1s[:, cols], w1_bf[a])

        def empty_scalar(dst, src):
            nc.scalar.activation(dst, src, RELU)

        def product(dst, tag, lhsT, lhsT_scale, parts, rhs_scale, empty):
            acc = bank(tag)
            c0, c1 = parts[0][0], parts[-1][1]
            for j0, j1, words in parts:
                nc.tensor.matmul_mx(
                    acc[:, j0 - c0 : j1 - c0], lhsT=lhsT, lhsT_scale=lhsT_scale,
                    rhs=words.bitcast(FP8X4), rhs_scale=rhs_scale(j0, j1), start=True, stop=True,
                )
            empty(dst[:, c0:c1], acc[:, 0 : c1 - c0])

        def picked(j0, j1):
            return xq[:, j0:j1] if j1 <= X_SPLIT else xq_last[:]

        def picked_scales(j0, j1):
            return xqs[j0 // BANK][:, j0 % BANK : j0 % BANK + j1 - j0]

        def first_product(a, tag, cuts):
            cols = slice(a * P, (a + 1) * P)
            parts = [(j0, j1, picked(j0, j1)) for j0, j1 in zip(cuts, cuts[1:])]
            product(h[a], tag, w1q[:, cols].bitcast(FP8X4), w1s[:, cols], parts, picked_scales, empty_scalar)

        def gather_words(j0, j1):
            nc.vector.tensor_copy(picked(j0, j1), xw[:].indirect(offs_t[:, j0 // 16 : j1 // 16]))

        ratio_t = [sb("ratio_rows%d" % d, [P, V], F32) for d in range(2)]
        nc.scalar.copy(ratio_t[0][:], spread_banks[0][:])
        round_pairs(0, nc.scalar.copy)
        nc.scalar.copy(ratio_t[1][:], spread_banks[1][:])
        round_odd(1, nc.scalar.copy)
        gather_words(0, X_SPLIT)
        round_odd(0, nc.vector.tensor_copy)
        quantise_w1(0)
        gather_words(X_SPLIT, S)
        for n in range(4):
            first_product(0, (0, 1, 4, 5)[n], (256 * n, 256 * (n + 1)))
        round_pairs(1, nc.vector.tensor_copy)
        quantise_w1(2)
        quantise_w1(1)

        def whole_product(a, tags):
            first_product(a, tags[0], (0, 512))
            first_product(a, tags[1], (512, 768, 1024))

        w2_words_by_t = w2w[:].bitcast(U16).rearrange("p (h m t) -> p h t m", h=2, t=PACK)
        w2_plane_by_t = w2s[:].rearrange("p (h m t) -> p h t m", h=2, t=PACK)
        w2_dealt = []

        def deal_w2(t0, t1, place):
            n = t1 - t0
            plane = shared("w2_plane%d" % t0, [P, n, P], U8, place)
            words = shared("w2_words%d" % t0, [P, n, 2 * P], U8, place + n * P)
            nc.vector.tensor_copy(plane[:].rearrange("p t (h m) -> p h t m", h=2), w2_plane_by_t[:, :, t0:t1])
            nc.vector.tensor_copy(words[:].bitcast(U16).rearrange("p t (h m) -> p h t m", h=2), w2_words_by_t[:, :, t0:t1])
            for t in range(n):
                w2_dealt.append((words[:, t].bitcast(FP4X4), plane[:, t]))

        def weighted(dst, window, lst, weight, c0, c1):
            nc.vector.tensor_tensor(dst, window[:].indirect(lst[:, c0 // 16 : c1 // 16]), weight[:, c0:c1], MULT)
            return dst

        def fetched(dst, window, lst, c0, c1):
            nc.scalar.activation(dst, window[:].indirect(lst[:, c0 // 16 : c1 // 16]), COPY)
            return dst

        def weigh(dst, raw, weight):
            nc.vector.tensor_tensor(dst, raw, weight, MULT)
            return dst

        def term(name, width):
            return sb(name, [P, width], F32)[:]

        def add_turned(sums, src, first, last):
            for s in range(len(sums)):
                nc.tensor.matmul(
                    sums[s], lhsT=src[:, s * P : (s + 1) * P], rhs=ident[:],
                    start=(first and s == 0), stop=(last and s == len(sums) - 1), is_transpose=True,
                )

        def pieces(acc, n):
            return [acc[:, s * P : (s + 1) * P] for s in range(n)]

        def add_marked(sums, src, first, last):
            for s in range(len(sums)):
                nc.tensor.matmul(
                    sums[s], lhsT=src[:, s * P : (s + 1) * P], rhs=ident[:],
                    start=s in first, stop=s in last, is_transpose=True,
                )

        zt01 = sb("zt01", [P, CHUNKS, 2 * P], BF16)
        zt23 = sb("zt23", [P, CHUNKS - 1, P, 2], BF16)
        zb = [sb("zb%d" % n, [P, HALF, PACK], BF16) for n in range(2)]
        late = sb("late", [P, 2, P], F32)
        zq = sb("zq", [P, V], U32)
        zs = sb("zs", [P, V], U8)

        def scaled(dst, src, c):
            nc.scalar.activation(dst, src, COPY, scale=factor[:, c : c + 1])

        def as_words(t):
            return t[:].rearrange("p v t -> p (v t)").bitcast(F32).rearrange("p (v u) -> p v u", u=2)

        def quantise_z(n, v0):
            v1 = v0 + zb[n].shape[1]
            nc.vector.quantize_mx(zq[:, v0:v1].bitcast(FP8X4), zs[:, v0:v1], zb[n][:].rearrange("p v t -> p (v t)"))

        def second_product(t, tag, v0, v1, empty=empty_scalar):
            product(g[t], tag, w2_dealt[t][0], w2_dealt[t][1], [(v0, v1, zq[:, v0:v1])], zs_cols, empty)

        def zs_cols(j0, j1):
            return zs[:, j0:j1]

        whole_product(1, (2, 6))
        pair_banks = [bank(4), bank(5)]
        pair_places = [[pair_banks[c // 2][:, (2 * (c % 2) + a) * P : (2 * (c % 2) + a + 1) * P] for c in range(CHUNKS)] for a in range(2)]
        for a in range(2):
            add_marked(pair_places[a], weighted(term("z%d_0" % a, V), h[a], pos_t[0], ratio_t[0], 0, V), (0, 2) if a == 0 else (), ())
            raw = fetched(term("raw%d" % a, V), h[a], pos_t[2], 0, V)
            whole_product(2 + a, ((0, 7), (1, 2))[a])
            second = weighted(term("z%d_1" % a, V), h[a], pos_t[1], ratio_t[1], 0, V)
            add_marked(pair_places[a], raw, (), ())
            add_marked(pair_places[a], second, (), (1, 3) if a == 1 else ())
        plane_banks = [bank(6), bank(7)]
        plane_places = [[plane_banks[c // 2][:, (2 * (c % 2) + e) * P : (2 * (c % 2) + e + 1) * P] for c in range(3)] for e in range(2)]
        raw23 = sb("raw23", [P, 2, V], F32)
        for e in range(2):
            add_marked(plane_places[e], weighted(term("z%d_0" % (2 + e), TURNED), h[2 + e], pos_t[0], ratio_t[0], 0, TURNED), (0, 2) if e == 0 else (), ())
            fetched(raw23[:, e, :], h[2 + e], pos_t[2], 0, V)
            second = weighted(shared("z%d_1" % (2 + e), [P, TURNED], F32, (6 + 2 * e) * KB)[:], h[2 + e], pos_t[1], ratio_t[1], 0, TURNED)
            add_marked(plane_places[e], raw23[:, e, 0:TURNED], (), ())
            add_marked(plane_places[e], second, (), (1, 2) if e == 1 else ())
        for c in range(CHUNKS):
            scaled(zt01[:, c, :], pair_banks[c // 2][:, (c % 2) * HALF : (c % 2 + 1) * HALF], c)
        back = [bank(0), bank(2)]
        turn(back[0][:, 0:HALF], zt01[:, 0:2, :].rearrange("v c w -> v (c w)").bitcast(F32))
        turn(back[1][:, 0:P], zt01[:, 2, :].bitcast(F32))
        late_bank = bank(1)
        turn(late_bank, zt01[:, 3, :].bitcast(F32))
        nc.scalar.copy(late[:, 0, :], late_bank[:, 0:P])
        for c in range(3):
            sums = plane_banks[c // 2][:, (c % 2) * HALF : (c % 2 + 1) * HALF]
            scaled(zt23[:, c], sums.rearrange("v (e p) -> v p e", e=2), c)
        turn(back[0][:, HALF:V], zt23[:, 0:2].rearrange("v c p e -> v (c p e)").bitcast(F32))
        turn(back[1][:, P:HALF], zt23[:, 2].rearrange("v p e -> v (p e)").bitcast(F32))
        nc.scalar.copy(as_words(zb[0]), back[0][:].rearrange("p (u v) -> p v u", u=2))
        nc.scalar.copy(as_words(zb[1])[:, 0:P], back[1][:, 0:HALF].rearrange("p (u v) -> p v u", u=2))

        weights = bank(3)
        turn(weights, root_runs[:])
        root_weight = sb("root_weight", [P, 2, 2], F32)
        nc.scalar.copy(root_weight[:], weights[:, 52:156].rearrange("p (d x) -> p d x", d=2)[:, :, 0:2])
        late_terms = [shared("late_term%d" % d, [P, 2, P], F32, (6 + 4 * d) * KB) for d in range(2)]
        for e in range(2):
            nc.vector.tensor_tensor(late_terms[0][:, e, :], h[2 + e][:].indirect(pos_t[0][:, TURNED // 16 : V // 16]), late_gate[:, 0, :], MULT)
        third = sb("late_third", [P, 2, P], F32)
        nc.vector.tensor_tensor(third[:], raw23[:, :, TURNED:V], late_gate[:, 2, :].unsqueeze(1).to_broadcast([P, 2, P]), MULT)
        nc.vector.tensor_tensor(late_terms[1][:, 0, :], h[2][:].indirect(pos_t[1][:, TURNED // 16 : V // 16]), late_gate[:, 1, :], MULT)
        partial = sb("partial_z", [P, 2, P], F32)
        nc.vector.tensor_tensor(partial[:], late_terms[0][:], third[:], ADD)
        nc.vector.tensor_tensor(late_terms[1][:, 1, :], h[3][:].indirect(pos_t[1][:, TURNED // 16 : V // 16]), late_gate[:, 1, :], MULT)
        deal_w2(0, 1, 8 * KB)
        nc.vector.tensor_tensor(
            late[:, 1, :].bitcast(BF16).rearrange("p (v e) -> p v e", e=2),
            partial[:].rearrange("p e v -> p v e"), late_terms[1][:].rearrange("p e v -> p v e"), ADD,
        )
        deal_w2(1, 2, 9 * KB)
        nc.vector.tensor_copy(as_words(zb[1])[:, P:HALF], late[:].rearrange("p u v -> p v u"))
        quantise_z(0, 0)
        second_product(0, 4, 0, HALF)
        quantise_z(1, HALF)
        second_product(0, 5, HALF, V)
        deal_w2(2, PACK, 10 * KB)

        y = [sb("y_%d" % u, [P, 2, U], F32) for u in range(2)]
        yb = sb("yb", [P, U, PACK], BF16)
        codes = sb("codes", [P, U], U32)
        scales = sb("scales", [P, U], U8)
        out_rows = out_0.rearrange("(p t) r -> p t r", t=PACK)
        code_rows = out_1[0].rearrange("p r t -> p (r t)").bitcast(I32)

        def take_turned(t, sums):
            turned = term("turned%d" % t, U)
            nc.scalar.copy(turned, sums[:, 0:U])
            back = bank(t)
            turn(back, turned)
            return back

        def take_back(t, back):
            nc.scalar.copy(y[t // 2][:, t % 2, :], back[:, 0:U])

        def round_pair(copy, u, r0, r1):
            copy(yb[:, r0:r1, 2 * u : 2 * u + 2], y[u][:, :, r0:r1].rearrange("p e r -> p r e"))

        second_product(1, 2, 0, V)
        sums0 = bank(5)
        for d in range(2):
            add_turned(pieces(sums0, 2), weighted(term("y0_%d" % d, U), g[0], nxt_t[d], gate2_t[d], 0, U), d == 0, False)
        raw0 = fetched(term("root0", U), g[0], nxt_t[2], 0, U)
        second_product(2, 3, 0, V)
        sums1 = bank(6)
        add_turned(pieces(sums1, 2), weighted(term("y1_0", U), g[1], nxt_t[0], gate2_t[0], 0, U), True, False)
        add_turned(pieces(sums0, 2), weigh(term("y0_2", U), raw0, gate2_t[2]), False, True)
        raw1 = fetched(term("root1", U), g[1], nxt_t[2], 0, U)
        turned2 = [bank(7), bank(3)]
        turn(turned2[0], fetched(term("root2_1", U), g[2], nxt_t[1], 0, U))
        second_product(3, 4, 0, V)
        turn(turned2[1], fetched(term("root2_2", U), g[2], nxt_t[2], 0, U))
        add_turned(pieces(sums1, 2), weighted(term("y1_1", U), g[1], nxt_t[1], gate2_t[1], 0, U), False, False)
        add_turned(pieces(sums1, 2), weigh(term("y1_2", U), raw1, gate2_t[2]), False, True)
        first2 = weighted(shared("y2_0", [P, U], F32, 14 * KB)[:], g[2], nxt_t[0], gate2_t[0], 0, U)
        sums2 = bank(2)

        def weigh_turned(d):
            for s in range(2):
                scaled = term("root2_scaled%d%d" % (d, s), P)
                nc.scalar.activation(scaled, turned2[d][:, s * P : (s + 1) * P], COPY, scale=root_weight[:, d, s : s + 1])
                add_turned([sums2[:, s * P : (s + 1) * P]], scaled, d + s == 0, d + s == 2)

        weigh_turned(0)
        back0 = take_turned(0, sums0)
        back1 = take_turned(1, sums1)
        weigh_turned(1)
        take_back(0, back0)
        take_back(1, back1)
        nc.sync.dma_start(out_rows[:, 0:2, :], y[0][:])
        for r0 in (0, P):
            round_pair(nc.scalar.copy, 0, r0, r0 + P)

        y3_0 = weighted(term("y3_0", U), g[3], nxt_t[0], gate2_t[0], 0, U)
        y3_2 = weighted(shared("y3_2", [P, U], F32, 15 * KB)[:], g[3], nxt_t[2], gate2_t[2], 0, U)
        y3_1 = weighted(shared("y3_1", [P, U], F32, 17 * KB)[:], g[3], nxt_t[1], gate2_t[1], 0, U)
        partial = term("partial_y", U)
        nc.vector.tensor_tensor(partial, y3_0, y3_2, ADD)
        nc.vector.tensor_tensor(y[1][:, 0, :], sums2[:, 0:U], first2, ADD)
        nc.sync.dma_start(out_rows[:, 2, :], y[1][:, 0, :])
        for r0 in (0, P):
            nc.vector.tensor_tensor(y[1][:, 1, r0 : r0 + P], partial[:, r0 : r0 + P], y3_1[:, r0 : r0 + P], ADD)
        nc.sync.dma_start(out_rows[:, 3, :], y[1][:, 1, :])
        for r0 in (0, P):
            round_pair(nc.vector.tensor_copy, 1, r0, r0 + P)
        for r0 in (0, P):
            nc.vector.quantize_mx(
                codes[:, r0 : r0 + P].bitcast(FP8X4), scales[:, r0 : r0 + P],
                yb[:, r0 : r0 + P, :].rearrange("p r t -> p (r t)"),
            )
        nc.sync.dma_start(code_rows, codes[:].bitcast(I32))
        for q in range(4):
            queue = nc.scalar if q % 2 else nc.sync
            queue.dma_start(out_2[0, 4 * q : 4 * q + 4, :].bitcast(I32), scales[32 * q : 32 * q + 4, :].bitcast(I32))
